import numpy as np, ml_dtypes
CORES = [10,34,74,98]
N = 4
BF = ml_dtypes.bfloat16
W, L, ST = 8192, 256, 32
STEPS = (1, 2, 3, 1)
def look(X, J, z, w, A):
    u = np.sum(w * z, axis=2) & 1023
    h = (((J * (2 * u + 1)[:, :, None, :]) >> 5) + J + A[:, None, None, None]) & (W - 1)
    x = np.take_along_axis(X, h.reshape(N, 8, 1, 16 * L), 3).reshape(N, 8, 16, 16, L)
    m = np.minimum(x, z[:, :, :, None, :])
    return u, x, np.sum(m, axis=2), 1 + np.sum(x - m, axis=2)
def parts(rng):
    top = rng.integers(6, 16, (N, 8, 1, W))
    X = rng.integers(0, top + 1, (N, 8, 16, W)); J = rng.integers(0, W, (N, 8, 16, L))
    return X, J, rng.integers(1, 16, (N, 8, 16, L)), rng.integers(0, 64, (N, 8, 16, 1))
def pack(X, J, z, w):
    return {"xt": X.reshape(N, 128, W).astype(np.float32).astype(BF), "jn": np.ascontiguousarray(J.reshape(N, 128, L)).astype(np.int32),
            "zd": z.reshape(N, 128, L).astype(np.float32).astype(BF), "wt": w.reshape(N, 128, 1).astype(np.float32)}
def setup_inputs(rng):
    return pack(*parts(rng))
def uphill(X, J, z, w):
    u, x, g, s = look(X, J, z, w, np.zeros(N, np.int64))
    o = np.argsort(g * np.power(s.astype(np.float64), -1.0), axis=2, kind="stable")
    return np.take_along_axis(J, o, 2)
def setup_inputs_corners(rng):
    X, J, z, w = parts(rng)
    w[:, 2] = 0; w[:, 2, :4] = 63; w[:, 2, 4] = 21; J[:, 2] = rng.integers(W - 120, W, (N, 16, L))
    w[:, 3] = 63; X[:, 3, :, 0] = 15; J[:, 3, 1:8] = W - 1 - 32 * rng.integers(0, 12, (N, 7, L)); J[:, 3, 15] = 0
    J[:, :, 0, :4] = 0; J[:, :, 1, :4] = W - 1
    c = W - 1 - 32 * np.arange(12); h = ((c * 2017 >> 5) + c + 128 * L) & (W - 1)
    X[0, 3][:, h] = 1; X[0, 3][:, (h + 1) & (W - 1)] = 15
    lead = np.concatenate([J[STEPS[0], 3, 1:], J[STEPS[0], 3, :1]], axis=0)
    strong = np.zeros((N, 8, 1, L), bool); short = np.zeros((N, 8, 1, L), bool); near = np.zeros((N, 8, 1, L), bool); m = 0
    for r in range(N):
        q = r ^ STEPS[0]
        if r > q: continue
        if m == 0: strong[r] = True
        elif m == 1:
            strong[q] = True; near[q, 7, 0, L - 1] = True
        else:
            strong[r, ::2] = True; strong[q, 1::2] = True
            strong[q, 1, 0, 0] = False; strong[r, 1, 0, 0] = True; strong[r, 6, 0, L - 1] = False; strong[q, 6, 0, L - 1] = True
            if m == 3:
                short[r] = True; short[q] = True
        m += 1
    z = np.where(strong, 15, 1) + np.zeros((1, 1, 16, 1), np.int64)
    up = uphill(X, J, z, w); down = up[:, :, ::-1]; most = np.concatenate([up[:, :, 1:], up[:, :, :1]], axis=2)
    J = np.where(strong, np.where(short, down, np.where(near, most, up)), J)
    for r in range(N):
        for g in range(8): J[r, g] = np.where(strong[r, g], J[r, g], up[r, g]) if g == 3 and r != STEPS[0] else J[r, g]
    J[STEPS[0], 3] = lead
    return pack(X, J, z, w)
def setup_inputs_crowd(rng):
    X, J, z, w = parts(rng); c = rng.integers(0, W, (N, 8)); c[0, 0] = 0; c[1, 0] = W - 1
    for g in (0, 4, 1, 5):
        J[:, g] = c[:, g][:, None, None]; z[:, g] = z[:, g, :, :1].copy()
    for g, o in ((1, int(rng.integers(0, L))), (5, L - 1)):
        J[:, g, :, o] = rng.integers(0, W, (N, 16)); z[:, g, :, o] = rng.integers(1, 16, (N, 16))
    for g in (2, 6): J[:, g] = rng.choice(np.array([0, 3, W // 2, W - 1]), (N, 16, L))
    for g in (3, 7): J[:, g] = J[:, g, :1].copy()
    for a in (X, J, z, w): a[:, 4] = a[0, 4].copy()
    return pack(X, J, z, w)
def setup_inputs_ends(rng):
    X = 15 * rng.integers(0, 2, (N, 8, 16, W)); X[:, 1::2] = 15 * rng.integers(0, 2, (N, 4, 1, W))
    J = (W - 1) * rng.integers(0, 2, (N, 8, 16, L)); kind = rng.integers(0, 3, (N, 8, 1, L))
    z = np.where(kind == 0, 1, np.where(kind == 1, 15, 1 + 14 * rng.integers(0, 2, (N, 8, 16, L))))
    w = 63 * rng.integers(0, 2, (N, 8, 16, 1)); w[:, 5] = 63
    for g in (0, 3, 7): w[:, g] = 0
    c = W // 32 - 2
    X[:, 0, :, 0] = 0; X[:, 0, :, c] = 0
    X[:, 3, :, 0] = 15; X[:, 3, :, c] = 15; X[:, 3, 0, c] = 0
    J[:, 3, :, -8:] = 0; J[:, 3, 0, -8:] = W - 1; z[:, 3, :, -8:] = 15
    X[:, 7, :, 0] = 15; X[:, 7, :, c] = 15; X[:, 7, 0, c] = 0
    duo = np.array([[0, 0], [0, 1], [1, 0], [1, 1], [2, 2], [2, 3], [3, 2], [3, 3], [4, 4]])
    pn = rng.integers(0, 9, L); pn[:9] = rng.permutation(9); pn[L - 1] = 8; pn[L - 2] = 5; pn[L - 3] = 0; pn[L - 4] = 7; pn[L - 5] = 6
    for r in range(N):
        if r < (r ^ STEPS[0]): X[r, 3, 1, c] = 14
        kd = duo[pn, int(r > (r ^ STEPS[0]))]
        J[r, 7] = 0; J[r, 7, 0] = np.where(kd >= 2, W - 1, 0)
        z[r, 7] = np.where((kd == 0) | (kd == 2), 15, 1)
        z[r, 7, :7] = np.where(kd == 4, 15, z[r, 7, :7])
    return pack(X, J, z, w)
def setup_inputs_spread(rng):
    def e(*shape): return np.exp2(rng.integers(-2, 4, shape))
    X = np.minimum((16 * rng.random((N, 8, 16, W)) ** e(N, 8, 1, W)).astype(np.int64), 15)
    J = np.minimum((W * rng.random((N, 8, 16, L)) ** e(N, 8, 1, L)).astype(np.int64), W - 1)
    z = np.minimum(1 + (15 * rng.random((N, 8, 16, L)) ** e(N, 8, 1, L)).astype(np.int64), 15)
    w = np.minimum((64 * rng.random((N, 8, 16, 1)) ** e(N, 8, 16, 1)).astype(np.int64), 63)
    high = [r for r in range(N) if r > (r ^ STEPS[0])]; few = 1 + rng.permutation(3)
    for r, n in zip(high[1:], few):
        at = np.array([L - 1, 0, L // 2])[:int(n)]
        X[r, :, :, ::4] = 0; J[r] = J[r] & -128
        w[r, 7] = 0; X[r, 7, :, 1] = 15
        J[r, 7, 0][at] = 1; z[r, 7][:, at] = 15; z[r ^ STEPS[0], 7][:, at] = 1
    return pack(X, J, z, w)
def setup_inputs_ties(rng):
    X, J, z, w = parts(rng); v = rng.integers(0, 16, (8, 16)); v[:, 0] = 15; v[:, 1] = 0
    ix = (np.arange(16)[None, None, :, None] + rng.integers(0, 16, (N, 8, 1, W))) & 15
    X = np.where(rng.random((N, 8, 1, W)) < 0.0625, X, v[np.arange(8)[None, :, None, None], ix])
    one = rng.integers(1, 16, (N, 8, 1, L)); one[:, ::2] = one[0, ::2].copy(); one[:, 7] = one[0, 7].copy()
    w[:, 6] = 0; kd = rng.integers(0, 4, L); kd[:4] = rng.permutation(4); kd[L - 4:] = rng.permutation(4)
    for c, g, s, d, n in ((1, 100, 61, 8, 9), (2, 120, 57, 8, 9), (3, 110, 51, 8, 9), (4, 108, 50, 8, 9), (5, 113, 53, 8, 9), (6, 56, 131, 4, 12), (7, 60, 87, 4, 12), (8, 60, 86, 4, 12)):
        X[:, 6, :n, c] = d + (s - 1 + np.arange(n)) // n
        X[:, 6, n:, c] = (g - d * n + np.arange(16 - n)) // (16 - n)
    for m, d, p, lo, hi in ((0, 8, 1, 2, 3), (1, 8, 1, 4, 5), (2, 4, 6, 7, 8)):
        at = kd == m; one[:, 6, 0, at] = d
        for r in range(N):
            J[r, 6][:, at] = p; J[r, 6, 15, at] = hi if r > (r ^ STEPS[0]) else lo
    return pack(X, J, one + np.zeros((1, 1, 16, 1), np.int64), w)
def check_inputs(d):
    bad = []
    for k, lo, hi in (("xt", 0, 15), ("jn", 0, W - 1), ("zd", 1, 15), ("wt", 0, 63)):
        a = np.asarray(d[k]).astype(np.float64)
        if not np.all((a >= lo) & (a <= hi)): bad.append("range of " + k)
        if not np.all(a == np.floor(a)): bad.append("whole numbers of " + k)
    return bad
def reference(xt, jn, zd, wt):
    X = xt.astype(np.float32).astype(np.int64).reshape(N, 8, 16, W); J = jn.astype(np.int64).reshape(N, 8, 16, L)
    z = zd.astype(np.float32).astype(np.int64).reshape(N, 8, 16, L); w = wt.astype(np.int64).reshape(N, 8, 16, 1)
    A = np.zeros(N, np.int64); r = np.arange(N); k16 = np.arange(16)
    for step in STEPS:
        q = r ^ step
        u, x, g, s = look(X, J, z, w, A)
        G = np.add.accumulate(g, axis=2); S = np.add.accumulate(s, axis=2)
        bG, bS, b = G[:, :, 0], S[:, :, 0], np.zeros((N, 8, L), np.int64)
        for k in range(1, 16):
            up = G[:, :, k] * bS > bG * S[:, :, k]
            bG = np.where(up, G[:, :, k], bG); bS = np.where(up, S[:, :, k], bS); b = np.where(up, k, b)
        y = np.max(np.where(k16[None, None, None, :, None] <= b[:, :, None, None, :], x, 0), axis=3)
        mine = bG * bS[q]; other = bG[q] * bS
        win = (mine > other) | ((mine == other) & (r < q)[:, None, None]); ww = win[:, :, None, :]
        both = np.concatenate([J, J[q]], axis=2)
        spliced = np.take_along_axis(both, k16[None, None, :, None] + (b + 1)[:, :, None, :], 2)
        col = (ST * np.arange(L)[None, None, :] + (u & (ST - 1)))[:, :, None, :]
        old = np.take_along_axis(X, col, 3)
        np.put_along_axis(X, np.broadcast_to(col, old.shape), np.where(ww, (old + y) >> 1, old), 3)
        z = np.where(ww, np.maximum(np.abs(z - y), 1), np.maximum((z + y[q]) >> 1, 1))
        J = np.where(ww, spliced, J)
        A = np.sum(np.where(win, b + 1, 0), axis=(1, 2))
    out = X[..., :W // 2] + 16 * X[..., W // 2:]
    return {"yx": out.reshape(N, 128, W // 2).astype(np.float32).astype(BF), "yj": J.reshape(N, 128, L).astype(np.float32), "yz": z.reshape(N, 128, L).astype(np.float32).astype(BF)}

@@ -1,0 +1,569 @@
+from concourse.mybir import AluOpType, ActivationFunctionType
+
+OP = AluOpType
+AF = ActivationFunctionType
+ROUNDS = 4
+STEPS = (1, 2, 3, 1)
+W = 8192
+L = 256
+YH, YW = 2048, 2176
+SLABS = 17
+S12 = 2.0 ** -12
+S20 = 2.0 ** -20
+LIFT = 192.0
+DROP = 32.0 * 5 * W
+
+CFG = {
+    "h": (((0, 64), (64, 128)), ((128, 192), (192, 256))),
+    "ga": ((0, 64), (64, 128), (128, 192), (192, 224), (224, 256)),
+    "gv": (),
+    "m": ((0, 64), (64, 128), (128, 192), (192, 224), (224, 256)),
+    "gap": {0: (0, 64), 1: (64, 128)},
+    "pre": ((128, 160),),
+    "fill": (),
+    "post": ((160, 256),),
+    "klate": False,
+    "lastlate": True,
+    "yearly": 6,
+    "z": {(0, 0): ((0, 128), (128, 256))},
+    "own": 3,
+    "early": True,
+    "dzlate": True,
+    "order": "ajb",
+}
+
+F, B, I, U = "float32", "bfloat16", "int32", "uint16"
+SCRATCH = {
+    "X": ("sbuf", [128, W + L], B), "Y": ("sbuf", [128, W // 2 + L], B),
+    "xg": ("sbuf", [128, 16 * L], B), "mn": ("sbuf", [128, 16 * L], B), "pm": ("sbuf", [128, 16 * L], B),
+    "mask": ("sbuf", [128, 16 * L], B),
+    "jin": ("sbuf", [128, L], I), "z": ("sbuf", [128, L], B), "w": ("sbuf", [128, 8], F),
+    "ij": ("sbuf", [128, L], F), "pi": ("sbuf", [128, 8], I), "qi": ("sbuf", [128, 8], I),
+    "q1": ("sbuf", [128, 8], F), "q16": ("sbuf", [128, 8], F), "q256": ("sbuf", [128, 8], F),
+    "bandv": ("sbuf", [128, 144], F), "blkv": ("sbuf", [128, 128], F),
+    "bm": ("sbuf", [128, 144], B), "band": ("sbuf", [128, 144], B), "wband": ("sbuf", [128, 144], B),
+    "blkm": ("sbuf", [128, 128], B), "w2": ("sbuf", [128, 128], B),
+    "id1": ("sbuf", [128, 128], B), "id16": ("sbuf", [128, 128], B),
+    "c19": ("sbuf", [128, 128], B), "c4096": ("sbuf", [128, 128], B),
+    "ones": ("sbuf", [128, L], B), "neg": ("sbuf", [128, L], B),
+    "kc": ("sbuf", [128, L], F), "kb": ("sbuf", [128, 16], F),
+    "col": ("sbuf", [128, 16], F), "pos": ("sbuf", [128, 16], F),
+    "colu": ("sbuf", [128, 16], U), "repu": ("sbuf", [128, 16], U),
+    "l32": ("sbuf", [128, 32], F), "cx": ("sbuf", [128, 48], F), "dump": ("sbuf", [128, 32], F),
+    "ol": ("sbuf", [128, 96], F), "dd": ("sbuf", [128, 48], F),
+    "c1": ("sbuf", [128, 256], F), "c2": ("sbuf", [128, 128], F), "c3": ("sbuf", [128, 64], F), "c4": ("sbuf", [128, 32], F),
+    "ha": ("sbuf", [128, L], I), "hb": ("sbuf", [128, L], I), "hc": ("sbuf", [128, L], F), "hd": ("sbuf", [128, L], I),
+    "he": ("sbuf", [128, L], I), "hu": ("sbuf", [128, L], U),
+    "ti": ("sbuf", [128, 16], I), "rc": ("sbuf", [128, 16], I), "rf": ("sbuf", [128, 16], F), "dx": ("sbuf", [128, 16], F),
+    "offr": ("sbuf", [128, 16], U), "offy": ("sbuf", [128, 16], U), "off": ("sbuf", [128, 48], U),
+    "gs": ("sbuf", [128, 256], F), "ts": ("sbuf", [128, 256], F), "pb": ("sbuf", [128, 128], F), "pa": ("sbuf", [128, 32], F),
+    "t1": ("sbuf", [128, 256], F), "k1": ("sbuf", [128, 256], F),
+    "g2": ("sbuf", [128, 128], F), "t2": ("sbuf", [128, 128], F), "k2": ("sbuf", [128, 128], F),
+    "g3": ("sbuf", [128, 64], F), "t3": ("sbuf", [128, 64], F), "k3": ("sbuf", [128, 64], F), "k4": ("sbuf", [128, 32], F),
+    "qq": ("sbuf", [128, 32], F), "win": ("sbuf", [128, 16], F), "wd": ("sbuf", [128, 48], F), "oo": ("sbuf", [128, 48], F),
+    "sb": ("sbuf", [128, 16], B), "aj": ("sbuf", [128, 16], F), "acol": ("sbuf", [128, 8], F),
+    "bw": ("sbuf", [128, 2 * L], F), "dz": ("sbuf", [128, L], F), "base": ("sbuf", [128, L], F), "oq": ("sbuf", [128, L], F),
+    "rec": ("sbuf", [128, L], B), "zl": ("sbuf", [128, L], B),
+    "d1": ("sbuf", [128, 128], B), "d16": ("sbuf", [128, 128], B), "ya": ("sbuf", [128, 128], B), "yb": ("sbuf", [128, 128], B),
+    "jfin": ("sbuf", [128, L], F),
+    "pU": ("psum", [128, 512], F), "pZ0": ("psum", [128, 512], F), "pZ1": ("psum", [128, 512], F), "pG": ("psum", [128, 512], F),
+    "pT": ("psum", [128, 512], F), "pP": ("psum", [128, 512], F), "pY0": ("psum", [128, 512], F), "pY1": ("psum", [128, 512], F),
+}
+SEMAPHORES = ["v", "a", "p", "g", "ldz", "ldw", "ldj", "ldx", "ldx2", "sent", "outj", "outz", "outx"]
+for _t in range(ROUNDS):
+    SCRATCH["tw%d" % _t] = ("sbuf", [128, SLABS * L], F)
+    SCRATCH["sv%d" % _t] = ("sbuf", [128, 96], F)
+    SCRATCH["lv%d" % _t] = ("sbuf", [128, 64], F)
+    SCRATCH["yh%d" % _t] = ("sbuf", [128, L], B)
+    SCRATCH["ly%d" % _t] = ("sbuf", [128, 2 * L], B)
+    SCRATCH["do%d" % _t] = ("dram", [8, 16 * L], F)
+    SCRATCH["dr%d" % _t] = ("dram", [8, 16 * L], F)
+    SEMAPHORES += ["aj%d" % _t, "av%d" % _t, "ay%d" % _t, "so%d" % _t, "sr%d" % _t, "tp%d" % _t]
+
+
+def emit(g, T, ops):
+    queue = {"v": g.vector, "a": g.scalar, "p": g.tensor, "g": g, "s": g.sync}
+    writer, readers, count, dmas = {}, {}, {}, {}
+    known = {e: {} for e in queue}
+    snap, waits, wanted = {}, [], set()
+    for e, fn, rd, wr, banks, dsem, ext in ops:
+        if ext is not None:
+            for tok in wr:
+                writer[tok] = ext
+                readers[tok] = []
+            snap[ext] = {}
+            waits.append(None)
+            continue
+        deps = []
+        for tok in rd:
+            if tok in writer:
+                deps.append(writer[tok])
+        for tok in wr:
+            if tok in writer:
+                deps.append(writer[tok])
+            deps += readers.get(tok, [])
+        for tok in banks:
+            if tok in writer and writer[tok][0] != e:
+                deps.append(writer[tok])
+        need = {}
+        for key, n in deps:
+            if key == "p" and e == "p":
+                continue
+            if key in dmas:
+                n = dmas[key]
+            need[key] = max(need.get(key, 0), n)
+        mine = []
+        for key in sorted(need):
+            n = need[key]
+            if known[e].get(key, 0) >= n:
+                continue
+            if any(snap[(k2, need[k2])].get(key, 0) >= n for k2 in need if k2 != key):
+                continue
+            mine.append((key, n))
+        for key, n in mine:
+            for k2, n2 in snap[(key, n)].items():
+                known[e][k2] = max(known[e].get(k2, 0), n2)
+            known[e][key] = max(known[e].get(key, 0), n)
+            wanted.add((key, n))
+        waits.append(mine)
+        if fn is None or dsem == "":
+            continue
+        if dsem is not None:
+            prev = snap.get((dsem, dmas.get(dsem, 0)), {})
+            dmas[dsem] = dmas.get(dsem, 0) + 16
+            me = (dsem, dmas[dsem])
+            s = dict(known[e])
+            for k2, n2 in prev.items():
+                s[k2] = max(s.get(k2, 0), n2)
+            snap[me] = s
+        else:
+            count[e] = count.get(e, 0) + 1
+            me = (e, count[e])
+            snap[me] = dict(known[e])
+        for tok in rd:
+            readers.setdefault(tok, []).append(me)
+        for tok in wr:
+            writer[tok] = me
+            readers[tok] = []
+        for tok in banks:
+            writer[tok] = me
+    level, seen, count = {}, {}, {}
+    for (e, fn, rd, wr, banks, dsem, ext), mine in zip(ops, waits):
+        if ext is not None:
+            continue
+        for key, n in mine:
+            queue[e].wait_ge(T.sem[key], level[(key, n)] if key in queue else n)
+        if fn is None:
+            continue
+        ins = fn()
+        if dsem == "":
+            continue
+        if dsem is not None:
+            ins.then_inc(T.sem[dsem], 16)
+        else:
+            count[e] = count.get(e, 0) + 1
+            if (e, count[e]) in wanted:
+                seen[e] = seen.get(e, 0) + 1
+                level[(e, count[e])] = seen[e]
+                ins.then_inc(T.sem[e], 1)
+
+
+def rank_program(g, core, T, topo):
+    rank = T.rank_of(core)
+    if rank is None:
+        return
+    ops = []
+    v, a, pe = g.vector, g.scalar, g.tensor
+    sent = [0]
+
+    def add(e, fn, rd=(), wr=(), banks=(), dsem=None, ext=None):
+        ops.append((e, fn, list(rd), list(wr), list(banks), dsem, ext))
+
+    def ts(out, in0, s1, s2, o0, o1, rd, wr, banks=()):
+        if o1 is None:
+            add("v", lambda: v.tensor_scalar(out, in0, s1, None, o0), rd, wr, banks)
+        else:
+            add("v", lambda: v.tensor_scalar(out, in0, s1, s2, o0, o1), rd, wr, banks)
+
+    def tt(out, in0, in1, op, rd, wr, banks=()):
+        add("v", lambda: v.tensor_tensor(out, in0, in1, op), rd, wr, banks)
+
+    def cp(out, in_, rd, wr, banks=()):
+        add("v", lambda: v.tensor_copy(out, in_), rd, wr, banks)
+
+    def ms(ap, c, wr):
+        add("v", lambda: v.memset(ap, c), (), wr)
+
+    def scan(out, d0, d1, o0, o1, rd, wr, banks=()):
+        add("v", lambda: v.tensor_tensor_scan(out, d0, d1, 0.0, o0, o1), rd, wr, banks)
+
+    def act(out, in_, func, rd, wr, banks=(), bias=0.0, scale=1.0, acc=None):
+        if acc is None:
+            add("a", lambda: a.activation(out, in_, func, bias=bias, scale=scale), rd, wr, banks)
+        else:
+            add("a", lambda: a.activation(out, in_, func, bias=bias, scale=scale, accum_out=acc), rd, wr, banks)
+
+    def mm(out, lhs, rhs, start, stop, rd, wr, banks):
+        add("p", lambda: pe.matmul(out, lhs, rhs, start, stop), rd, wr, banks)
+
+    def dma(e, out, in_, rd, wr, sem):
+        q = g.sync if e == "s" else g.scalar
+        add(e, lambda: q.dma_start(out, in_), rd, wr, (), sem)
+
+    def iota(out, pat, mult, wr, flag=True):
+        if flag:
+            add("g", lambda: g.iota(out, pat, 0, mult, allow_small_or_imprecise_dtypes=True), (), wr)
+        else:
+            add("g", lambda: g.iota(out, pat, 0, mult), (), wr)
+
+    def swap(t, out, in_, rd, tok, sem):
+        peer = T.cores[rank ^ STEPS[t]]
+        rid, pid, _ = topo.addr(peer)
+        add("g", lambda: g.remote_dma(out, in_, T.sem[sem], T.sem.sent, pid, rid, topo.mask(core, peer)), rd, (), (), "")
+        sent[0] += len(topo.engines(core, peer))
+        add(None, None, (), [tok], ext=(sem, len(topo.engines(peer, core))))
+
+    def qs(lo, hi, name):
+        return ["%s%d" % (name, q) for q in range(lo // 16, hi // 16)]
+
+    tw = [T["tw%d" % t] for t in range(ROUNDS)]
+    zall, xall = qs(0, L, "z"), ["X", "X2"]
+
+    def lists(t, after):
+        w_, do, dr = tw[t], T["do%d" % t], T["dr%d" % t]
+        swap(t, w_[:, 16 * L:17 * L], w_[:, 0:L], ["j%d" % t] + after[:1], "jr%d" % t, "aj%d" % t)
+        dma("s", do[:], w_[:, 0:L], ["j%d" % t] + after, ["do%d" % t], "so%d" % t)
+        for k in range(15):
+            if k == (0 if t == 0 else CFG["own"]):
+                dma("s", dr[:], w_[:, 16 * L:17 * L], ["jr%d" % t], ["dr%d" % t], "sr%d" % t)
+            dma("s", w_[k::16, L:(16 - k) * L], do[:, (k + 1) * L:16 * L], ["do%d" % t], ["to%d.%d" % (t, k)], "tp%d" % t)
+        for k in range(1, 16):
+            dma("s", w_[k::16, (16 - k) * L:16 * L], dr[:, 0:k * L], ["dr%d" % t], ["tr%d.%d" % (t, k)], "tp%d" % t)
+
+    dma("s", T.z[:], T.zd[:], (), zall, "ldz")
+    dma("a", T.X[:, 0:W // 2], T.xt[:, 0:W // 2], (), ["X"], "ldx")
+    dma("s", T.w[:, 0:1], T.wt[:], (), ["w"], "ldw")
+    dma("s", T.jin[:], T.jn[:], (), ["jin"], "ldj")
+    dma("s", T.X[:, W // 2:W], T.xt[:, W // 2:W], (), ["X2"], "ldx2")
+    iota(T.pi[:, 0:1], [[0, 1]], 1, ["pi"], False)
+    iota(T.blkv[:], [[16, 8], [0, 16]], -1, ["blkv"])
+    iota(T.bandv[:], [[1, 144]], -1, ["bandv"])
+    iota(T.ij[:], [[1, L]], 0, ["ij"])
+    q1, q16, q256, w = T.q1[:, 0:1], T.q16[:, 0:1], T.q256[:, 0:1], T.w[:, 0:1]
+    nmask = 16 * max(hi - lo for lo, hi in list(CFG["pre"]) + list(CFG["post"]) + list(CFG["fill"]) + list(CFG["gap"].values()))
+    ms(T.c19[:], 2.0 ** -19, ["c19"])
+    ms(T.ones[:], 1.0, ["ones"])
+    ts(T.qi[:, 0:1], T.pi[:, 0:1], 15, None, OP.bitwise_and, None, ["pi"], ["qi"])
+    ms(T.neg[:], -LIFT, ["neg"])
+    cp(q1, T.qi[:, 0:1], ["qi"], ["q1"])
+    ms(T.c4096[:], 4096.0, ["c4096"])
+    ts(T.blkm[:], T.blkv[:], q1, 0.0, OP.add, OP.is_equal, ["blkv", "q1"], ["blkm"])
+    ts(q16, q1, 16.0, None, OP.mult, None, ["q1"], ["q16"])
+    ts(q256, q1, 256.0, None, OP.mult, None, ["q1"], ["q256"])
+    ts(T.bm[:], T.bandv[:], q1, 15.0, OP.add, OP.is_equal, ["bandv", "q1"], ["bm"])
+    ts(T.id1[:], T.bandv[:, 0:128], 0.0, None, OP.is_equal, None, ["bandv"], ["id1"])
+    ms(T.mask[:, 0:nmask], 1.0, ["mask"])
+    ts(T.band[:], T.bm[:], S12, None, OP.mult, None, ["bm"], ["band"])
+    ms(T.mask[:, 0:nmask:16], 0.0, ["mask"])
+    ts(T.col[:], T.ij[:, 0:16], q16, None, OP.add, None, ["ij", "q16"], ["col"])
+    ts(T.pos[:], T.ij[:, 0::16], q1, None, OP.add, None, ["ij", "q1"], ["pos"])
+    ts(T.kc[:], T.ij[:], q256, S12, OP.add, OP.mult, ["ij", "q256"], ["kc"])
+    ts(T.w2[:], T.blkm[:], w, 2.0, OP.mult, OP.mult, ["blkm", "w"], ["w2"])
+    ts(T.wband[:], T.bm[:], w, None, OP.mult, None, ["bm", "w"], ["wband"])
+    cp(tw[0][:, 0:L], T.jin[:], ["jin"], ["j0"])
+    lists(0, xall)
+    act(T.pP[:, 0:L], tw[0][:, 0:L], AF.Identity, ["j0"], ["pJ"], ["pP"])
+    act(T.pP[:, L:2 * L], tw[0][:, 0:L], AF.Identity, ["j0"], ["pJA"], ["pP"], bias=-DROP, scale=32.0)
+
+    def late_constants():
+        cp(T.colu[:], T.col[:], ["col"], ["colu"])
+        ts(T.repu[:, 0:4], T.ij[:, 0:4], 0.0, q1, OP.mult, OP.add, ["ij", "q1"], ["repu"])
+        ts(T.kb[:], T.kc[:, 0::16], -S12, None, OP.add, None, ["kc"], ["kb"])
+        ts(T.l32[:, 0:16], T.col[:], 32.0, None, OP.mult, None, ["col"], ["l32a"])
+        ts(T.l32[:, 16:32], T.pos[:], 32.0, None, OP.mult, None, ["pos"], ["l32b"])
+        ts(T.dump[:, 0:16], T.pos[:], float(W), None, OP.add, None, ["pos"], ["dumpa"])
+        for j in range(4):
+            ts(T.dump[:, 16 + 4 * j:20 + 4 * j], T.pos[:, 4 * j:4 * j + 4], float(YH - 64 * j), None, OP.add, None, ["pos"],
+               ["dumpb%d" % j])
+        for o in (0, 48):
+            ts(T.ol[:, o:o + 16], T.col[:], S20, None, OP.mult, None, ["col"], ["ol%d" % o])
+            ts(T.ol[:, o + 16:o + 32], T.pos[:], S20, None, OP.mult, None, ["pos"], ["ol%d" % (o + 16)])
+        ts(T.ol[:, 32:48], T.dump[:, 0:16], S20, None, OP.mult, None, ["dumpa"], ["ol32"])
+        ts(T.ol[:, 80:96], T.dump[:, 16:32], S20, None, OP.mult, None, ["dumpb%d" % j for j in range(4)], ["ol80"])
+        tt(T.cx[:, 0:16], T.l32[:, 0:16], T.dump[:, 0:16], OP.subtract, ["l32a", "dumpa"], ["cx0"])
+        tt(T.cx[:, 16:32], T.l32[:, 16:32], T.dump[:, 0:16], OP.subtract, ["l32b", "dumpa"], ["cx1"])
+        tt(T.cx[:, 32:48], T.l32[:, 16:32], T.dump[:, 16:32], OP.subtract, ["l32b"] + ["dumpb%d" % j for j in range(4)], ["cx2"])
+        for j in range(1, 4):
+            ts(T.cx[:, 32 + 4 * j:36 + 4 * j], T.cx[:, 32 + 4 * j:36 + 4 * j], float(-YH * j), None, OP.add, None, ["cx2"],
+               ["cx2"])
+        ms(T.dd[:, 16:32], L * S20, ["ddz"])
+        for n in (1, 2, 3, 4):
+            ms(T["c%d" % n][:], 1.0, ["c%d" % n])
+        ts(T.id16[:], T.id1[:], 16.0, None, OP.mult, None, ["id1"], ["id16"])
+        ms(T.X[:, W:W + L], 0.0, ["Xd"])
+        for hf in range(2):
+            ms(T.Y[:, hf * YW + YH:hf * YW + YW], 0.0, ["Yd%d" % hf])
+        for t in range(ROUNDS):
+            ms(T["ly%d" % t][:, L:2 * L], LIFT, ["lyc%d" % t])
+
+    def newz(t, lo, hi):
+        ly = T["ly%d" % t]
+        tt(T.zl[:, lo:hi], ly[:].indirect(T.off[:, 16 + lo // 16:16 + hi // 16]), T.base[:, lo:hi], OP.add,
+           ["ly", "lyc%d" % t, "off", "base"], qs(lo, hi, "zl"))
+        ts(T.z[:, lo:hi], T.zl[:, lo:hi], -LIFT, 1.0, OP.add, OP.max, qs(lo, hi, "zl"), qs(lo, hi, "z"))
+
+    for t in range(ROUNDS):
+        last = t == ROUNDS - 1
+        par = t % 2
+        sv, lv, yh, ly = T["sv%d" % t], T["lv%d" % t], T["yh%d" % t], T["ly%d" % t]
+        pJ = T.pP[:, 0:L]
+        zparts = CFG["z"] if t > 0 else {(0, 0): ((0, L),)}
+        ubank = {}
+
+        def demands(lo, hi):
+            if t > 0:
+                newz(t - 1, lo, hi)
+            bank = ("pU", "pY1", "pY0")[len(set(ubank.values()))]
+            for q in range(lo // 16, hi // 16):
+                ubank[q] = bank
+            mm(T[bank][:, lo:hi], T.w2[:], T.z[:, lo:hi], True, True, ["w2"] + qs(lo, hi, "z"), qs(lo, hi, "u"), [bank])
+
+        def picks(step, lo, hi):
+            s = str(lo)
+            bank = ubank[lo // 16]
+            if step == 0:
+                ts(T.ha[:, lo:hi], T[bank][:, lo:hi], 1.0, None, OP.add, None, qs(lo, hi, "u"), ["ha" + s], [bank])
+            elif step == 1:
+                ts(T.hb[:, lo:hi], T.ha[:, lo:hi], 2047, None, OP.bitwise_and, None, ["ha" + s], ["hb" + s])
+            elif step == 2:
+                tt(T.hc[:, lo:hi], T.hb[:, lo:hi], T.pP[:, lo:hi], OP.mult, ["hb" + s, "pJ"], ["hc" + s], ["pP"])
+            elif step == 3:
+                tt(T.hd[:, lo:hi], T.hc[:, lo:hi], T.pP[:, L + lo:L + hi], OP.add, ["hc" + s, "pJA"], ["hd" + s], ["pP"])
+            elif step == 4:
+                ts(T.he[:, lo:hi], T.hd[:, lo:hi], 5, W - 1, OP.arith_shift_right, OP.bitwise_and, ["hd" + s], ["he" + s])
+            else:
+                cp(T.hu[:, lo:hi], T.he[:, lo:hi], ["he" + s], qs(lo, hi, "hu"))
+
+        for n, group in enumerate(CFG["h"]):
+            for step in range(6):
+                for lo, hi in zparts.get((n, step), ()):
+                    demands(lo, hi)
+                for lo, hi in group:
+                    picks(step, lo, hi)
+        for hf in range(2):
+            for r in range(4):
+                mm(T["pZ%d" % hf][:, r::4], T.id1[:], T.z[:, 128 * hf:128 * hf + 128], True, True, ["id1"] + zall,
+                   ["zp%d" % hf], ["pZ%d" % hf])
+        mm(T.pT[:, 0:L], T.c19[:], T.ones[:], True, False, ["c19", "ones"], ["tsum"], ["pT"])
+        early = last and CFG["early"]
+
+        def ulanes():
+            for q in range(16):
+                mm(T.pU[:, L:L + 16], T.wband[:, 15 - q:143 - q], T.z[:, 16 * q:16 * q + 16], q == 0, q == 15,
+                   ["wband"] + zall, ["ul"], ["pU"])
+
+        def record():
+            cxo = 32 if last else 16 * par
+            cp(T.ti[:], T.pU[:, L:L + 16], ["ul"], ["ti"], ["pU"])
+            if not early:
+                blocks()
+            ts(T.rc[:], T.ti[:], 31, None, OP.bitwise_and, None, ["ti"], ["rc"])
+            tt(T.rf[:], T.rc[:], T.l32[:, 16 * par:16 * par + 16], OP.add, ["rc", "l32a", "l32b"], ["rf"])
+            tt(T.dx[:], T.rc[:], T.cx[:, cxo:cxo + 16], OP.add, ["rc", "cx0", "cx1", "cx2"], ["dx"])
+            cp(T.offr[:], T.rf[:], ["rf"], ["offr"])
+
+        def halves():
+            act(T.oq[:], T.X[:, 0:W].indirect(T.offr[:]), AF.Identity, xall + ["offr"], ["oq"], bias=LIFT - 0.25,
+                scale=-0.5 if last else 0.5)
+            act(T.dd[:, 32:48], T.dx[:], AF.Identity, ["dx"], ["ddx"], scale=S20)
+
+        def blocks():
+            tt(T.dd[:, 0:16], T.k4[:, 1::2], T.kb[:], OP.subtract, ["k4", "kb"], ["ddj"])
+            scan(sv[:, 64:96], T.c4[:], T.t3[:, 1::2], OP.max, OP.min, ["c4", "t3"], ["t4b"])
+
+        if early:
+            ulanes()
+            record()
+        if t == 0:
+            late_constants()
+        for lo, hi in CFG["ga"]:
+            act(T.xg[:, 16 * lo:16 * hi], T.X[:, 0:W].indirect(T.hu[:, lo:hi]), AF.Identity,
+                xall + qs(lo, hi, "hu"), qs(lo, hi, "x"))
+        for lo, hi in CFG["gv"]:
+            cp(T.xg[:, 16 * lo:16 * hi], T.X[:, 0:W].indirect(T.hu[:, lo:hi]), xall + qs(lo, hi, "hu"), qs(lo, hi, "x"))
+
+        def mins(n):
+            lo, hi = CFG["m"][n]
+            hf = lo // 128
+            for k in range(4):
+                tt(T.mn[:, 16 * lo + k:16 * hi:4], T.xg[:, 16 * lo + k:16 * hi:4],
+                   T["pZ%d" % hf][:, 4 * (lo - 128 * hf):4 * (hi - 128 * hf)], OP.min,
+                   qs(lo, hi, "x") + ["zp%d" % hf], ["m%d.%d" % (n, k)], ["pZ%d" % hf])
+
+        def sums(n, kind):
+            lo, hi = CFG["m"][n]
+            for q in range(lo // 16, hi // 16):
+                if kind == "x":
+                    mm(T.pT[:, 0:L], T.band[:, 15 - q:143 - q], T.xg[:, L * q:L * q + L], False, q == 15,
+                       ["band", "x%d" % q], ["tsum"], ["pT"])
+                else:
+                    mm(T.pG[:, 0:L], T.band[:, 15 - q:143 - q], T.mn[:, L * q:L * q + L], q == 0, q == 15,
+                       ["band"] + ["m%d.%d" % (n, k) for k in range(4)], ["gsum"], ["pG"])
+
+        def runmax(lo, hi):
+            scan(T.pm[:, 16 * lo:16 * hi], T.mask[:, 0:16 * (hi - lo)], T.xg[:, 16 * lo:16 * hi], OP.mult, OP.max,
+                 ["mask"] + qs(lo, hi, "x"), qs(lo, hi, "pm"))
+
+        nm = len(CFG["m"])
+        sums(0, "x")
+        for n in range(nm):
+            mins(n)
+            if n in CFG["gap"]:
+                runmax(*CFG["gap"][n])
+            if n + 1 < nm:
+                sums(n + 1, "x")
+            sums(n, "m")
+        act(T.bw[:, 0:L], T.z[:].indirect(T.colu[:]), AF.Identity, zall + ["colu"], ["zq"], bias=LIFT - 0.25, scale=0.5)
+
+        def pack(blk):
+            bank = "pY%d" % (blk % 2)
+            c0 = 512 * blk
+            mm(T[bank][:], T.id1[:], T.X[:, c0:c0 + 512], True, False, ["id1"] + xall, [bank + "d"], [bank])
+            mm(T[bank][:], T.id16[:], T.X[:, W // 2 + c0:W // 2 + c0 + 512], False, True, ["id16"] + xall, [bank + "d"], [bank])
+            y0 = c0 + (YW - YH) * (blk // 4)
+            act(T.Y[:, y0:y0 + 512], T[bank][:], AF.Identity, [bank + "d"], ["Y%d" % blk], [bank])
+
+        if early:
+            halves()
+        else:
+            ulanes()
+        if last:
+            for blk in range(CFG["yearly"]):
+                pack(blk)
+        for lo, hi in CFG["pre"]:
+            runmax(lo, hi)
+        ks = []
+        klate = CFG["klate"] or (last and CFG["lastlate"])
+        fill = [] if klate else list(CFG["fill"])
+
+        def filler():
+            if fill:
+                runmax(*fill.pop(0))
+
+        def kscan(n):
+            src = T.kc[:] if n == 1 else T["k%d" % (n - 1)][:, 1::2]
+            scan(T["k%d" % n][:], T["c%d" % n][:], src, OP.max, OP.min, ["c%d" % n, "kc" if n == 1 else "k%d" % (n - 1)], ["k%d" % n])
+
+        def kstep(n):
+            if klate:
+                ks.append(n)
+            else:
+                kscan(n)
+
+        scan(T.ts[:], T.mask[:, 0:L], T.pT[:, 0:L], OP.mult, OP.add, ["mask", "tsum"], ["ts"], ["pT"])
+        scan(T.gs[:], T.mask[:, 0:L], T.pG[:, 0:L], OP.mult, OP.add, ["mask", "gsum"], ["gs"], ["pG"])
+        tt(T.pP[:, 0:128], T.pG[:, 1:L:2], T.ts[:, 0::2], OP.mult, ["gsum", "ts"], ["pJ"], ["pG", "pP"])
+        tt(T.pb[:], T.pT[:, 1:L:2], T.gs[:, 0::2], OP.mult, ["tsum", "gs"], ["pb"], ["pT"])
+        filler()
+        tt(T.c1[:, 1::2], T.pP[:, 0:128], T.pb[:], OP.is_gt, ["pJ", "pb"], ["c1"], ["pP"])
+        filler()
+        scan(T.pP[:, L:2 * L], T.c1[:], T.gs[:], OP.max, OP.min, ["c1", "gs"], ["pJA"], ["pP"])
+        scan(T.t1[:], T.c1[:], T.ts[:], OP.max, OP.min, ["c1", "ts"], ["t1"])
+        kstep(1)
+        tt(T.pP[:, 0:64], T.pP[:, L + 3:2 * L:4], T.t1[:, 1::4], OP.mult, ["pJA", "t1"], ["pJ"], ["pP"])
+        tt(T.pb[:, 0:64], T.pP[:, L + 1:2 * L:4], T.t1[:, 3::4], OP.mult, ["pJA", "t1"], ["pb"], ["pP"])
+        filler()
+        tt(T.c2[:, 1::2], T.pP[:, 0:64], T.pb[:, 0:64], OP.is_gt, ["pJ", "pb"], ["c2"], ["pP"])
+        filler()
+        scan(T.g2[:], T.c2[:], T.pP[:, L + 1:2 * L:2], OP.max, OP.min, ["c2", "pJA"], ["g2"], ["pP"])
+        scan(T.t2[:], T.c2[:], T.t1[:, 1::2], OP.max, OP.min, ["c2", "t1"], ["t2"])
+        kstep(2)
+        for n, cnt in ((3, 32), (4, 16)):
+            gi, ti_, c_ = T["g%d" % (n - 1)], T["t%d" % (n - 1)], T["c%d" % n]
+            gn, tn, cn = "g%d" % (n - 1), "t%d" % (n - 1), "c%d" % n
+            tt(T.pa[:, 0:cnt], gi[:, 3::4], ti_[:, 1::4], OP.mult, [gn, tn], ["pa"])
+            tt(T.pb[:, 0:cnt], gi[:, 1::4], ti_[:, 3::4], OP.mult, [gn, tn], ["pb"])
+            filler()
+            tt(c_[:, 1::2], T.pa[:, 0:cnt], T.pb[:, 0:cnt], OP.is_gt, ["pa", "pb"], [cn])
+            filler()
+            go, to = (T.g3[:], T.t3[:]) if n == 3 else (sv[:, 32:64], sv[:, 0:32])
+            scan(go, c_[:], gi[:, 1::2], OP.max, OP.min, [cn, gn], ["g%d" % n])
+            scan(to, c_[:], ti_[:, 1::2], OP.max, OP.min, [cn, tn], ["t%d" % n])
+            if n == 4:
+                swap(t, lv[:], sv[:, 0:64], ["g4", "t4"], "lv", "av%d" % t)
+            kstep(n)
+        post = (list(CFG["fill"]) if klate else fill) + list(CFG["post"])
+        for n in ks:
+            kscan(n)
+            if len(post) > 1:
+                runmax(*post.pop(0))
+        ts(T.offy[:], T.k4[:, 1::2], 4096.0, None, OP.mult, None, ["k4"], ["offy"])
+        for lo, hi in post:
+            runmax(lo, hi)
+        act(yh[:], T.pm[:].indirect(T.offy[:]), AF.Identity, qs(0, L, "pm") + ["offy"], ["yh"], scale=0.5)
+        swap(t, ly[:, 0:L], yh[:], ["yh"], "ly", "ay%d" % t)
+        if early:
+            blocks()
+        else:
+            record()
+            halves()
+        ys = [["Y%d" % b for b in range(4 * hf, 4 * hf + 4)] + ["Yd%d" % hf] for hf in range(2)]
+
+        def winz():
+            tt(T.dz[:], T.bw[:, 0:L], yh[:], OP.subtract, ["zq", "yh"], ["dz"])
+            act(T.bw[:, L:2 * L], T.dz[:], AF.Abs, ["dz"], ["zw"], bias=0.5 - 2 * LIFT, scale=2.0)
+
+        dzlate = last and CFG["dzlate"]
+        if not dzlate:
+            winz()
+        tt(T.rec[:], T.oq[:], yh[:], OP.add, ["oq", "yh"], ["rec"])
+        if last:
+            for blk in range(CFG["yearly"], 8):
+                pack(blk)
+            ts(T.d1[:], T.rec[:, 0:128], -LIFT, None, OP.add, None, ["rec"], ["d1"])
+            ts(T.d16[:], T.rec[:, 128:L], -LIFT, 16.0, OP.add, OP.mult, ["rec"], ["d16"])
+            tt(T.ya[:, 0:64], T.Y[:, 0:YW].indirect(T.offr[:, 0:4]), T.d1[:, 0:64], OP.add, ys[0] + ["offr", "d1"], ["ya0"])
+            tt(T.ya[:, 64:128], T.Y[:, YW - YH:2 * YW].indirect(T.offr[:, 4:8]), T.d1[:, 64:128], OP.add,
+               ys[0] + ys[1] + ["offr", "d1"], ["ya1"])
+        tt(T.qq[:], sv[:, 33:96:2], lv[:, 1::2], OP.mult, ["g4", "t4b", "lv"], ["qq"])
+        tt(T.win[:], T.qq[:, 0:16], T.qq[:, 16:32], OP.is_ge if rank < (rank ^ STEPS[t]) else OP.is_gt, ["qq"], ["win"])
+        tt(T.wd[:], T.win[:].indirect(T.repu[:, 0:3]), T.dd[:], OP.mult, ["win", "repu", "ddj", "ddz", "ddx"], ["wd"])
+        if not last:
+            tt(T.sb[:], T.win[:], T.dd[:, 0:16], OP.mult, ["win", "ddj"], ["sb"])
+            mm(T.pU[:, L + 16:L + 32], T.c4096[:], T.sb[:], True, True, ["c4096", "sb"], ["asum"], ["pU"])
+        o = 48 if last else 0
+        tt(T.oo[:], T.wd[:], T.ol[:, o:o + 48], OP.add, ["wd"] + ["ol%d" % (o + d) for d in (0, 16, 32)], ["oo"])
+        ts(T.off[:], T.oo[:], 2.0 ** 20, None, OP.mult, None, ["oo"], ["off"])
+        nxt = T.jfin[:] if last else tw[t + 1][:, 0:L]
+        for what in (CFG["order"] if not last else "j" if dzlate else "bj"):
+            if what == "a":
+                act(T.aj[:], T.pU[:, L + 16:L + 32], AF.Identity, ["asum"], ["acol"], ["pU"], bias=-DROP / 16, scale=32.0,
+                    acc=T.acol[:, 0:1])
+            elif what == "b":
+                act(T.base[:], T.bw[:].indirect(T.off[:, 16:32]), AF.Identity, ["zq", "zw", "off"], ["base"])
+            else:
+                act(nxt, tw[t][:].indirect(T.off[:, 0:16]), AF.Identity,
+                    ["off", "j%d" % t, "jr%d" % t] + ["to%d.%d" % (t, k) for k in range(15)]
+                    + ["tr%d.%d" % (t, k) for k in range(1, 16)], ["j%d" % (t + 1)])
+        if not last:
+            lists(t + 1, [])
+            tt(T.X[:, 0:W + L].indirect(T.off[:, 32:48]), T.rec[:], T.neg[:], OP.add, ["off", "rec", "neg", "Xd"], xall)
+            act(pJ, nxt, AF.Identity, ["j%d" % (t + 1)], ["pJ"], ["pP"])
+            act(T.pP[:, L:2 * L], nxt, AF.Identity, ["j%d" % (t + 1), "acol"], ["pJA"], ["pP"], bias=T.acol[:, 0:1], scale=32.0)
+        else:
+            for hf in range(2):
+                yw, c = T.Y[:, hf * YW:hf * YW + YW], 64 * hf
+                lo, hi = T.off[:, 32 + 4 * hf:36 + 4 * hf], T.off[:, 40 + 4 * hf:44 + 4 * hf]
+                cp(yw.indirect(lo), T.ya[:, c:c + 64], ["off", "ya%d" % hf], ys[hf])
+                tt(T.yb[:, c:c + 64], yw.indirect(hi), T.d16[:, c:c + 64], OP.add, ys[hf] + ["off", "d16"], ["yb%d" % hf])
+                cp(yw.indirect(hi), T.yb[:, c:c + 64], ["off", "yb%d" % hf], ys[hf])
+                dma("s", T.yx[:, hf * YH:hf * YH + YH], T.Y[:, hf * YW:hf * YW + YH], ys[hf], ["yx%d" % hf], "outx")
+            dma("a", T.yj[:], T.jfin[:], ["j4"] + ys[0], ["yj"], "outj")
+            if dzlate:
+                winz()
+                act(T.base[:], T.bw[:].indirect(T.off[:, 16:32]), AF.Identity, ["zq", "zw", "off"], ["base"])
+            newz(t, 0, L)
+    dma("a", T.yz[:], T.z[:], zall, ["yz"], "outz")
+    add("s", None, ["yj", "yx0", "yx1", "yz"])
+    emit(g, T, ops)
+    g.wait_ge(T.sem.sent, sent[0])

@@ -6,6 +6,7 @@ ROUNDS = 4
 STEPS = (1, 2, 3, 1)
 W = 8192
 L = 256
+FA = 64
 YH, YW = 2048, 2176
 SLABS = 17
 S12 = 2.0 ** -12
@@ -14,60 +15,56 @@ LIFT = 192.0
 DROP = 32.0 * 5 * W
 
 CFG = {
-    "h": (((0, 64), (64, 128)), ((128, 192), (192, 256))),
-    "ga": ((0, 64), (64, 128), (128, 192), (192, 224), (224, 256)),
-    "gv": (),
-    "m": ((0, 64), (64, 128), (128, 192), (192, 224), (224, 256)),
-    "gap": {0: (0, 64), 1: (64, 128)},
-    "pre": ((128, 160),),
-    "fill": (),
-    "post": ((160, 256),),
-    "klate": False,
-    "lastlate": True,
-    "yearly": 6,
-    "z": {(0, 0): ((0, 128), (128, 256))},
+    "phase": "dd T0 m0dddd G0 dsds| g3 T1 m1 G1 T2 ssss g4 a00 a01 T3 m2 G2 m3 G3 T4 p00 p01 a10 t0a ss m4 p10 G4 a11 t1a p11 i LL",
+    "meet": "MMlMlMlM l S l S l S P S P P",
+    "scat": (64, 64, 64, 64),
     "own": 3,
-    "early": True,
-    "dzlate": True,
-    "order": "ajb",
+    "yearly": 4,
 }
+PIECES = ((0, 4), (4, 8), (8, 12), (12, 14), (14, 16))
+
+PLACE = ((("pH0", 0, 256), ("pH0", 128, 384)), (("pZ0", 0, 128), ("pH1", 0, 128)))
+
+TURN_Q = ((32, 2), (2, 0), (16, 3), (1, 0))
+TURN_C = (((4, 8),), ((1, 2), (32, 4)), ((2, 8),), ((16, 8),))
 
 F, B, I, U = "float32", "bfloat16", "int32", "uint16"
 SCRATCH = {
-    "X": ("sbuf", [128, W + L], B), "Y": ("sbuf", [128, W // 2 + L], B),
-    "xg": ("sbuf", [128, 16 * L], B), "mn": ("sbuf", [128, 16 * L], B), "pm": ("sbuf", [128, 16 * L], B),
-    "mask": ("sbuf", [128, 16 * L], B),
-    "jin": ("sbuf", [128, L], I), "z": ("sbuf", [128, L], B), "w": ("sbuf", [128, 8], F),
-    "ij": ("sbuf", [128, L], F), "pi": ("sbuf", [128, 8], I), "qi": ("sbuf", [128, 8], I),
-    "q1": ("sbuf", [128, 8], F), "q16": ("sbuf", [128, 8], F), "q256": ("sbuf", [128, 8], F),
+    "X": ("sbuf", [128, W + L], B), "Y": ("sbuf", [128, 2 * YW], B),
+    "xg": ("sbuf", [128, 16 * L], B), "mn": ("sbuf", [128, 16 * L], B), "pm": ("sbuf", [128, 16 * L], B), "mask": ("sbuf", [128, L], B),
+    "jin": ("sbuf", [128, L], I), "zin": ("sbuf", [128, L], B), "z": ("sbuf", [128, L], B), "w": ("sbuf", [128, 8], F),
+    "kv": ("sbuf", [128, L], F), "pi": ("sbuf", [128, 8], I), "lt": ("sbuf", [128, 112], F),
+    "q1": ("sbuf", [128, 16], F),
     "bandv": ("sbuf", [128, 144], F), "blkv": ("sbuf", [128, 128], F),
-    "bm": ("sbuf", [128, 144], B), "band": ("sbuf", [128, 144], B), "wband": ("sbuf", [128, 144], B),
+    "bm": ("sbuf", [128, 144], B), "wband": ("sbuf", [128, 144], B),
     "blkm": ("sbuf", [128, 128], B), "w2": ("sbuf", [128, 128], B),
-    "id1": ("sbuf", [128, 128], B), "id16": ("sbuf", [128, 128], B),
-    "c19": ("sbuf", [128, 128], B), "c4096": ("sbuf", [128, 128], B),
-    "ones": ("sbuf", [128, L], B), "neg": ("sbuf", [128, L], B),
-    "kc": ("sbuf", [128, L], F), "kb": ("sbuf", [128, 16], F),
-    "col": ("sbuf", [128, 16], F), "pos": ("sbuf", [128, 16], F),
-    "colu": ("sbuf", [128, 16], U), "repu": ("sbuf", [128, 16], U),
-    "l32": ("sbuf", [128, 32], F), "cx": ("sbuf", [128, 48], F), "dump": ("sbuf", [128, 32], F),
-    "ol": ("sbuf", [128, 96], F), "dd": ("sbuf", [128, 48], F),
+    "id1": ("sbuf", [128, 128], B), "id16": ("sbuf", [128, 128], B), "idm2": ("sbuf", [128, 128], B),
+    "idh": ("sbuf", [128, 128], B), "idmh": ("sbuf", [128, 128], B),
+    "trv": ("sbuf", [128, 128], B), "tri": ("sbuf", [128, 128], B), "c4096": ("sbuf", [128, 128], F),
+    "ssb": ("sbuf", [128, 512], B), "neg": ("sbuf", [128, L], B),
+    "kc": ("sbuf", [128, L], F), "kb": ("sbuf", [128, 16], F), "pos": ("sbuf", [128, 32], F),
+    "repu": ("sbuf", [128, 48], U), "l32": ("sbuf", [128, 64], F), "cx": ("sbuf", [128, 64], F),
+    "ol": ("sbuf", [128, 48], F), "dd": ("sbuf", [128, 48], F),
     "c1": ("sbuf", [128, 256], F), "c2": ("sbuf", [128, 128], F), "c3": ("sbuf", [128, 64], F), "c4": ("sbuf", [128, 32], F),
     "ha": ("sbuf", [128, L], I), "hb": ("sbuf", [128, L], I), "hc": ("sbuf", [128, L], F), "hd": ("sbuf", [128, L], I),
     "he": ("sbuf", [128, L], I), "hu": ("sbuf", [128, L], U),
+    "wa": ("sbuf", [128, 2 * FA], I), "wc": ("sbuf", [128, FA], F), "jw": ("sbuf", [128, 3 * FA], F),
+    "hw": ("sbuf", [128, L + FA], F), "zz": ("sbuf", [128, L + FA], B),
     "ti": ("sbuf", [128, 16], I), "rc": ("sbuf", [128, 16], I), "rf": ("sbuf", [128, 16], F), "dx": ("sbuf", [128, 16], F),
     "offr": ("sbuf", [128, 16], U), "offy": ("sbuf", [128, 16], U), "off": ("sbuf", [128, 48], U),
-    "gs": ("sbuf", [128, 256], F), "ts": ("sbuf", [128, 256], F), "pb": ("sbuf", [128, 128], F), "pa": ("sbuf", [128, 32], F),
+    "ow": ("sbuf", [128, 8], F), "offw": ("sbuf", [128, 8], U),
+    "ts": ("sbuf", [128, 256], F), "pb": ("sbuf", [128, 128], F), "pa": ("sbuf", [128, 32], F),
     "t1": ("sbuf", [128, 256], F), "k1": ("sbuf", [128, 256], F),
     "g2": ("sbuf", [128, 128], F), "t2": ("sbuf", [128, 128], F), "k2": ("sbuf", [128, 128], F),
     "g3": ("sbuf", [128, 64], F), "t3": ("sbuf", [128, 64], F), "k3": ("sbuf", [128, 64], F), "k4": ("sbuf", [128, 32], F),
     "qq": ("sbuf", [128, 32], F), "win": ("sbuf", [128, 16], F), "wd": ("sbuf", [128, 48], F), "oo": ("sbuf", [128, 48], F),
-    "sb": ("sbuf", [128, 16], B), "aj": ("sbuf", [128, 16], F), "acol": ("sbuf", [128, 8], F),
-    "bw": ("sbuf", [128, 2 * L], F), "dz": ("sbuf", [128, L], F), "base": ("sbuf", [128, L], F), "oq": ("sbuf", [128, L], F),
+    "aj": ("sbuf", [128, 16], F), "acol": ("sbuf", [128, 8], F),
+    "bw": ("sbuf", [128, 2 * L], F), "base": ("sbuf", [128, L], F), "old": ("sbuf", [128, L], B),
     "rec": ("sbuf", [128, L], B), "zl": ("sbuf", [128, L], B),
     "d1": ("sbuf", [128, 128], B), "d16": ("sbuf", [128, 128], B), "ya": ("sbuf", [128, 128], B), "yb": ("sbuf", [128, 128], B),
     "jfin": ("sbuf", [128, L], F),
-    "pU": ("psum", [128, 512], F), "pZ0": ("psum", [128, 512], F), "pZ1": ("psum", [128, 512], F), "pG": ("psum", [128, 512], F),
-    "pT": ("psum", [128, 512], F), "pP": ("psum", [128, 512], F), "pY0": ("psum", [128, 512], F), "pY1": ("psum", [128, 512], F),
+    "pH0": ("psum", [128, 512], F), "pH1": ("psum", [128, 512], F), "pZ0": ("psum", [128, 512], F), "pZ1": ("psum", [128, 512], F),
+    "pU": ("psum", [128, 512], F), "pP": ("psum", [128, 512], F), "pD": ("psum", [128, 512], F), "pA": ("psum", [128, 512], F),
 }
 SEMAPHORES = ["v", "a", "p", "g", "ldz", "ldw", "ldj", "ldx", "ldx2", "sent", "outj", "outz", "outx"]
 for _t in range(ROUNDS):
@@ -78,7 +75,7 @@ for _t in range(ROUNDS):
     SCRATCH["ly%d" % _t] = ("sbuf", [128, 2 * L], B)
     SCRATCH["do%d" % _t] = ("dram", [8, 16 * L], F)
     SCRATCH["dr%d" % _t] = ("dram", [8, 16 * L], F)
-    SEMAPHORES += ["aj%d" % _t, "av%d" % _t, "ay%d" % _t, "so%d" % _t, "sr%d" % _t, "tp%d" % _t]
+    SEMAPHORES += ["aj%d" % _t, "av%d" % _t, "ay%d" % _t, "ab%d" % _t, "so%d" % _t, "sr%d" % _t, "tp%d" % _t]
 
 
 def emit(g, T, ops):
@@ -168,6 +165,14 @@ def emit(g, T, ops):
                 ins.then_inc(T.sem[e], 1)
 
 
+def weave(*chains):
+    chains = [list(c) for c in chains]
+    while any(chains):
+        for c in chains:
+            if c:
+                c.pop(0)()
+
+
 def rank_program(g, core, T, topo):
     rank = T.rank_of(core)
     if rank is None:
@@ -210,18 +215,18 @@ def rank_program(g, core, T, topo):
         q = g.sync if e == "s" else g.scalar
         add(e, lambda: q.dma_start(out, in_), rd, wr, (), sem)
 
-    def iota(out, pat, mult, wr, flag=True):
+    def iota(out, pat, mult, wr, flag=True, base=0):
         if flag:
-            add("g", lambda: g.iota(out, pat, 0, mult, allow_small_or_imprecise_dtypes=True), (), wr)
+            add("g", lambda: g.iota(out, pat, base, mult, allow_small_or_imprecise_dtypes=True), (), wr)
         else:
             add("g", lambda: g.iota(out, pat, 0, mult), (), wr)
 
-    def swap(t, out, in_, rd, tok, sem):
+    def swap(t, out, in_, rd, toks, sem):
         peer = T.cores[rank ^ STEPS[t]]
         rid, pid, _ = topo.addr(peer)
         add("g", lambda: g.remote_dma(out, in_, T.sem[sem], T.sem.sent, pid, rid, topo.mask(core, peer)), rd, (), (), "")
         sent[0] += len(topo.engines(core, peer))
-        add(None, None, (), [tok], ext=(sem, len(topo.engines(peer, core))))
+        add(None, None, (), toks, ext=(sem, len(topo.engines(peer, core))))
 
     def qs(lo, hi, name):
         return ["%s%d" % (name, q) for q in range(lo // 16, hi // 16)]
@@ -231,7 +236,7 @@ def rank_program(g, core, T, topo):
 
     def lists(t, after):
         w_, do, dr = tw[t], T["do%d" % t], T["dr%d" % t]
-        swap(t, w_[:, 16 * L:17 * L], w_[:, 0:L], ["j%d" % t] + after[:1], "jr%d" % t, "aj%d" % t)
+        swap(t, w_[:, 16 * L:17 * L], w_[:, 0:L], ["j%d" % t] + after[:1], ["jr%d" % t], "aj%d" % t)
         dma("s", do[:], w_[:, 0:L], ["j%d" % t] + after, ["do%d" % t], "so%d" % t)
         for k in range(15):
             if k == (0 if t == 0 else CFG["own"]):
@@ -240,317 +245,416 @@ def rank_program(g, core, T, topo):
         for k in range(1, 16):
             dma("s", w_[k::16, (16 - k) * L:16 * L], dr[:, 0:k * L], ["dr%d" % t], ["tr%d.%d" % (t, k)], "tp%d" % t)
 
-    dma("s", T.z[:], T.zd[:], (), zall, "ldz")
+    def shifted(t):
+        return (["j%d" % t, "jr%d" % t] + ["to%d.%d" % (t, k) for k in range(15)] + ["tr%d.%d" % (t, k) for k in range(1, 16)])
+
+    dma("s", T.zin[:], T.zd[:], (), ["zin"], "ldz")
     dma("a", T.X[:, 0:W // 2], T.xt[:, 0:W // 2], (), ["X"], "ldx")
     dma("s", T.w[:, 0:1], T.wt[:], (), ["w"], "ldw")
     dma("s", T.jin[:], T.jn[:], (), ["jin"], "ldj")
     dma("s", T.X[:, W // 2:W], T.xt[:, W // 2:W], (), ["X2"], "ldx2")
     iota(T.pi[:, 0:1], [[0, 1]], 1, ["pi"], False)
     iota(T.blkv[:], [[16, 8], [0, 16]], -1, ["blkv"])
+    iota(T.lt[:, 64:80], [[128, 2], [1, 4], [64, 2]], 0, ["lt4"])
     iota(T.bandv[:], [[1, 144]], -1, ["bandv"])
-    iota(T.ij[:], [[1, L]], 0, ["ij"])
-    q1, q16, q256, w = T.q1[:, 0:1], T.q16[:, 0:1], T.q256[:, 0:1], T.w[:, 0:1]
-    nmask = 16 * max(hi - lo for lo, hi in list(CFG["pre"]) + list(CFG["post"]) + list(CFG["fill"]) + list(CFG["gap"].values()))
-    ms(T.c19[:], 2.0 ** -19, ["c19"])
-    ms(T.ones[:], 1.0, ["ones"])
-    ts(T.qi[:, 0:1], T.pi[:, 0:1], 15, None, OP.bitwise_and, None, ["pi"], ["qi"])
-    ms(T.neg[:], -LIFT, ["neg"])
-    cp(q1, T.qi[:, 0:1], ["qi"], ["q1"])
-    ms(T.c4096[:], 4096.0, ["c4096"])
+    iota(T.kv[:], [[8 * L, 2], [16, 8], [1, 16]], 0, ["kv"])
+    for t, pat in enumerate(TURN_C):
+        iota(T.lt[:, 16 * t:16 * t + 16], [[32 * 128, 2]] + [[32 * s, n] for s, n in pat], 0, ["lt%d" % t])
+    iota(T.lt[:, 80:96], [[31 * 64 + 64 - YH, 4], [31 * 16, 4]], 0, ["lt5"], base=-YH)
+    iota(T.lt[:, 96:112], [[0, 4], [16, 4]], 0, ["lt6"], base=YH)
+    q1, q128, q4, q31, w = T.q1[:, 0:1], T.q1[:, 1:2], T.q1[:, 2:3], T.q1[:, 3:4], T.w[:, 0:1]
+    pos, col, colu, firstu = T.pos[:, 0:16], T.pos[:, 16:32], T.repu[:, 16:32], T.repu[:, 32:48]
+    ms(T.mask[:], 1.0, ["mask"])
+    ts(T.pi[:, 1:2], T.pi[:, 0:1], 15, None, OP.bitwise_and, None, ["pi"], ["qi"])
+    ts(T.pi[:, 2:3], T.pi[:, 0:1], 2, 3, OP.arith_shift_right, OP.bitwise_and, ["pi"], ["qi2"])
+    ts(T.pi[:, 3:4], T.pi[:, 0:1], 3, 1, OP.arith_shift_right, OP.bitwise_and, ["pi"], ["qi3"])
+    cp(q1, T.pi[:, 1:2], ["qi"], ["q1"])
+    ms(T.mask[:, 0::16], 0.0, ["mask"])
+    ts(q4, q1, 4.0, None, OP.mult, None, ["q1"], ["q4"])
     ts(T.blkm[:], T.blkv[:], q1, 0.0, OP.add, OP.is_equal, ["blkv", "q1"], ["blkm"])
-    ts(q16, q1, 16.0, None, OP.mult, None, ["q1"], ["q16"])
-    ts(q256, q1, 256.0, None, OP.mult, None, ["q1"], ["q256"])
-    ts(T.bm[:], T.bandv[:], q1, 15.0, OP.add, OP.is_equal, ["bandv", "q1"], ["bm"])
+    ts(firstu, T.lt[:, 64:80], q4, None, OP.add, None, ["lt4", "q4"], ["firstu"])
+    ts(q128, q1, 128.0, None, OP.mult, None, ["q1"], ["q128"])
+    ts(q31, q1, 31.0, None, OP.mult, None, ["q1"], ["q31"])
+    for t, (m, sh) in enumerate(TURN_Q):
+        ts(T.q1[:, 4 + t:5 + t], q1, 32.0 * m, None, OP.mult, None, ["q1"], ["qa%d" % t])
     ts(T.id1[:], T.bandv[:, 0:128], 0.0, None, OP.is_equal, None, ["bandv"], ["id1"])
-    ms(T.mask[:, 0:nmask], 1.0, ["mask"])
-    ts(T.band[:], T.bm[:], S12, None, OP.mult, None, ["bm"], ["band"])
-    ms(T.mask[:, 0:nmask:16], 0.0, ["mask"])
-    ts(T.col[:], T.ij[:, 0:16], q16, None, OP.add, None, ["ij", "q16"], ["col"])
-    ts(T.pos[:], T.ij[:, 0::16], q1, None, OP.add, None, ["ij", "q1"], ["pos"])
-    ts(T.kc[:], T.ij[:], q256, S12, OP.add, OP.mult, ["ij", "q256"], ["kc"])
+    ts(T.bm[:], T.bandv[:], q1, 15.0, OP.add, OP.is_equal, ["bandv", "q1"], ["bm"])
+    ts(T.trv[:], T.bandv[:, 0:128], 0.0, S12, OP.is_ge, OP.mult, ["bandv"], ["trv"])
+    for t, (m, sh) in enumerate(TURN_Q):
+        if sh:
+            ts(T.q1[:, 4 + t:5 + t], T.pi[:, sh:sh + 1], -32.0 * 127, T.q1[:, 4 + t:5 + t], OP.mult, OP.add,
+               ["qi%d" % sh, "qa%d" % t], ["qa%d" % t])
+    tt(T.tri[:], T.trv[:], T.blkm[:], OP.mult, ["trv", "blkm"], ["tri"])
+    for name, c in (("id16", 16.0), ("idm2", -2.0), ("idh", 0.5), ("idmh", -0.5)):
+        act(T[name][:], T.id1[:], AF.Identity, ["id1"], [name], scale=c)
+    ms(T.dd[:, 16:32], L * S20, ["ddz"])
+    ts(T.kc[:], T.kv[:], q128, S12, OP.add, OP.mult, ["kv", "q128"], ["kc"])
+    ts(T.repu[:, 0:4], T.kv[:, 0:4], 0.0, q1, OP.mult, OP.add, ["kv", "q1"], ["repu"])
+    ts(col, T.kv[:, 0::16], q128, 1.0 / 16, OP.add, OP.mult, ["kv", "q128"], ["col"])
+    ts(T.kb[:], T.kc[:, 0::16], -S12, None, OP.add, None, ["kc"], ["kb"])
+    cp(colu, col, ["col"], ["colu"])
+    ts(T.ol[:, 0:16], col, S20, None, OP.mult, None, ["col"], ["ol0"])
+    for t in range(ROUNDS):
+        ts(T.l32[:, 16 * t:16 * t + 16], T.lt[:, 16 * t:16 * t + 16], T.q1[:, 4 + t:5 + t], None, OP.add, None,
+           ["lt%d" % t, "qa%d" % t], ["l32.%d" % t])
+    ts(T.cx[:, 48:64], T.lt[:, 80:96], q31, None, OP.add, None, ["lt5", "q31"], ["cx3"])
+    ts(pos, T.l32[:, 48:64], 1.0 / 32, float(W), OP.mult, OP.add, ["l32.3"], ["pos"])
+    ts(T.ol[:, 16:32], T.l32[:, 48:64], S20 / 32, None, OP.mult, None, ["l32.3"], ["ol16"])
+    ts(T.ol[:, 32:48], pos, S20, None, OP.mult, None, ["pos"], ["ol32"])
+    for t in range(ROUNDS - 1):
+        tt(T.cx[:, 16 * t:16 * t + 16], T.l32[:, 16 * t:16 * t + 16], pos, OP.subtract, ["l32.%d" % t, "pos"], ["cx%d" % t])
     ts(T.w2[:], T.blkm[:], w, 2.0, OP.mult, OP.mult, ["blkm", "w"], ["w2"])
+    act(T.z[:], T.zin[:].indirect(firstu), AF.Identity, ["zin", "firstu"], zall)
     ts(T.wband[:], T.bm[:], w, None, OP.mult, None, ["bm", "w"], ["wband"])
-    cp(tw[0][:, 0:L], T.jin[:], ["jin"], ["j0"])
+    cp(tw[0][:, 0:L], T.jin[:].indirect(firstu), ["jin", "firstu"], ["j0"])
     lists(0, xall)
-    act(T.pP[:, 0:L], tw[0][:, 0:L], AF.Identity, ["j0"], ["pJ"], ["pP"])
-    act(T.pP[:, L:2 * L], tw[0][:, 0:L], AF.Identity, ["j0"], ["pJA"], ["pP"], bias=-DROP, scale=32.0)
 
-    def late_constants():
-        cp(T.colu[:], T.col[:], ["col"], ["colu"])
-        ts(T.repu[:, 0:4], T.ij[:, 0:4], 0.0, q1, OP.mult, OP.add, ["ij", "q1"], ["repu"])
-        ts(T.kb[:], T.kc[:, 0::16], -S12, None, OP.add, None, ["kc"], ["kb"])
-        ts(T.l32[:, 0:16], T.col[:], 32.0, None, OP.mult, None, ["col"], ["l32a"])
-        ts(T.l32[:, 16:32], T.pos[:], 32.0, None, OP.mult, None, ["pos"], ["l32b"])
-        ts(T.dump[:, 0:16], T.pos[:], float(W), None, OP.add, None, ["pos"], ["dumpa"])
-        for j in range(4):
-            ts(T.dump[:, 16 + 4 * j:20 + 4 * j], T.pos[:, 4 * j:4 * j + 4], float(YH - 64 * j), None, OP.add, None, ["pos"],
-               ["dumpb%d" % j])
-        for o in (0, 48):
-            ts(T.ol[:, o:o + 16], T.col[:], S20, None, OP.mult, None, ["col"], ["ol%d" % o])
-            ts(T.ol[:, o + 16:o + 32], T.pos[:], S20, None, OP.mult, None, ["pos"], ["ol%d" % (o + 16)])
-        ts(T.ol[:, 32:48], T.dump[:, 0:16], S20, None, OP.mult, None, ["dumpa"], ["ol32"])
-        ts(T.ol[:, 80:96], T.dump[:, 16:32], S20, None, OP.mult, None, ["dumpb%d" % j for j in range(4)], ["ol80"])
-        tt(T.cx[:, 0:16], T.l32[:, 0:16], T.dump[:, 0:16], OP.subtract, ["l32a", "dumpa"], ["cx0"])
-        tt(T.cx[:, 16:32], T.l32[:, 16:32], T.dump[:, 0:16], OP.subtract, ["l32b", "dumpa"], ["cx1"])
-        tt(T.cx[:, 32:48], T.l32[:, 16:32], T.dump[:, 16:32], OP.subtract, ["l32b"] + ["dumpb%d" % j for j in range(4)], ["cx2"])
-        for j in range(1, 4):
-            ts(T.cx[:, 32 + 4 * j:36 + 4 * j], T.cx[:, 32 + 4 * j:36 + 4 * j], float(-YH * j), None, OP.add, None, ["cx2"],
-               ["cx2"])
-        ms(T.dd[:, 16:32], L * S20, ["ddz"])
-        for n in (1, 2, 3, 4):
-            ms(T["c%d" % n][:], 1.0, ["c%d" % n])
-        ts(T.id16[:], T.id1[:], 16.0, None, OP.mult, None, ["id1"], ["id16"])
-        ms(T.X[:, W:W + L], 0.0, ["Xd"])
-        for hf in range(2):
-            ms(T.Y[:, hf * YW + YH:hf * YW + YW], 0.0, ["Yd%d" % hf])
-        for t in range(ROUNDS):
-            ms(T["ly%d" % t][:, L:2 * L], LIFT, ["lyc%d" % t])
+    def fill(ap, n, c, wr):
+        iota(ap, [[0, n]], 0, wr, base=int(c))
+
+    for n in (1, 2, 3, 4):
+        fill(T["c%d" % n][:], 512 >> n, 1, ["c%d.0" % n, "c%d.1" % n])
+    fill(T.c4096[:], 128, 4096, ["c4096"])
+    fill(T.neg[:], L, -LIFT, ["neg"])
+    fill(T.X[:, W:W + L], L, 0, ["Xd"])
+    fill(T.zz[:], L + FA, 0, ["zzl", "zzw"])
+    fill(T.hw[:], L + FA, 0, ["hl", "hw"])
+    for t in range(ROUNDS):
+        fill(T["ly%d" % t][:, L:2 * L], L, LIFT, ["lyc%d" % t])
+    for hf in range(2):
+        fill(T.Y[:, hf * YW + YH:hf * YW + YW], YW - YH, 0, ["Yd%d" % hf])
+
+    def forms(src, rd, lo, hi, bias, fb="pP", fo=0):
+        act(T[fb][:, fo + lo:fo + hi], src, AF.Identity, rd[:1], qs(lo, hi, fb + "J"), [fb])
+        act(T[fb][:, L + fo + lo:L + fo + hi], src, AF.Identity, rd, qs(lo, hi, fb + "JA"), [fb], bias=bias, scale=32.0)
+
+    forms(tw[0][:, 0:L], ["j0"], 0, L, -DROP)
 
     def newz(t, lo, hi):
         ly = T["ly%d" % t]
-        tt(T.zl[:, lo:hi], ly[:].indirect(T.off[:, 16 + lo // 16:16 + hi // 16]), T.base[:, lo:hi], OP.add,
-           ["ly", "lyc%d" % t, "off", "base"], qs(lo, hi, "zl"))
-        ts(T.z[:, lo:hi], T.zl[:, lo:hi], -LIFT, 1.0, OP.add, OP.max, qs(lo, hi, "zl"), qs(lo, hi, "z"))
+        return [lambda: tt(T.zl[:, lo:hi], ly[:].indirect(T.off[:, 16 + lo // 16:16 + hi // 16]), T.base[:, lo:hi], OP.add,
+                           ["lya", "lyb", "lyc%d" % t, "off", "base"], qs(lo, hi, "zl")),
+                lambda: ts(T.z[:, lo:hi], T.zl[:, lo:hi], -LIFT, 1.0, OP.add, OP.max, qs(lo, hi, "zl"), qs(lo, hi, "z"))]
+
+    def picks(lo, hi, bank, zsrc=None, zt=None, out=None, ot=None):
+        s = str(lo)
+        fb, fo = ("pP", 0) if zsrc is None else ("pA", 64)
+        zsrc, zt = (T.z[:, lo:hi], qs(lo, hi, "z")) if zsrc is None else (zsrc, zt)
+
+        def first():
+            mm(T[bank][:, lo:hi], T.w2[:], zsrc, True, True, ["w2"] + zt, ["u" + s], [bank])
+            ts(T.ha[:, lo:hi], T[bank][:, lo:hi], 1.0, None, OP.add, None, ["u" + s], ["ha" + s], [bank])
+
+        steps = [first,
+                 lambda: ts(T.hb[:, lo:hi], T.ha[:, lo:hi], 2047, None, OP.bitwise_and, None, ["ha" + s], ["hb" + s]),
+                 lambda: tt(T.hc[:, lo:hi], T.hb[:, lo:hi], T[fb][:, fo + lo:fo + hi], OP.mult, ["hb" + s] + qs(lo, hi, fb + "J"),
+                            ["hc" + s], [fb]),
+                 lambda: tt(T.hd[:, lo:hi] if out is None else out, T.hc[:, lo:hi], T[fb][:, L + fo + lo:L + fo + hi], OP.add,
+                            ["hc" + s] + qs(lo, hi, fb + "JA"), ["hd" + s] if out is None else ot, [fb])]
+        return steps + ([] if out is not None else finish(lo, hi))
+
+    def finish(lo, hi):
+        s = str(lo)
+        return [lambda: ts(T.he[:, lo:hi], T.hd[:, lo:hi], 5, W - 1, OP.arith_shift_right, OP.bitwise_and, ["hd" + s], ["he" + s]),
+                lambda: cp(T.hu[:, lo:hi], T.he[:, lo:hi], ["he" + s], qs(lo, hi, "hu"))]
 
     for t in range(ROUNDS):
         last = t == ROUNDS - 1
-        par = t % 2
         sv, lv, yh, ly = T["sv%d" % t], T["lv%d" % t], T["yh%d" % t], T["ly%d" % t]
-        pJ = T.pP[:, 0:L]
-        zparts = CFG["z"] if t > 0 else {(0, 0): ((0, L),)}
-        ubank = {}
 
-        def demands(lo, hi):
-            if t > 0:
-                newz(t - 1, lo, hi)
-            bank = ("pU", "pY1", "pY0")[len(set(ubank.values()))]
-            for q in range(lo // 16, hi // 16):
-                ubank[q] = bank
-            mm(T[bank][:, lo:hi], T.w2[:], T.z[:, lo:hi], True, True, ["w2"] + qs(lo, hi, "z"), qs(lo, hi, "u"), [bank])
+        def gather(n):
+            c0, c1 = PIECES[n]
+            act(T.xg[:, L * c0:L * c1], T.X[:, 0:W].indirect(T.hu[:, 16 * c0:16 * c1]), AF.Identity,
+                xall + qs(16 * c0, 16 * c1, "hu"), qs(16 * c0, 16 * c1, "x"))
 
-        def picks(step, lo, hi):
-            s = str(lo)
-            bank = ubank[lo // 16]
-            if step == 0:
-                ts(T.ha[:, lo:hi], T[bank][:, lo:hi], 1.0, None, OP.add, None, qs(lo, hi, "u"), ["ha" + s], [bank])
-            elif step == 1:
-                ts(T.hb[:, lo:hi], T.ha[:, lo:hi], 2047, None, OP.bitwise_and, None, ["ha" + s], ["hb" + s])
-            elif step == 2:
-                tt(T.hc[:, lo:hi], T.hb[:, lo:hi], T.pP[:, lo:hi], OP.mult, ["hb" + s, "pJ"], ["hc" + s], ["pP"])
-            elif step == 3:
-                tt(T.hd[:, lo:hi], T.hc[:, lo:hi], T.pP[:, L + lo:L + hi], OP.add, ["hc" + s, "pJA"], ["hd" + s], ["pP"])
-            elif step == 4:
-                ts(T.he[:, lo:hi], T.hd[:, lo:hi], 5, W - 1, OP.arith_shift_right, OP.bitwise_and, ["hd" + s], ["he" + s])
-            else:
-                cp(T.hu[:, lo:hi], T.he[:, lo:hi], ["he" + s], qs(lo, hi, "hu"))
-
-        for n, group in enumerate(CFG["h"]):
-            for step in range(6):
-                for lo, hi in zparts.get((n, step), ()):
-                    demands(lo, hi)
-                for lo, hi in group:
-                    picks(step, lo, hi)
-        for hf in range(2):
+        def zrep(n):
+            c0, c1 = n
+            bank, o = "pZ%d" % (c0 // 8), 64 * (c0 % 8)
             for r in range(4):
-                mm(T["pZ%d" % hf][:, r::4], T.id1[:], T.z[:, 128 * hf:128 * hf + 128], True, True, ["id1"] + zall,
-                   ["zp%d" % hf], ["pZ%d" % hf])
-        mm(T.pT[:, 0:L], T.c19[:], T.ones[:], True, False, ["c19", "ones"], ["tsum"], ["pT"])
-        early = last and CFG["early"]
+                mm(T[bank][:, o + r:o + 64 * (c1 - c0):4], T.id1[:], T.z[:, 16 * c0:16 * c1], True, True,
+                   ["id1"] + qs(16 * c0, 16 * c1, "z"), qs(16 * c0, 16 * c1, "zp") + (["S10", "P10"] if c0 < 8 else []), [bank])
 
-        def ulanes():
-            for q in range(16):
-                mm(T.pU[:, L:L + 16], T.wband[:, 15 - q:143 - q], T.z[:, 16 * q:16 * q + 16], q == 0, q == 15,
-                   ["wband"] + zall, ["ul"], ["pU"])
-
-        def record():
-            cxo = 32 if last else 16 * par
-            cp(T.ti[:], T.pU[:, L:L + 16], ["ul"], ["ti"], ["pU"])
-            if not early:
-                blocks()
-            ts(T.rc[:], T.ti[:], 31, None, OP.bitwise_and, None, ["ti"], ["rc"])
-            tt(T.rf[:], T.rc[:], T.l32[:, 16 * par:16 * par + 16], OP.add, ["rc", "l32a", "l32b"], ["rf"])
-            tt(T.dx[:], T.rc[:], T.cx[:, cxo:cxo + 16], OP.add, ["rc", "cx0", "cx1", "cx2"], ["dx"])
-            cp(T.offr[:], T.rf[:], ["rf"], ["offr"])
-
-        def halves():
-            act(T.oq[:], T.X[:, 0:W].indirect(T.offr[:]), AF.Identity, xall + ["offr"], ["oq"], bias=LIFT - 0.25,
-                scale=-0.5 if last else 0.5)
-            act(T.dd[:, 32:48], T.dx[:], AF.Identity, ["dx"], ["ddx"], scale=S20)
-
-        def blocks():
-            tt(T.dd[:, 0:16], T.k4[:, 1::2], T.kb[:], OP.subtract, ["k4", "kb"], ["ddj"])
-            scan(sv[:, 64:96], T.c4[:], T.t3[:, 1::2], OP.max, OP.min, ["c4", "t3"], ["t4b"])
-
-        if early:
-            ulanes()
-            record()
         if t == 0:
-            late_constants()
-        for lo, hi in CFG["ga"]:
-            act(T.xg[:, 16 * lo:16 * hi], T.X[:, 0:W].indirect(T.hu[:, lo:hi]), AF.Identity,
-                xall + qs(lo, hi, "hu"), qs(lo, hi, "x"))
-        for lo, hi in CFG["gv"]:
-            cp(T.xg[:, 16 * lo:16 * hi], T.X[:, 0:W].indirect(T.hu[:, lo:hi]), xall + qs(lo, hi, "hu"), qs(lo, hi, "x"))
+            weave(picks(0, 64, "pU"), picks(64, 128, "pA"))
+            gather(0)
+            weave(picks(128, 192, "pU"), picks(192, L, "pA"))
+            zrep((0, 8))
+            late = []
+        else:
+            zrep((0, 4))
+            gather(0)
+            weave(newz(t - 1, 64, 128) + picks(64, 128, "pU"), newz(t - 1, 128, 192) + picks(128, 192, "pA"))
+            late = newz(t - 1, 192, L) + picks(192, L, "pU")
+            zrep((4, 8))
+        gather(1)
+        gather(2)
 
-        def mins(n):
-            lo, hi = CFG["m"][n]
-            hf = lo // 128
+        def after_late():
+            zrep((8, 16))
+            for h in range(2):
+                for q in range(16):
+                    mm(T.pA[:, L + 8 * h:L + 8 * h + 8], T.wband[:, 15 - q:143 - q], T.z[:, 128 * h + 8 * q:128 * h + 8 * q + 8],
+                       q == 0, q == 15, ["wband"] + zall, ["ul"], ["pA"])
+
+        def idle():
+            act(T.bw[:, 0:L], T.z[:].indirect(colu), AF.Identity, zall + ["colu"], ["zq"], bias=LIFT - 0.25, scale=0.5)
+            if not last:
+                jl = T.jw[:, 2 * FA:3 * FA]
+                act(jl, tw[t][:, 0:L].indirect(T.repu[:, 16:16 + FA // 16]), AF.Identity, ["j%d" % t, "colu"], ["jl"])
+                forms(jl, ["jl"], 0, FA, -DROP, "pA", 64)
+
+        def mins(n, beside):
+            c0, c1 = PIECES[n]
+            bank, o = "pZ%d" % (c0 // 8), 64 * (c0 % 8)
             for k in range(4):
-                tt(T.mn[:, 16 * lo + k:16 * hi:4], T.xg[:, 16 * lo + k:16 * hi:4],
-                   T["pZ%d" % hf][:, 4 * (lo - 128 * hf):4 * (hi - 128 * hf)], OP.min,
-                   qs(lo, hi, "x") + ["zp%d" % hf], ["m%d.%d" % (n, k)], ["pZ%d" % hf])
+                tt(T.mn[:, L * c0 + k:L * c1:4], T.xg[:, L * c0 + k:L * c1:4], T[bank][:, o:o + 64 * (c1 - c0)], OP.min,
+                   qs(16 * c0, 16 * c1, "x") + qs(16 * c0, 16 * c1, "zp"), ["m%d.%d" % (n, k)], [bank])
+                if k < len(beside):
+                    step(beside[k])
 
         def sums(n, kind):
-            lo, hi = CFG["m"][n]
-            for q in range(lo // 16, hi // 16):
-                if kind == "x":
-                    mm(T.pT[:, 0:L], T.band[:, 15 - q:143 - q], T.xg[:, L * q:L * q + L], False, q == 15,
-                       ["band", "x%d" % q], ["tsum"], ["pT"])
-                else:
-                    mm(T.pG[:, 0:L], T.band[:, 15 - q:143 - q], T.mn[:, L * q:L * q + L], q == 0, q == 15,
-                       ["band"] + ["m%d.%d" % (n, k) for k in range(4)], ["gsum"], ["pG"])
+            c0, c1 = PIECES[n]
+            h = c0 // 8
+            bank, o, _ = PLACE[h][kind]
+            rd = qs(16 * c0, 16 * c1, "x") if kind == 0 else ["m%d.%d" % (n, k) for k in range(4)]
+            for j in range(2 * c0, 2 * c1):
+                mm(T[bank][:, o + j % 16:o + 128:16], (T.xg, T.mn)[kind][:, 128 * j:128 * j + 128], T.blkm[:, 0::16], True, True,
+                   ["blkm"] + rd, ["S%d%d" % (h, kind)] + (qs(0, 128, "zp") if bank == "pZ0" else []), [bank])
 
-        def runmax(lo, hi):
-            scan(T.pm[:, 16 * lo:16 * hi], T.mask[:, 0:16 * (hi - lo)], T.xg[:, 16 * lo:16 * hi], OP.mult, OP.max,
-                 ["mask"] + qs(lo, hi, "x"), qs(lo, hi, "pm"))
+        def turn(h, kind, e):
+            bank, o, op_ = PLACE[h][kind]
+            s, sb = "%d%d" % (h, kind), T.ssb[:, 256 * h + 128 * kind:256 * h + 128 * kind + 128]
+            if e == "a":
+                act(sb, T[bank][:, o:o + 128], AF.Identity, ["S" + s], ["sb" + s], [bank], bias=1.0 - kind)
+            elif e == "v":
+                ts(sb, T[bank][:, o:o + 128], 1.0 - kind, None, OP.add, None, ["S" + s], ["sb" + s], [bank])
+            else:
+                mm(T[bank][:, op_:op_ + 128], sb, T.tri[:], True, True, ["sb" + s, "tri"], ["P" + s], [bank])
 
-        nm = len(CFG["m"])
-        sums(0, "x")
-        for n in range(nm):
-            mins(n)
-            if n in CFG["gap"]:
-                runmax(*CFG["gap"][n])
-            if n + 1 < nm:
-                sums(n + 1, "x")
-            sums(n, "m")
-        act(T.bw[:, 0:L], T.z[:].indirect(T.colu[:]), AF.Identity, zall + ["colu"], ["zq"], bias=LIFT - 0.25, scale=0.5)
+        def tcopy(h, e):
+            bank, _, op_ = PLACE[h][0]
+            if e == "a":
+                act(T.ts[:, 128 * h:128 * h + 128], T[bank][:, op_:op_ + 128], AF.Identity, ["P%d0" % h], ["ts.%d" % h], [bank])
+            else:
+                cp(T.ts[:, 128 * h:128 * h + 128], T[bank][:, op_:op_ + 128], ["P%d0" % h], ["ts.%d" % h], [bank])
 
-        def pack(blk):
-            bank = "pY%d" % (blk % 2)
+        scanned = []
+
+        def runmax(c):
+            scanned.append(c)
+            scan(T.pm[:, L * c:L * c + L], T.mask[:], T.xg[:, L * c:L * c + L], OP.mult, OP.max, ["mask", "x%d" % c], ["pm%d" % c])
+
+        def low(h):
+            lo, hi, n, s = 128 * h, 128 * h + 128, 128, ".%d" % h
+            bank, _, o = PLACE[h][1]
+            sm = "P%d1" % h
+            g1, pa, pa2 = T.pD[:, lo:hi], T.pD[:, L + lo // 2:L + hi // 2], T.pD[:, L + lo // 2:L + lo // 2 + n // 4]
+            pb, pb2 = T.pb[:, lo // 2:hi // 2], T.pb[:, lo // 2:lo // 2 + n // 4]
+            c1_, c2_ = T.c1[:, lo:hi], T.c2[:, lo // 2:hi // 2]
+
+            def s1():
+                tt(pa, T[bank][:, o + 1:o + n:2], T.ts[:, lo:hi:2], OP.mult, [sm, "ts" + s], ["pa" + s, "D", "R"], [bank, "pD"])
+                tt(pb, T[bank][:, o:o + n:2], T.ts[:, lo + 1:hi:2], OP.mult, [sm, "ts" + s], ["pb" + s], [bank])
+
+            def s2():
+                tt(T.c1[:, lo + 1:hi:2], pa, pb, OP.is_gt, ["pa" + s, "pb" + s], ["c1" + s], ["pD"])
+
+            def s3():
+                scan(g1, c1_, T[bank][:, o:o + n], OP.max, OP.min, ["c1" + s, sm], ["g1" + s, "D"], [bank, "pD"])
+                scan(T.t1[:, lo:hi], c1_, T.ts[:, lo:hi], OP.max, OP.min, ["c1" + s, "ts" + s], ["t1" + s])
+
+            def s4():
+                tt(pa2, T.pD[:, lo + 3:hi:4], T.t1[:, lo + 1:hi:4], OP.mult, ["g1" + s, "t1" + s], ["pa" + s], ["pD"])
+                tt(pb2, T.pD[:, lo + 1:hi:4], T.t1[:, lo + 3:hi:4], OP.mult, ["g1" + s, "t1" + s], ["pb" + s], ["pD"])
+                scan(T.k1[:, lo:hi], c1_, T.kc[:, lo:hi], OP.max, OP.min, ["c1" + s, "kc"], ["k1" + s])
+
+            def s5():
+                tt(T.c2[:, lo // 2 + 1:hi // 2:2], pa2, pb2, OP.is_gt, ["pa" + s, "pb" + s], ["c2" + s], ["pD"])
+
+            def s6():
+                scan(T.g2[:, lo // 2:hi // 2], c2_, T.pD[:, lo + 1:hi:2], OP.max, OP.min, ["c2" + s, "g1" + s], ["g2" + s], ["pD"])
+                scan(T.t2[:, lo // 2:hi // 2], c2_, T.t1[:, lo + 1:hi:2], OP.max, OP.min, ["c2" + s, "t1" + s], ["t2" + s])
+
+            def s7():
+                scan(T.k2[:, lo // 2:hi // 2], c2_, T.k1[:, lo + 1:hi:2], OP.max, OP.min, ["c2" + s, "k1" + s], ["k2" + s])
+
+            return [s1, s2, s3, s4, s5, s6, s7]
+
+        record = [lambda: cp(T.ti[:], T.pA[:, L:L + 16], ["ul"], ["ti"], ["pA"]),
+                  lambda: ts(T.rc[:], T.ti[:], 31, None, OP.bitwise_and, None, ["ti"], ["rc"]),
+                  lambda: tt(T.rf[:], T.rc[:], T.l32[:, 16 * t:16 * t + 16], OP.add, ["rc", "l32.%d" % t], ["rf"]),
+                  lambda: cp(T.offr[:], T.rf[:], ["rf"], ["offr"]),
+                  lambda: tt(T.dx[:], T.rc[:], T.cx[:, 16 * t:16 * t + 16], OP.add, ["rc", "cx%d" % t], ["dx"])]
+        first = low(0)
+        second = low(1)
+        chains = {"d": late, "r": record, "L": first, "H": second}
+        single = {"s": lambda: runmax(len(scanned)), "|": lambda: (weave(late), after_late()), "i": idle, ".": lambda: None}
+
+        def step(what):
+            if what in single:
+                single[what]()
+            elif chains[what]:
+                chains[what].pop(0)()
+
+        for what in CFG["phase"].split():
+            if what[0] == "m":
+                mins(int(what[1]), what[2:])
+            elif what[0] == "g":
+                gather(int(what[1]))
+            elif what[0] in "TG":
+                sums(int(what[1]), "TG".index(what[0]))
+            elif what[0] in "avp":
+                turn(int(what[1]), int(what[2]), what[0])
+            elif what[0] == "t":
+                tcopy(int(what[1]), what[2])
+            else:
+                for x in what:
+                    step(x)
+        weave(first, second)
+
+        def pack(blk, e="a"):
+            bank = ("pP", "pU", "pZ1")[blk % 3]
             c0 = 512 * blk
             mm(T[bank][:], T.id1[:], T.X[:, c0:c0 + 512], True, False, ["id1"] + xall, [bank + "d"], [bank])
             mm(T[bank][:], T.id16[:], T.X[:, W // 2 + c0:W // 2 + c0 + 512], False, True, ["id16"] + xall, [bank + "d"], [bank])
             y0 = c0 + (YW - YH) * (blk // 4)
-            act(T.Y[:, y0:y0 + 512], T[bank][:], AF.Identity, [bank + "d"], ["Y%d" % blk], [bank])
+            if e == "a":
+                act(T.Y[:, y0:y0 + 512], T[bank][:], AF.Identity, [bank + "d"], ["Y%d" % blk], [bank])
+            else:
+                cp(T.Y[:, y0:y0 + 512], T[bank][:], [bank + "d"], ["Y%d" % blk], [bank])
 
-        if early:
-            halves()
-        else:
-            ulanes()
         if last:
             for blk in range(CFG["yearly"]):
                 pack(blk)
-        for lo, hi in CFG["pre"]:
-            runmax(lo, hi)
-        ks = []
-        klate = CFG["klate"] or (last and CFG["lastlate"])
-        fill = [] if klate else list(CFG["fill"])
 
         def filler():
-            if fill:
-                runmax(*fill.pop(0))
+            if record:
+                record.pop(0)()
 
-        def kscan(n):
-            src = T.kc[:] if n == 1 else T["k%d" % (n - 1)][:, 1::2]
-            scan(T["k%d" % n][:], T["c%d" % n][:], src, OP.max, OP.min, ["c%d" % n, "kc" if n == 1 else "k%d" % (n - 1)], ["k%d" % n])
-
-        def kstep(n):
-            if klate:
-                ks.append(n)
-            else:
-                kscan(n)
-
-        scan(T.ts[:], T.mask[:, 0:L], T.pT[:, 0:L], OP.mult, OP.add, ["mask", "tsum"], ["ts"], ["pT"])
-        scan(T.gs[:], T.mask[:, 0:L], T.pG[:, 0:L], OP.mult, OP.add, ["mask", "gsum"], ["gs"], ["pG"])
-        tt(T.pP[:, 0:128], T.pG[:, 1:L:2], T.ts[:, 0::2], OP.mult, ["gsum", "ts"], ["pJ"], ["pG", "pP"])
-        tt(T.pb[:], T.pT[:, 1:L:2], T.gs[:, 0::2], OP.mult, ["tsum", "gs"], ["pb"], ["pT"])
-        filler()
-        tt(T.c1[:, 1::2], T.pP[:, 0:128], T.pb[:], OP.is_gt, ["pJ", "pb"], ["c1"], ["pP"])
-        filler()
-        scan(T.pP[:, L:2 * L], T.c1[:], T.gs[:], OP.max, OP.min, ["c1", "gs"], ["pJA"], ["pP"])
-        scan(T.t1[:], T.c1[:], T.ts[:], OP.max, OP.min, ["c1", "ts"], ["t1"])
-        kstep(1)
-        tt(T.pP[:, 0:64], T.pP[:, L + 3:2 * L:4], T.t1[:, 1::4], OP.mult, ["pJA", "t1"], ["pJ"], ["pP"])
-        tt(T.pb[:, 0:64], T.pP[:, L + 1:2 * L:4], T.t1[:, 3::4], OP.mult, ["pJA", "t1"], ["pb"], ["pP"])
-        filler()
-        tt(T.c2[:, 1::2], T.pP[:, 0:64], T.pb[:, 0:64], OP.is_gt, ["pJ", "pb"], ["c2"], ["pP"])
-        filler()
-        scan(T.g2[:], T.c2[:], T.pP[:, L + 1:2 * L:2], OP.max, OP.min, ["c2", "pJA"], ["g2"], ["pP"])
-        scan(T.t2[:], T.c2[:], T.t1[:, 1::2], OP.max, OP.min, ["c2", "t1"], ["t2"])
-        kstep(2)
         for n, cnt in ((3, 32), (4, 16)):
-            gi, ti_, c_ = T["g%d" % (n - 1)], T["t%d" % (n - 1)], T["c%d" % n]
-            gn, tn, cn = "g%d" % (n - 1), "t%d" % (n - 1), "c%d" % n
-            tt(T.pa[:, 0:cnt], gi[:, 3::4], ti_[:, 1::4], OP.mult, [gn, tn], ["pa"])
-            tt(T.pb[:, 0:cnt], gi[:, 1::4], ti_[:, 3::4], OP.mult, [gn, tn], ["pb"])
+            gi, ti_, ki, c_ = T["g%d" % (n - 1)], T["t%d" % (n - 1)], T["k%d" % (n - 1)], T["c%d" % n]
+            gn, tn, kn = [[x + "2.0", x + "2.1"] if n == 3 else [x + "3"] for x in "gtk"]
+            cn = ["c%d.0" % n]
+            tt(T.pa[:, 0:cnt], gi[:, 3::4], ti_[:, 1::4], OP.mult, gn + tn, ["pa"])
+            tt(T.pb[:, 0:cnt], gi[:, 1::4], ti_[:, 3::4], OP.mult, gn + tn, ["pb.0"])
             filler()
-            tt(c_[:, 1::2], T.pa[:, 0:cnt], T.pb[:, 0:cnt], OP.is_gt, ["pa", "pb"], [cn])
+            tt(c_[:, 1::2], T.pa[:, 0:cnt], T.pb[:, 0:cnt], OP.is_gt, ["pa", "pb.0"], cn)
             filler()
             go, to = (T.g3[:], T.t3[:]) if n == 3 else (sv[:, 32:64], sv[:, 0:32])
-            scan(go, c_[:], gi[:, 1::2], OP.max, OP.min, [cn, gn], ["g%d" % n])
-            scan(to, c_[:], ti_[:, 1::2], OP.max, OP.min, [cn, tn], ["t%d" % n])
+            scan(go, c_[:], gi[:, 1::2], OP.max, OP.min, cn + gn, ["g%d" % n])
+            scan(to, c_[:], ti_[:, 1::2], OP.max, OP.min, cn + tn, ["t%d" % n])
             if n == 4:
-                swap(t, lv[:], sv[:, 0:64], ["g4", "t4"], "lv", "av%d" % t)
-            kstep(n)
-        post = (list(CFG["fill"]) if klate else fill) + list(CFG["post"])
-        for n in ks:
-            kscan(n)
-            if len(post) > 1:
-                runmax(*post.pop(0))
+                swap(t, lv[:], sv[:, 0:64], ["g4", "t4"], ["lv"], "av%d" % t)
+            scan(T["k%d" % n][:], c_[:], ki[:, 1::2], OP.max, OP.min, cn + kn, ["k%d" % n])
+        filler()
         ts(T.offy[:], T.k4[:, 1::2], 4096.0, None, OP.mult, None, ["k4"], ["offy"])
-        for lo, hi in post:
-            runmax(lo, hi)
-        act(yh[:], T.pm[:].indirect(T.offy[:]), AF.Identity, qs(0, L, "pm") + ["offy"], ["yh"], scale=0.5)
-        swap(t, ly[:, 0:L], yh[:], ["yh"], "ly", "ay%d" % t)
-        if early:
-            blocks()
-        else:
-            record()
-            halves()
+
+        def profile(lo, hi, toks, sem):
+            top = 128 if hi <= 128 else L
+            act(yh[:, lo:hi], T.pm[:, 0:16 * top].indirect(T.offy[:, lo // 16:hi // 16]), AF.Identity,
+                qs(0, top, "pm") + ["offy"], qs(lo, hi, "yh"), scale=0.5)
+            swap(t, ly[:, lo:hi], yh[:, lo:hi], qs(lo, hi, "yh"), toks, sem)
+
+        def apart(lo, hi):
+            mm(T.pD[:, lo:hi], T.idm2[:], yh[:, lo:hi], True, False, ["idm2"] + qs(lo, hi, "yh"), ["D", "g1.0", "g1.1"], ["pD"])
+            for c in range(lo // 16, hi // 16):
+                h0 = 128 * (c // 8)
+                mm(T.pD[:, 16 * c:16 * c + 16], T.id1[:], T.z[:, h0 + c % 8:h0 + 128:8], False, c == hi // 16 - 1, ["id1"] + zall,
+                   ["D"], ["pD"])
+            act(T.bw[:, L + lo:L + hi], T.pD[:, lo:hi], AF.Abs, ["D"], qs(lo, hi, "zw"), ["pD"])
+
+        def change():
+            mm(T.pD[:, L:2 * L], (T.idmh if last else T.idh)[:], T.old[:], True, False, ["idh", "idmh", "old"],
+               ["R", "pa.0", "pa.1"], ["pD"])
+            mm(T.pD[:, L:2 * L], T.id1[:], yh[:], False, True, ["id1"] + qs(0, L, "yh"), ["R"], ["pD"])
+            act(T.rec[:], T.pD[:, L:2 * L], AF.Identity, ["R"], ["rec"], ["pD"], bias=LIFT - 0.25)
+
+        def oldrec():
+            act(T.old[:], T.X[:, 0:W].indirect(T.offr[:]), AF.Identity, xall + ["offr"], ["old"])
+            act(T.dd[:, 32:48], T.dx[:], AF.Identity, ["dx"], ["ddx"], scale=S20)
+
+        rest = [lambda c=c: runmax(c) for c in range(16) if c not in scanned]
+        tt(T.dd[:, 0:16], T.k4[:, 1::2], T.kb[:], OP.subtract, ["k4", "kb"], ["ddj"])
         ys = [["Y%d" % b for b in range(4 * hf, 4 * hf + 4)] + ["Yd%d" % hf] for hf in range(2)]
-
-        def winz():
-            tt(T.dz[:], T.bw[:, 0:L], yh[:], OP.subtract, ["zq", "yh"], ["dz"])
-            act(T.bw[:, L:2 * L], T.dz[:], AF.Abs, ["dz"], ["zw"], bias=0.5 - 2 * LIFT, scale=2.0)
-
-        dzlate = last and CFG["dzlate"]
-        if not dzlate:
-            winz()
-        tt(T.rec[:], T.oq[:], yh[:], OP.add, ["oq", "yh"], ["rec"])
-        if last:
-            for blk in range(CFG["yearly"], 8):
-                pack(blk)
+        if not last:
+            profile(0, FA, ["lya"], "ay%d" % t)
+            act(sv[:, 64:96], sv[:, 0:32], AF.Identity, ["t4"], ["t4b"])
+            apart(0, FA)
+            n4 = FA // 16
+            rest.pop(0)()
+            tt(T.ow[:, 0:n4], T.dd[:, 0:n4], T.ol[:, 0:n4], OP.add, ["ddj", "ol0"], ["ow"])
+            rest.pop(0)()
+            ts(T.offw[:, 0:n4], T.ow[:, 0:n4], 2.0 ** 20, None, OP.mult, None, ["ow"], ["offw"])
+            oldrec()
+            weave(rest)
+            profile(FA, L, ["lyb"], "ab%d" % t)
+            jw, jw32, wa, wb = T.jw[:, 0:FA], T.jw[:, FA:2 * FA], T.wa[:, 0:FA], T.wa[:, FA:2 * FA]
+            act(jw, tw[t][:].indirect(T.offw[:, 0:n4]), AF.Identity, ["offw"] + shifted(t), ["jw"])
+            act(jw32, jw, AF.Identity, ["jw"], ["jw32"], bias=-DROP, scale=32.0)
+            ts(T.zz[:, L:L + FA], T.bw[:, L:L + FA], 1.0, None, OP.max, None, qs(0, FA, "zw"), ["zzw"])
+            mm(T.pU[:, 0:FA], T.w2[:], T.zz[:, L:L + FA], True, True, ["w2", "zzw"], ["u0"], ["pU"])
+            change()
+            apart(FA, L)
+            ts(wa, T.pU[:, 0:FA], 1.0, None, OP.add, None, ["u0"], ["wa"], ["pU"])
+            ts(wb, wa, 2047, None, OP.bitwise_and, None, ["wa"], ["wb"])
+            tt(T.wc[:], wb, jw, OP.mult, ["wb", "jw"], ["wc"])
+            tt(T.hw[:, L:L + FA], T.wc[:], jw32, OP.add, ["wc", "jw32"], ["hw"])
+        else:
+            act(sv[:, 64:96], sv[:, 0:32], AF.Identity, ["t4"], ["t4b"])
+            oldrec()
+            pack(CFG["yearly"])
+            weave(rest)
+            profile(0, L, ["lya", "lyb"], "ay%d" % t)
+            for blk in range(CFG["yearly"] + 1, 8):
+                pack(blk, "v")
+            change()
+            ts(T.ol[:, 32:48], T.lt[:, 96:112], q1, S20, OP.add, OP.mult, ["lt6", "q1"], ["ol32"])
             ts(T.d1[:], T.rec[:, 0:128], -LIFT, None, OP.add, None, ["rec"], ["d1"])
             ts(T.d16[:], T.rec[:, 128:L], -LIFT, 16.0, OP.add, OP.mult, ["rec"], ["d16"])
             tt(T.ya[:, 0:64], T.Y[:, 0:YW].indirect(T.offr[:, 0:4]), T.d1[:, 0:64], OP.add, ys[0] + ["offr", "d1"], ["ya0"])
             tt(T.ya[:, 64:128], T.Y[:, YW - YH:2 * YW].indirect(T.offr[:, 4:8]), T.d1[:, 64:128], OP.add,
                ys[0] + ys[1] + ["offr", "d1"], ["ya1"])
-        tt(T.qq[:], sv[:, 33:96:2], lv[:, 1::2], OP.mult, ["g4", "t4b", "lv"], ["qq"])
-        tt(T.win[:], T.qq[:, 0:16], T.qq[:, 16:32], OP.is_ge if rank < (rank ^ STEPS[t]) else OP.is_gt, ["qq"], ["win"])
-        tt(T.wd[:], T.win[:].indirect(T.repu[:, 0:3]), T.dd[:], OP.mult, ["win", "repu", "ddj", "ddz", "ddx"], ["wd"])
-        if not last:
-            tt(T.sb[:], T.win[:], T.dd[:, 0:16], OP.mult, ["win", "ddj"], ["sb"])
-            mm(T.pU[:, L + 16:L + 32], T.c4096[:], T.sb[:], True, True, ["c4096", "sb"], ["asum"], ["pU"])
-        o = 48 if last else 0
-        tt(T.oo[:], T.wd[:], T.ol[:, o:o + 48], OP.add, ["wd"] + ["ol%d" % (o + d) for d in (0, 16, 32)], ["oo"])
-        ts(T.off[:], T.oo[:], 2.0 ** 20, None, OP.mult, None, ["oo"], ["off"])
+            apart(0, L)
         nxt = T.jfin[:] if last else tw[t + 1][:, 0:L]
-        for what in (CFG["order"] if not last else "j" if dzlate else "bj"):
-            if what == "a":
-                act(T.aj[:], T.pU[:, L + 16:L + 32], AF.Identity, ["asum"], ["acol"], ["pU"], bias=-DROP / 16, scale=32.0,
+
+        def deltas():
+            tt(T.wd[:], T.win[:].indirect(T.repu[:, 0:3]), T.dd[:], OP.mult, ["win", "repu", "ddj", "ddz", "ddx"], ["wd"])
+            if not last:
+                mm(T.pD[:, 0:16], T.c4096[:], T.wd[:, 0:16], True, True, ["c4096", "wd"], ["D"], ["pD"])
+                act(T.aj[:], T.pD[:, 0:16], AF.Identity, ["D"], ["acol"], ["pD"], bias=-DROP / 16, scale=32.0,
                     acc=T.acol[:, 0:1])
-            elif what == "b":
-                act(T.base[:], T.bw[:].indirect(T.off[:, 16:32]), AF.Identity, ["zq", "zw", "off"], ["base"])
-            else:
-                act(nxt, tw[t][:].indirect(T.off[:, 0:16]), AF.Identity,
-                    ["off", "j%d" % t, "jr%d" % t] + ["to%d.%d" % (t, k) for k in range(15)]
-                    + ["tr%d.%d" % (t, k) for k in range(1, 16)], ["j%d" % (t + 1)])
+
+        def offsets():
+            ts(T.off[:], T.oo[:], 2.0 ** 20, None, OP.mult, None, ["oo"], ["off"])
+            act(nxt, tw[t][:].indirect(T.off[:, 0:16]), AF.Identity, ["off"] + shifted(t), ["j%d" % (t + 1)])
+
+        meet = [lambda: tt(T.qq[:], sv[:, 33:96:2], lv[:, 1::2], OP.mult, ["g4", "t4b", "lv"], ["qq"]),
+                lambda: tt(T.win[:], T.qq[:, 0:16], T.qq[:, 16:32], OP.is_ge if rank < (rank ^ STEPS[t]) else OP.is_gt,
+                           ["qq"], ["win"]),
+                deltas,
+                lambda: tt(T.oo[:], T.wd[:], T.ol[:], OP.add, ["wd", "ol0", "ol16", "ol32"], ["oo"]),
+                offsets]
         if not last:
+            scat, lo = [], 0
+            for n in CFG["scat"]:
+                scat.append(lambda lo=lo, n=n: tt(T.X[:, 0:W + L].indirect(T.off[:, 32 + lo // 16:32 + (lo + n) // 16]),
+                                                  T.rec[:, lo:lo + n], T.neg[:, 0:n], OP.add, ["off", "rec", "neg", "Xd"], xall))
+                lo += n
+            lose = [lambda: tt(T.zl[:, 0:FA], ly[:, 0:FA], T.bw[:, 0:FA], OP.add, ["lya", "zq"], qs(0, FA, "zl")),
+                    lambda: ts(T.zz[:, 0:FA], T.zl[:, 0:FA], -LIFT, 1.0, OP.add, OP.max, qs(0, FA, "zl"), ["zzl"])]
+            lose += picks(0, FA, "pU", T.zz[:, 0:FA], ["zzl"], T.hw[:, 0:FA], ["hl"])
+            pick = [lambda: ts(T.hd[:, 0:FA], T.hw[:].indirect(T.off[:, 16:16 + n4]), T.acol[:, 0:1], DROP, OP.add, OP.add,
+                               ["hl", "hw", "off", "acol"], ["hd0"])] + finish(0, FA)
+            for x in CFG["meet"].replace(" ", ""):
+                {"M": meet, "l": lose, "S": scat, "P": pick}[x].pop(0)()
             lists(t + 1, [])
-            tt(T.X[:, 0:W + L].indirect(T.off[:, 32:48]), T.rec[:], T.neg[:], OP.add, ["off", "rec", "neg", "Xd"], xall)
-            act(pJ, nxt, AF.Identity, ["j%d" % (t + 1)], ["pJ"], ["pP"])
-            act(T.pP[:, L:2 * L], nxt, AF.Identity, ["j%d" % (t + 1), "acol"], ["pJA"], ["pP"], bias=T.acol[:, 0:1], scale=32.0)
+            forms(tw[t + 1][:, FA:L], ["j%d" % (t + 1), "acol"], FA, L, T.acol[:, 0:1])
+            act(T.base[:, FA:L], T.bw[:].indirect(T.off[:, 16 + n4:32]), AF.Identity, ["zq", "off"] + qs(0, L, "zw"), ["base"])
+            act(T.z[:, 0:FA], T.zz[:].indirect(T.off[:, 16:16 + n4]), AF.Identity, ["zzl", "zzw", "off"], qs(0, FA, "z"))
         else:
+            weave(meet)
+            act(T.base[:], T.bw[:].indirect(T.off[:, 16:32]), AF.Identity, ["zq", "off"] + qs(0, L, "zw"), ["base"])
+            znew = newz(t, 0, L)
             for hf in range(2):
                 yw, c = T.Y[:, hf * YW:hf * YW + YW], 64 * hf
                 lo, hi = T.off[:, 32 + 4 * hf:36 + 4 * hf], T.off[:, 40 + 4 * hf:44 + 4 * hf]
@@ -558,11 +662,8 @@ def rank_program(g, core, T, topo):
                 tt(T.yb[:, c:c + 64], yw.indirect(hi), T.d16[:, c:c + 64], OP.add, ys[hf] + ["off", "d16"], ["yb%d" % hf])
                 cp(yw.indirect(hi), T.yb[:, c:c + 64], ["off", "yb%d" % hf], ys[hf])
                 dma("s", T.yx[:, hf * YH:hf * YH + YH], T.Y[:, hf * YW:hf * YW + YH], ys[hf], ["yx%d" % hf], "outx")
-            dma("a", T.yj[:], T.jfin[:], ["j4"] + ys[0], ["yj"], "outj")
-            if dzlate:
-                winz()
-                act(T.base[:], T.bw[:].indirect(T.off[:, 16:32]), AF.Identity, ["zq", "zw", "off"], ["base"])
-            newz(t, 0, L)
+            dma("a", T.yj[:], T.jfin[:], ["j4"], ["yj"], "outj")
+            weave(znew)
     dma("a", T.yz[:], T.z[:], zall, ["yz"], "outz")
     add("s", None, ["yj", "yx0", "yx1", "yz"])
     emit(g, T, ops)

@@ -6,76 +6,123 @@ ROUNDS = 4
 STEPS = (1, 2, 3, 1)
 W = 8192
 L = 256
-FA = 64
+H = 128
 YH, YW = 2048, 2176
 SLABS = 17
 S12 = 2.0 ** -12
-S20 = 2.0 ** -20
+S19 = 2.0 ** -19
+TOP = 16384
 LIFT = 192.0
 DROP = 32.0 * 5 * W
 
-CFG = {
-    "phase": "dd T0 m0dddd G0 dsds| g3 T1 m1 G1 T2 ssss g4 a00 a01 T3 m2 G2 m3 G3 T4 p00 p01 a10 t0a ss m4 p10 G4 a11 t1a p11 i LL",
-    "meet": "MMlMlMlM l S l S l S P S P P",
-    "scat": (64, 64, 64, 64),
-    "own": 3,
-    "yearly": 4,
-}
-PIECES = ((0, 4), (4, 8), (8, 12), (12, 14), (14, 16))
-
-PLACE = ((("pH0", 0, 256), ("pH0", 128, 384)), (("pZ0", 0, 128), ("pH1", 0, 128)))
-
+PIECES = ((0, 64), (64, 128), (128, 192), (192, 224), (224, 256))
+CFG = {"run": 32, "scat": 64, "vpack": 2, "lead": 0.0, "late": (0.5, 0.4, 0.1, 0.2),
+       "cyc": 0.00087, "pe": 0.00044, "wake": 0.2, "gat": 1.56, "sca": 3.8, "dma": 2.2, "far": 3.2, "passes": 2, "look": 0.1, "fit": 0.03}
 TURN_Q = ((32, 2), (2, 0), (16, 3), (1, 0))
 TURN_C = (((4, 8),), ((1, 2), (32, 4)), ((2, 8),), ((16, 8),))
 
 F, B, I, U = "float32", "bfloat16", "int32", "uint16"
-SCRATCH = {
-    "X": ("sbuf", [128, W + L], B), "Y": ("sbuf", [128, 2 * YW], B),
-    "xg": ("sbuf", [128, 16 * L], B), "mn": ("sbuf", [128, 16 * L], B), "pm": ("sbuf", [128, 16 * L], B), "mask": ("sbuf", [128, L], B),
-    "jin": ("sbuf", [128, L], I), "zin": ("sbuf", [128, L], B), "z": ("sbuf", [128, L], B), "w": ("sbuf", [128, 8], F),
-    "kv": ("sbuf", [128, L], F), "pi": ("sbuf", [128, 8], I), "lt": ("sbuf", [128, 112], F),
-    "q1": ("sbuf", [128, 16], F),
-    "bandv": ("sbuf", [128, 144], F), "blkv": ("sbuf", [128, 128], F),
-    "bm": ("sbuf", [128, 144], B), "wband": ("sbuf", [128, 144], B),
-    "blkm": ("sbuf", [128, 128], B), "w2": ("sbuf", [128, 128], B),
-    "id1": ("sbuf", [128, 128], B), "id16": ("sbuf", [128, 128], B), "idm2": ("sbuf", [128, 128], B),
-    "idh": ("sbuf", [128, 128], B), "idmh": ("sbuf", [128, 128], B),
-    "trv": ("sbuf", [128, 128], B), "tri": ("sbuf", [128, 128], B), "c4096": ("sbuf", [128, 128], F),
-    "ssb": ("sbuf", [128, 512], B), "neg": ("sbuf", [128, L], B),
-    "kc": ("sbuf", [128, L], F), "kb": ("sbuf", [128, 16], F), "pos": ("sbuf", [128, 32], F),
-    "repu": ("sbuf", [128, 48], U), "l32": ("sbuf", [128, 64], F), "cx": ("sbuf", [128, 64], F),
-    "ol": ("sbuf", [128, 48], F), "dd": ("sbuf", [128, 48], F),
-    "c1": ("sbuf", [128, 256], F), "c2": ("sbuf", [128, 128], F), "c3": ("sbuf", [128, 64], F), "c4": ("sbuf", [128, 32], F),
-    "ha": ("sbuf", [128, L], I), "hb": ("sbuf", [128, L], I), "hc": ("sbuf", [128, L], F), "hd": ("sbuf", [128, L], I),
-    "he": ("sbuf", [128, L], I), "hu": ("sbuf", [128, L], U),
-    "wa": ("sbuf", [128, 2 * FA], I), "wc": ("sbuf", [128, FA], F), "jw": ("sbuf", [128, 3 * FA], F),
-    "hw": ("sbuf", [128, L + FA], F), "zz": ("sbuf", [128, L + FA], B),
-    "ti": ("sbuf", [128, 16], I), "rc": ("sbuf", [128, 16], I), "rf": ("sbuf", [128, 16], F), "dx": ("sbuf", [128, 16], F),
-    "offr": ("sbuf", [128, 16], U), "offy": ("sbuf", [128, 16], U), "off": ("sbuf", [128, 48], U),
-    "ow": ("sbuf", [128, 8], F), "offw": ("sbuf", [128, 8], U),
-    "ts": ("sbuf", [128, 256], F), "pb": ("sbuf", [128, 128], F), "pa": ("sbuf", [128, 32], F),
-    "t1": ("sbuf", [128, 256], F), "k1": ("sbuf", [128, 256], F),
-    "g2": ("sbuf", [128, 128], F), "t2": ("sbuf", [128, 128], F), "k2": ("sbuf", [128, 128], F),
-    "g3": ("sbuf", [128, 64], F), "t3": ("sbuf", [128, 64], F), "k3": ("sbuf", [128, 64], F), "k4": ("sbuf", [128, 32], F),
-    "qq": ("sbuf", [128, 32], F), "win": ("sbuf", [128, 16], F), "wd": ("sbuf", [128, 48], F), "oo": ("sbuf", [128, 48], F),
-    "aj": ("sbuf", [128, 16], F), "acol": ("sbuf", [128, 8], F),
-    "bw": ("sbuf", [128, 2 * L], F), "base": ("sbuf", [128, L], F), "old": ("sbuf", [128, L], B),
-    "rec": ("sbuf", [128, L], B), "zl": ("sbuf", [128, L], B),
-    "d1": ("sbuf", [128, 128], B), "d16": ("sbuf", [128, 128], B), "ya": ("sbuf", [128, 128], B), "yb": ("sbuf", [128, 128], B),
-    "jfin": ("sbuf", [128, L], F),
-    "pH0": ("psum", [128, 512], F), "pH1": ("psum", [128, 512], F), "pZ0": ("psum", [128, 512], F), "pZ1": ("psum", [128, 512], F),
-    "pU": ("psum", [128, 512], F), "pP": ("psum", [128, 512], F), "pD": ("psum", [128, 512], F), "pA": ("psum", [128, 512], F),
-}
+SCRATCH = {}
+for _names, _n, _d in (
+        ("X", W + L, B), ("Y", 2 * YW, B), ("xg mn pm", 16 * L, B), ("mask", 1024, B), ("jin ha hb hd he", L, I), ("hu", L, U),
+        ("zin z old rec zd_", L, B), ("ones neg blkm w2 id1 id16 idm2 idh idmh c19 c17 sb d1 d16 ya yb", H, B), ("bm band wband", 144, B),
+        ("bandv", 144, F), ("blkv kv kc hf c2 k2 pb c5 sa", H, F), ("hc zq jfin gs ts c1 t1 k1 qq rp lt", L, F), ("zz", 2 * L, B),
+        ("sd", 320, F), ("se", 384, F), ("sv", 96, F), ("c3 g3 t3 k3 l32 pa", 64, F), ("c4 k4", 32, F), ("q1 rf aj", 16, F),
+        ("w acol kb kj col", 8, F), ("pi", 8, I), ("ti rc", 16, I), ("offr offy", 16, U), ("offh", 8, U), ("off lists", 64, U)):
+    for _x in _names.split():
+        SCRATCH[_x] = ("sbuf", [128, _n], _d)
+for _x in ("pT0", "pT1", "pG0", "pG1", "pZ0", "pZ1", "pU", "pP"):
+    SCRATCH[_x] = ("psum", [128, 512], F)
 SEMAPHORES = ["v", "a", "p", "g", "ldz", "ldw", "ldj", "ldx", "ldx2", "sent", "outj", "outz", "outx"]
 for _t in range(ROUNDS):
     SCRATCH["tw%d" % _t] = ("sbuf", [128, SLABS * L], F)
-    SCRATCH["sv%d" % _t] = ("sbuf", [128, 96], F)
-    SCRATCH["lv%d" % _t] = ("sbuf", [128, 64], F)
+    SCRATCH["sm%d" % _t] = ("sbuf", [128, L], F)
+    SCRATCH["lm%d" % _t] = ("sbuf", [128, L], F)
     SCRATCH["yh%d" % _t] = ("sbuf", [128, L], B)
-    SCRATCH["ly%d" % _t] = ("sbuf", [128, 2 * L], B)
-    SCRATCH["do%d" % _t] = ("dram", [8, 16 * L], F)
-    SCRATCH["dr%d" % _t] = ("dram", [8, 16 * L], F)
-    SEMAPHORES += ["aj%d" % _t, "av%d" % _t, "ay%d" % _t, "ab%d" % _t, "so%d" % _t, "sr%d" % _t, "tp%d" % _t]
+    SCRATCH["ly%d" % _t] = ("sbuf", [128, L], B)
+    SCRATCH["do%d" % _t] = ("dram", [16, 16 * H], F)
+    SCRATCH["dr%d" % _t] = ("dram", [16, 16 * H], F)
+    SEMAPHORES += ["%s%d%d" % (x, h, _t) for x in ("aj", "av", "ay", "so", "sr", "tp") for h in range(2)]
+
+
+TURNS = {"sq", "gq"}
+
+
+def arrange(ops):
+    n, wake = len(ops), CFG["wake"]
+    preds, succs, writer, readers = [set() for _ in ops], [[] for _ in ops], {}, {}
+    for i, op in enumerate(ops):
+        for tok in op[2] + op[3]:
+            if tok in writer:
+                preds[i].add(writer[tok])
+        for tok in op[3]:
+            preds[i].update(readers.get(tok, ()))
+        preds[i].discard(i)
+        for tok in op[2]:
+            readers.setdefault(tok, []).append(i)
+        for tok in op[3]:
+            writer[tok], readers[tok] = i, []
+    for i in range(n):
+        for j in preds[i]:
+            succs[j].append(i)
+
+    def gap(j, i):
+        busy, late = ops[j][7]
+        if ops[j][0] == ops[i][0] and (ops[i][0] == "p" or not set(ops[j][3]) & set(ops[i][2] + ops[i][3]) - TURNS
+                                       and not set(ops[j][2]) & set(ops[i][3])):
+            return busy
+        return busy + late + (wake if ops[i][0] else 0.0)
+
+    chain = [0.0] * n
+    for i in reversed(range(n)):
+        chain[i] = max([gap(i, k) + chain[k] for k in succs[i]] + [sum(ops[i][7])])
+    chain = [c + op[8] for c, op in zip(chain, ops)]
+
+    def place(rank, back):
+        before, after = (succs, preds) if back else (preds, succs)
+        ready, left, time = [op[7][1] if back else 0.0 for op in ops], [len(p) for p in before], [0.0] * n
+        pool, free, bank = {}, {}, {}
+        for i in range(n):
+            if not left[i]:
+                pool.setdefault(ops[i][0], []).append(i)
+
+        def earliest(i):
+            t = max(ready[i], free.get(ops[i][0], 0.0)) if ops[i][0] else ready[i]
+            for b in ops[i][4]:
+                if b in bank and bank[b][0] != ops[i][0]:
+                    t = max(t, bank[b][1] + wake)
+            return t
+
+        for _ in range(n):
+            t0, e = min((min(earliest(i) for i in p), str(e)) for e, p in pool.items() if p)
+            e = None if e == "None" else e
+            near = [(earliest(i), i) for i in pool[e]]
+            t, i = max((x for x in near if x[0] <= t0 + CFG["look"]), key=lambda x: (rank[x[1]], -x[1]))
+            fits = [x for x in near if x[0] + ops[x[1]][7][0] <= t + CFG["fit"] and x[1] != i]
+            if t > t0 and fits:
+                t, i = max(fits, key=lambda x: (rank[x[1]], -x[1]))
+            pool[e].remove(i)
+            busy = ops[i][7][0]
+            time[i], free[e] = t, t + busy
+            for b in ops[i][4]:
+                bank[b] = (e, t + busy)
+            for k in after[i]:
+                ready[k] = max(ready[k], t + (gap(k, i) - ops[k][7][0] + busy if back else gap(i, k)))
+                left[k] -= 1
+                if not left[k]:
+                    pool.setdefault(ops[k][0], []).append(k)
+        return time
+
+    best = None
+    for _ in range(CFG["passes"]):
+        time = place(chain, False)
+        end = max(time[i] + sum(ops[i][7]) for i in range(n))
+        CFG.get("log", []).append((end, time))
+        if best is None or end < best[0]:
+            best = (end, time)
+        back = place([time[i] + ops[i][7][0] for i in range(n)], True)
+        chain = [back[i] + ops[i][7][0] for i in range(n)]
+    return [ops[i] for i in sorted(range(n), key=lambda i: (best[1][i], i))]
 
 
 def emit(g, T, ops):
@@ -83,7 +130,8 @@ def emit(g, T, ops):
     writer, readers, count, dmas = {}, {}, {}, {}
     known = {e: {} for e in queue}
     snap, waits, wanted = {}, [], set()
-    for e, fn, rd, wr, banks, dsem, ext in ops:
+    for e, fn, rd, wr, banks, dsem, ext in [op[:7] for op in ops]:
+        wr = [tok for tok in wr if tok not in TURNS]
         if ext is not None:
             for tok in wr:
                 writer[tok] = ext
@@ -145,7 +193,7 @@ def emit(g, T, ops):
         for tok in banks:
             writer[tok] = me
     level, seen, count = {}, {}, {}
-    for (e, fn, rd, wr, banks, dsem, ext), mine in zip(ops, waits):
+    for (e, fn, rd, wr, banks, dsem, ext), mine in zip([op[:7] for op in ops], waits):
         if ext is not None:
             continue
         for key, n in mine:
@@ -165,506 +213,377 @@ def emit(g, T, ops):
                 ins.then_inc(T.sem[e], 1)
 
 
-def weave(*chains):
-    chains = [list(c) for c in chains]
-    while any(chains):
-        for c in chains:
-            if c:
-                c.pop(0)()
-
-
 def rank_program(g, core, T, topo):
     rank = T.rank_of(core)
     if rank is None:
         return
     ops = []
     v, a, pe = g.vector, g.scalar, g.tensor
-    sent = [0]
+    sent, lead = [0], [0.0]
+    cyc, gat, sca = CFG["cyc"], CFG["gat"], CFG["sca"]
 
-    def add(e, fn, rd=(), wr=(), banks=(), dsem=None, ext=None):
-        ops.append((e, fn, list(rd), list(wr), list(banks), dsem, ext))
+    def add(e, fn, rd=(), wr=(), banks=(), dsem=None, ext=None, cost=(0.0, 0.0)):
+        ops.append((e, fn, list(rd), list(wr), list(banks), dsem, ext, cost, lead[0]))
 
-    def ts(out, in0, s1, s2, o0, o1, rd, wr, banks=()):
+    def dve(n, r):
+        return (max(64.0, n * r) * cyc if r <= 1 or r == 2 else 0.05 + n * r * cyc, 0.0)
+
+    def ts(n, out, in0, s1, s2, o0, o1, rd, wr, banks=(), r=1):
         if o1 is None:
-            add("v", lambda: v.tensor_scalar(out, in0, s1, None, o0), rd, wr, banks)
+            add("v", lambda: v.tensor_scalar(out, in0, s1, None, o0), rd, wr, banks, cost=dve(n, r))
         else:
-            add("v", lambda: v.tensor_scalar(out, in0, s1, s2, o0, o1), rd, wr, banks)
+            add("v", lambda: v.tensor_scalar(out, in0, s1, s2, o0, o1), rd, wr, banks, cost=dve(n, r))
 
-    def tt(out, in0, in1, op, rd, wr, banks=()):
-        add("v", lambda: v.tensor_tensor(out, in0, in1, op), rd, wr, banks)
+    def tt(n, out, in0, in1, op, rd, wr, banks=(), r=None):
+        add("v", lambda: v.tensor_tensor(out, in0, in1, op), rd, wr, banks, cost=dve(n, r or (1 if banks else 2)))
 
-    def cp(out, in_, rd, wr, banks=()):
-        add("v", lambda: v.tensor_copy(out, in_), rd, wr, banks)
+    def cp(n, out, in_, rd, wr, banks=(), r=1):
+        add("v", lambda: v.tensor_copy(out, in_), rd, wr, banks, cost=dve(n, r))
 
-    def ms(ap, c, wr):
-        add("v", lambda: v.memset(ap, c), (), wr)
+    def ms(n, ap, c, wr):
+        add("v", lambda: v.memset(ap, c), (), wr, cost=dve(n, 0.5))
 
-    def scan(out, d0, d1, o0, o1, rd, wr, banks=()):
-        add("v", lambda: v.tensor_tensor_scan(out, d0, d1, 0.0, o0, o1), rd, wr, banks)
+    def scan(n, out, d0, d1, o0, o1, rd, wr, banks=(), r=1):
+        add("v", lambda: v.tensor_tensor_scan(out, d0, d1, 0.0, o0, o1), rd, wr, banks, cost=dve(n, r))
 
-    def act(out, in_, func, rd, wr, banks=(), bias=0.0, scale=1.0, acc=None):
+    def act(n, out, in_, func, rd, wr, banks=(), bias=0.0, scale=1.0, acc=None, r=1):
+        cost = (0.06 + max(64.0, n * r) * cyc + (0.0 if acc is None else 0.02), 0.0)
         if acc is None:
-            add("a", lambda: a.activation(out, in_, func, bias=bias, scale=scale), rd, wr, banks)
+            add("a", lambda: a.activation(out, in_, func, bias=bias, scale=scale), rd, wr, banks, cost=cost)
         else:
-            add("a", lambda: a.activation(out, in_, func, bias=bias, scale=scale, accum_out=acc), rd, wr, banks)
+            add("a", lambda: a.activation(out, in_, func, bias=bias, scale=scale, accum_out=acc), rd, wr, banks, cost=cost)
 
-    def mm(out, lhs, rhs, start, stop, rd, wr, banks):
-        add("p", lambda: pe.matmul(out, lhs, rhs, start, stop), rd, wr, banks)
+    def mm(n, bank, out, lhs, rhs, start, stop, rd, wr):
+        add("p", lambda: pe.matmul(out, lhs, rhs, start, stop), rd, wr + ["group" + bank], [bank],
+            cost=(max(64, n) * CFG["pe"], 0.03))
 
-    def dma(e, out, in_, rd, wr, sem):
+    def dma(e, out, in_, rd, wr, sem, late=0.0):
         q = g.sync if e == "s" else g.scalar
-        add(e, lambda: q.dma_start(out, in_), rd, wr, (), sem)
+        add(e, lambda: q.dma_start(out, in_), rd, wr + (["sq"] if late and e == "s" else []), (), sem, cost=(0.06, CFG["dma"] + late))
 
-    def iota(out, pat, mult, wr, flag=True, base=0):
+    def iota(out, pat, base, mult, wr, flag=True):
+        n = 1
+        for _, k in pat:
+            n *= k
         if flag:
-            add("g", lambda: g.iota(out, pat, base, mult, allow_small_or_imprecise_dtypes=True), (), wr)
+            add("g", lambda: g.iota(out, pat, base, mult, allow_small_or_imprecise_dtypes=True), (), wr, cost=(0.13 + 2 * n * cyc, 0.0))
         else:
-            add("g", lambda: g.iota(out, pat, 0, mult), (), wr)
+            add("g", lambda: g.iota(out, pat, base, mult), (), wr, cost=(0.13 + 2 * n * cyc, 0.0))
 
-    def swap(t, out, in_, rd, toks, sem):
+    def swap(t, out, in_, rd, tok, sem, late=0.0):
         peer = T.cores[rank ^ STEPS[t]]
         rid, pid, _ = topo.addr(peer)
-        add("g", lambda: g.remote_dma(out, in_, T.sem[sem], T.sem.sent, pid, rid, topo.mask(core, peer)), rd, (), (), "")
+        add("g", lambda: g.remote_dma(out, in_, T.sem[sem], T.sem.sent, pid, rid, topo.mask(core, peer)), rd, ["went" + sem], (), "",
+            cost=(0.3, 0.0))
         sent[0] += len(topo.engines(core, peer))
-        add(None, None, (), toks, ext=(sem, len(topo.engines(peer, core))))
+        add(None, None, ["went" + sem], [tok], ext=(sem, len(topo.engines(peer, core))), cost=(0.0, CFG["far"] - 0.3 + late))
 
     def qs(lo, hi, name):
         return ["%s%d" % (name, q) for q in range(lo // 16, hi // 16)]
 
     tw = [T["tw%d" % t] for t in range(ROUNDS)]
-    zall, xall = qs(0, L, "z"), ["X", "X2"]
+    zall, xall = ["z0", "z1"], ["X", "X2"]
 
-    def lists(t, after):
-        w_, do, dr = tw[t], T["do%d" % t], T["dr%d" % t]
-        swap(t, w_[:, 16 * L:17 * L], w_[:, 0:L], ["j%d" % t] + after[:1], ["jr%d" % t], "aj%d" % t)
-        dma("s", do[:], w_[:, 0:L], ["j%d" % t] + after, ["do%d" % t], "so%d" % t)
+    def names(t):
+        return ["j%d.0" % t, "j%d.1" % t]
+
+    def slab(t, h, s0, s1):
+        return slice(SLABS * H * h + H * s0, SLABS * H * h + H * s1)
+
+    def lists(t, h, after):
+        w_, do, dr, s, rows = tw[t], T["do%d" % t], T["dr%d" % t], "%d.%d" % (t, h), slice(8 * h, 8 * h + 8)
+        sem = "%d%d" % (h, t)
+        swap(t, w_[:, slab(t, h, 16, 17)], w_[:, slab(t, h, 0, 1)], ["j" + s] + after[:1], "jr" + s, "aj" + sem, 0.8)
+        dma("s", do[rows, :], w_[:, slab(t, h, 0, 1)], ["j" + s] + after, ["do" + s], "so" + sem)
+        dma("s", dr[rows, :], w_[:, slab(t, h, 16, 17)], ["jr" + s], ["dr" + s], "sr" + sem)
         for k in range(15):
-            if k == (0 if t == 0 else CFG["own"]):
-                dma("s", dr[:], w_[:, 16 * L:17 * L], ["jr%d" % t], ["dr%d" % t], "sr%d" % t)
-            dma("s", w_[k::16, L:(16 - k) * L], do[:, (k + 1) * L:16 * L], ["do%d" % t], ["to%d.%d" % (t, k)], "tp%d" % t)
+            dma("s", w_[k::16, slab(t, h, 1, 16 - k)], do[rows, (k + 1) * H:16 * H], ["do" + s], ["to%s.%d" % (s, k)], "tp" + sem)
         for k in range(1, 16):
-            dma("s", w_[k::16, (16 - k) * L:16 * L], dr[:, 0:k * L], ["dr%d" % t], ["tr%d.%d" % (t, k)], "tp%d" % t)
+            dma("s", w_[k::16, slab(t, h, 16 - k, 16)], dr[rows, 0:k * H], ["dr" + s], ["tr%s.%d" % (s, k)], "tp" + sem)
 
-    def shifted(t):
-        return (["j%d" % t, "jr%d" % t] + ["to%d.%d" % (t, k) for k in range(15)] + ["tr%d.%d" % (t, k) for k in range(1, 16)])
+    def shifted(t, h):
+        s = "%d.%d" % (t, h)
+        return ["j" + s, "jr" + s] + ["to%s.%d" % (s, k) for k in range(15)] + ["tr%s.%d" % (s, k) for k in range(1, 16)]
 
-    dma("s", T.zin[:], T.zd[:], (), ["zin"], "ldz")
-    dma("a", T.X[:, 0:W // 2], T.xt[:, 0:W // 2], (), ["X"], "ldx")
-    dma("s", T.w[:, 0:1], T.wt[:], (), ["w"], "ldw")
-    dma("s", T.jin[:], T.jn[:], (), ["jin"], "ldj")
-    dma("s", T.X[:, W // 2:W], T.xt[:, W // 2:W], (), ["X2"], "ldx2")
-    iota(T.pi[:, 0:1], [[0, 1]], 1, ["pi"], False)
-    iota(T.blkv[:], [[16, 8], [0, 16]], -1, ["blkv"])
-    iota(T.lt[:, 64:80], [[128, 2], [1, 4], [64, 2]], 0, ["lt4"])
-    iota(T.bandv[:], [[1, 144]], -1, ["bandv"])
-    iota(T.kv[:], [[8 * L, 2], [16, 8], [1, 16]], 0, ["kv"])
+    dma("s", T.zin[:], T.zd[:], [], ["zin"], "ldz", 0.5)
+    dma("a", T.X[:, 0:W // 2], T.xt[:, 0:W // 2], [], ["X"], "ldx", 1.0)
+    dma("s", T.w[:, 0:1], T.wt[:], [], ["w"], "ldw", 0.5)
+    dma("s", T.jin[:], T.jn[:], [], ["jin"], "ldj", 0.5)
+    dma("s", T.X[:, W // 2:W], T.xt[:, W // 2:W], [], ["X2"], "ldx2", 2.5)
+    iota(T.pi[:, 0:1], [[0, 1]], 0, 1, ["pi"], False)
+    iota(T.blkv[:], [[16, 8], [0, 16]], 0, -1, ["blkv"])
+    iota(T.bandv[:], [[1, 144]], 0, -1, ["bandv"])
+    iota(T.kv[:], [[16, 8], [1, 16]], 0, 0, ["kv"])
     for t, pat in enumerate(TURN_C):
-        iota(T.lt[:, 16 * t:16 * t + 16], [[32 * 128, 2]] + [[32 * s, n] for s, n in pat], 0, ["lt%d" % t])
-    iota(T.lt[:, 80:96], [[31 * 64 + 64 - YH, 4], [31 * 16, 4]], 0, ["lt5"], base=-YH)
-    iota(T.lt[:, 96:112], [[0, 4], [16, 4]], 0, ["lt6"], base=YH)
-    q1, q128, q4, q31, w = T.q1[:, 0:1], T.q1[:, 1:2], T.q1[:, 2:3], T.q1[:, 3:4], T.w[:, 0:1]
-    pos, col, colu, firstu = T.pos[:, 0:16], T.pos[:, 16:32], T.repu[:, 16:32], T.repu[:, 32:48]
-    ms(T.mask[:], 1.0, ["mask"])
-    ts(T.pi[:, 1:2], T.pi[:, 0:1], 15, None, OP.bitwise_and, None, ["pi"], ["qi"])
-    ts(T.pi[:, 2:3], T.pi[:, 0:1], 2, 3, OP.arith_shift_right, OP.bitwise_and, ["pi"], ["qi2"])
-    ts(T.pi[:, 3:4], T.pi[:, 0:1], 3, 1, OP.arith_shift_right, OP.bitwise_and, ["pi"], ["qi3"])
-    cp(q1, T.pi[:, 1:2], ["qi"], ["q1"])
-    ms(T.mask[:, 0::16], 0.0, ["mask"])
-    ts(q4, q1, 4.0, None, OP.mult, None, ["q1"], ["q4"])
-    ts(T.blkm[:], T.blkv[:], q1, 0.0, OP.add, OP.is_equal, ["blkv", "q1"], ["blkm"])
-    ts(firstu, T.lt[:, 64:80], q4, None, OP.add, None, ["lt4", "q4"], ["firstu"])
-    ts(q128, q1, 128.0, None, OP.mult, None, ["q1"], ["q128"])
-    ts(q31, q1, 31.0, None, OP.mult, None, ["q1"], ["q31"])
+        iota(T.lt[:, 16 * t:16 * t + 16], [[32 * H, 2]] + [[32 * s, n] for s, n in pat], 0, 0, ["lt%d" % t])
+    iota(T.lt[:, 64:80], [[H, 2], [1, 4], [64, 2]], 0, 0, ["lt4"])
+    iota(T.lt[:, 80:88], [[-16, 2], [4, 4]], 17, 0, ["lt5"])
+    iota(T.lt[:, 128:192], [[1, 8], [0, 8]], 0, 0, ["ia"])
+    iota(T.lt[:, 192:256], [[0, 2], [1, 4], [0, 8]], 0, 0, ["ib"])
+    q1, q128, q4, q22, qm, qe, w = [T.q1[:, i:i + 1] for i in (0, 1, 2, 3, 8, 9)] + [T.w[:, 0:1]]
+    firstu, colu, rep8 = T.lists[:, 0:16], T.lists[:, 16:24], T.lists[:, 24:32]
+    ia, ib = T.lt[:, 128:192], T.lt[:, 192:256]
+    ts(1, T.pi[:, 1:2], T.pi[:, 0:1], 15, None, OP.bitwise_and, None, ["pi"], ["qi"])
+    ts(1, T.pi[:, 2:3], T.pi[:, 0:1], 2, 3, OP.arith_shift_right, OP.bitwise_and, ["pi"], ["qi2"])
+    ts(1, T.pi[:, 3:4], T.pi[:, 0:1], 3, 1, OP.arith_shift_right, OP.bitwise_and, ["pi"], ["qi3"])
+    ts(1, T.pi[:, 4:5], T.pi[:, 0:1], 7, None, OP.bitwise_and, None, ["pi"], ["qi7"])
+    cp(1, q1, T.pi[:, 1:2], ["qi"], ["q1"])
+    for ap, c, tok in ((q4, 4.0, "q4"), (q128, 128.0, "q128")):
+        ts(1, ap, T.pi[:, 1:2], c, None, OP.mult, None, ["qi"], [tok])
+    ts(1, q22, T.pi[:, 3:4], 2.0, None, OP.mult, None, ["qi3"], ["q22"])
+    ts(1, qm, T.pi[:, 4:5], 0.0, None, OP.not_equal, None, ["qi7"], ["qm"])
+    ts(1, qe, T.pi[:, 4:5], 0.0, 32.0, OP.is_equal, OP.mult, ["qi7"], ["qe"])
+    qc = {}
+    for i, (x, m, c) in enumerate((("j", 8, 0), ("z", 1, 0), ("zw", 1, H), ("x0", -1, TOP - W), ("x1", -1, TOP - W - H),
+                                   ("xl", -1, TOP - YH))):
+        qc[x] = T.q1[:, 10 + i:11 + i]
+        ts(1, qc[x], T.pi[:, 1:2], m * S19, c * S19, OP.mult, OP.add, ["qi"], ["qc" + x])
     for t, (m, sh) in enumerate(TURN_Q):
-        ts(T.q1[:, 4 + t:5 + t], q1, 32.0 * m, None, OP.mult, None, ["q1"], ["qa%d" % t])
-    ts(T.id1[:], T.bandv[:, 0:128], 0.0, None, OP.is_equal, None, ["bandv"], ["id1"])
-    ts(T.bm[:], T.bandv[:], q1, 15.0, OP.add, OP.is_equal, ["bandv", "q1"], ["bm"])
-    ts(T.trv[:], T.bandv[:, 0:128], 0.0, S12, OP.is_ge, OP.mult, ["bandv"], ["trv"])
-    for t, (m, sh) in enumerate(TURN_Q):
+        qa = T.q1[:, 4 + t:5 + t]
+        ts(1, qa, T.pi[:, 1:2], 32.0 * m, None, OP.mult, None, ["qi"], ["qa%d" % t])
         if sh:
-            ts(T.q1[:, 4 + t:5 + t], T.pi[:, sh:sh + 1], -32.0 * 127, T.q1[:, 4 + t:5 + t], OP.mult, OP.add,
-               ["qi%d" % sh, "qa%d" % t], ["qa%d" % t])
-    tt(T.tri[:], T.trv[:], T.blkm[:], OP.mult, ["trv", "blkm"], ["tri"])
+            ts(1, qa, T.pi[:, sh:sh + 1], -32.0 * 127, qa, OP.mult, OP.add, ["qi%d" % sh, "qa%d" % t], ["qa%d" % t])
+        ts(16, T.l32[:, 16 * t:16 * t + 16], T.lt[:, 16 * t:16 * t + 16], qa, None, OP.add, None, ["lt%d" % t, "qa%d" % t], ["l32.%d" % t])
+    ts(16, firstu, T.lt[:, 64:80], q4, None, OP.add, None, ["lt4", "q4"], ["firstu"])
+    ts(4, T.lt[:, 88:92], T.lt[:, 80:84], q22, None, OP.add, None, ["lt5", "q22"], ["lt6"])
+    ts(4, T.lists[:, 24:28], T.lt[:, 88:92], qm, qe, OP.mult, OP.add, ["lt6", "qm", "qe"], ["rep8g"])
+    ts(4, T.lists[:, 28:32], T.lt[:, 84:88], q22, None, OP.add, None, ["lt5", "q22"], ["rep8t"])
+    ts(H, T.blkm[:], T.blkv[:], q1, 0.0, OP.add, OP.is_equal, ["blkv", "q1"], ["blkm"])
+    ts(H, T.id1[:], T.bandv[:, 0:128], 0.0, None, OP.is_equal, None, ["bandv"], ["id1"])
+    ts(144, T.bm[:], T.bandv[:], q1, 15.0, OP.add, OP.is_equal, ["bandv", "q1"], ["bm"])
+    act(144, T.band[:], T.bm[:], AF.Identity, ["bm"], ["band"], scale=S12)
     for name, c in (("id16", 16.0), ("idm2", -2.0), ("idh", 0.5), ("idmh", -0.5)):
-        act(T[name][:], T.id1[:], AF.Identity, ["id1"], [name], scale=c)
-    ms(T.dd[:, 16:32], L * S20, ["ddz"])
-    ts(T.kc[:], T.kv[:], q128, S12, OP.add, OP.mult, ["kv", "q128"], ["kc"])
-    ts(T.repu[:, 0:4], T.kv[:, 0:4], 0.0, q1, OP.mult, OP.add, ["kv", "q1"], ["repu"])
-    ts(col, T.kv[:, 0::16], q128, 1.0 / 16, OP.add, OP.mult, ["kv", "q128"], ["col"])
-    ts(T.kb[:], T.kc[:, 0::16], -S12, None, OP.add, None, ["kc"], ["kb"])
-    cp(colu, col, ["col"], ["colu"])
-    ts(T.ol[:, 0:16], col, S20, None, OP.mult, None, ["col"], ["ol0"])
-    for t in range(ROUNDS):
-        ts(T.l32[:, 16 * t:16 * t + 16], T.lt[:, 16 * t:16 * t + 16], T.q1[:, 4 + t:5 + t], None, OP.add, None,
-           ["lt%d" % t, "qa%d" % t], ["l32.%d" % t])
-    ts(T.cx[:, 48:64], T.lt[:, 80:96], q31, None, OP.add, None, ["lt5", "q31"], ["cx3"])
-    ts(pos, T.l32[:, 48:64], 1.0 / 32, float(W), OP.mult, OP.add, ["l32.3"], ["pos"])
-    ts(T.ol[:, 16:32], T.l32[:, 48:64], S20 / 32, None, OP.mult, None, ["l32.3"], ["ol16"])
-    ts(T.ol[:, 32:48], pos, S20, None, OP.mult, None, ["pos"], ["ol32"])
-    for t in range(ROUNDS - 1):
-        tt(T.cx[:, 16 * t:16 * t + 16], T.l32[:, 16 * t:16 * t + 16], pos, OP.subtract, ["l32.%d" % t, "pos"], ["cx%d" % t])
-    ts(T.w2[:], T.blkm[:], w, 2.0, OP.mult, OP.mult, ["blkm", "w"], ["w2"])
-    act(T.z[:], T.zin[:].indirect(firstu), AF.Identity, ["zin", "firstu"], zall)
-    ts(T.wband[:], T.bm[:], w, None, OP.mult, None, ["bm", "w"], ["wband"])
-    cp(tw[0][:, 0:L], T.jin[:].indirect(firstu), ["jin", "firstu"], ["j0"])
-    lists(0, xall)
+        act(H, T[name][:], T.id1[:], AF.Identity, ["id1"], [name], scale=c)
+    ts(H, T.kc[:], T.kv[:], q128, S12, OP.add, OP.mult, ["kv", "q128"], ["kc"])
+    ts(8, T.col[:], T.kv[:, 0::16], q128, 1.0 / 16, OP.add, OP.mult, ["kv", "q128"], ["col"])
+    ts(8, T.kb[:], T.kc[:, 0::16], -S12, None, OP.add, None, ["kc"], ["kb"])
+    ts(8, T.kj[:], T.kc[:, 0::16], 1 - S19 / (16 * S12), -S12, OP.mult, OP.add, ["kc"], ["kj"])
+    cp(8, colu, T.col[:], ["col"], ["colu"])
+    ms(H, T.c19[:], 2.0 ** -19, ["c19"])
+    ms(H, T.c17[:], 32 / S12, ["c17"])
+    ms(H, T.sa[:], 0.0, ["sa.0", "sa.1"])
+    ms(96, T.sv[:], -1.0, ["g4.0", "t4.0", "g4.1", "t4.1"])
+    run = CFG["run"]
+    ms(16 * run, T.mask[:, 0:16 * run], 1.0, ["mask"])
+    ms(run, T.mask[:, 0:16 * run:16], 0.0, ["mask"])
+    ts(64, T.sd[:, 128:192], ia, 16 * S19, qc["z"], OP.mult, OP.add, ["ia", "qcz"], ["sdz"])
+    ts(8, T.sd[:, 128:192:8], T.lt[:, 128:192:8], 16 * S19, qc["zw"], OP.mult, OP.add, ["ia", "qczw"], ["sdz"])
+    for h in range(2):
+        ts(64, T.sd[:, 64 * h:64 * h + 64], ia, S19, qc["j"], OP.mult, OP.add, ["ia", "qcj"], ["sdj.%d" % h])
+        ts(64, T.sd[:, 192 + 64 * h:256 + 64 * h], ia, -16 * S19, qc["x%d" % h], OP.mult, OP.add, ["ia", "qcx%d" % h], ["sdx.%d" % h])
+    ts(H, T.w2[:], T.blkm[:], w, 2.0, OP.mult, OP.mult, ["blkm", "w"], ["w2"], r=0.5)
+    ts(144, T.wband[:], T.bm[:], w, None, OP.mult, None, ["bm", "w"], ["wband"], r=0.5)
+    act(L, T.z[:], T.zin[:].indirect(firstu), AF.Identity, ["zin", "firstu"], zall, r=gat)
+    for h in range(2):
+        cp(H, tw[0][:, slab(0, h, 0, 1)], T.jin[:].indirect(T.lists[:, 8 * h:8 * h + 8]), ["jin", "firstu"], ["j0.%d" % h], r=gat)
+        lists(0, h, xall)
 
     def fill(ap, n, c, wr):
-        iota(ap, [[0, n]], 0, wr, base=int(c))
+        iota(ap, [[0, n]], int(c), 0, wr)
 
+    fill(T.ones[:], H, 1, ["ones"])
     for n in (1, 2, 3, 4):
         fill(T["c%d" % n][:], 512 >> n, 1, ["c%d.0" % n, "c%d.1" % n])
-    fill(T.c4096[:], 128, 4096, ["c4096"])
-    fill(T.neg[:], L, -LIFT, ["neg"])
+    fill(T.neg[:], H, -LIFT, ["neg"])
     fill(T.X[:, W:W + L], L, 0, ["Xd"])
-    fill(T.zz[:], L + FA, 0, ["zzl", "zzw"])
-    fill(T.hw[:], L + FA, 0, ["hl", "hw"])
-    for t in range(ROUNDS):
-        fill(T["ly%d" % t][:, L:2 * L], L, LIFT, ["lyc%d" % t])
     for hf in range(2):
         fill(T.Y[:, hf * YW + YH:hf * YW + YW], YW - YH, 0, ["Yd%d" % hf])
 
-    def forms(src, rd, lo, hi, bias, fb="pP", fo=0):
-        act(T[fb][:, fo + lo:fo + hi], src, AF.Identity, rd[:1], qs(lo, hi, fb + "J"), [fb])
-        act(T[fb][:, L + fo + lo:L + fo + hi], src, AF.Identity, rd, qs(lo, hi, fb + "JA"), [fb], bias=bias, scale=32.0)
+    def picks(t, h, bias, rd, parts, later):
+        lo, s = H * h, ".%d" % h
+        bJ, bU = ("pP", "pT1")[h], ("pU", "pG1")[h]
+        act(H, T[bJ][:, H:L], tw[t][:, slab(t, h, 0, 1)], AF.Identity, ["j%d%s" % (t, s)], ["pJ" + s] + ["g1.1"] * h, [bJ])
+        act(H, T[bJ][:, L:L + H], tw[t][:, slab(t, h, 0, 1)], AF.Identity, ["j%d%s" % (t, s)] + rd, ["pJA" + s] + ["pa.1"] * h, [bJ],
+            bias=bias, scale=32.0)
+        mm(H, bU, T[bU][:, lo:lo + H], T.w2[:], T.z[:, lo:lo + H], True, True, ["w2", "z%d" % h], ["u" + s])
+        for c0 in range(lo, lo + H, parts):
+            c1, o = c0 + parts, c0 - lo
+            ts(parts, T.ha[:, c0:c1], T[bU][:, c0:c1], 1.0, None, OP.add, None, ["u" + s], qs(c0, c1, "ha"), [bU])
+            ts(parts, T.hb[:, c0:c1], T.ha[:, c0:c1], 2047, None, OP.bitwise_and, None, qs(c0, c1, "ha"), qs(c0, c1, "hb"))
+            tt(parts, T.hc[:, c0:c1], T.hb[:, c0:c1], T[bJ][:, H + o:H + o + parts], OP.mult, qs(c0, c1, "hb") + ["pJ" + s],
+               qs(c0, c1, "hc"), [bJ])
+            tt(parts, (T.hf if later else T.hd)[:, c0:c1], T.hc[:, c0:c1], T[bJ][:, L + o:L + o + parts], OP.add,
+               qs(c0, c1, "hc") + ["pJA" + s], qs(c0, c1, "hf" if later else "hd"), [bJ])
+            if not later:
+                finish(c0, c1)
 
-    forms(tw[0][:, 0:L], ["j0"], 0, L, -DROP)
+    def finish(c0, c1):
+        n = c1 - c0
+        ts(n, T.he[:, c0:c1], T.hd[:, c0:c1], 5, W - 1, OP.arith_shift_right, OP.bitwise_and, qs(c0, c1, "hd"), qs(c0, c1, "he"))
+        cp(n, T.hu[:, c0:c1], T.he[:, c0:c1], qs(c0, c1, "he"), qs(c0, c1, "hu"))
 
-    def newz(t, lo, hi):
-        ly = T["ly%d" % t]
-        return [lambda: tt(T.zl[:, lo:hi], ly[:].indirect(T.off[:, 16 + lo // 16:16 + hi // 16]), T.base[:, lo:hi], OP.add,
-                           ["lya", "lyb", "lyc%d" % t, "off", "base"], qs(lo, hi, "zl")),
-                lambda: ts(T.z[:, lo:hi], T.zl[:, lo:hi], -LIFT, 1.0, OP.add, OP.max, qs(lo, hi, "zl"), qs(lo, hi, "z"))]
-
-    def picks(lo, hi, bank, zsrc=None, zt=None, out=None, ot=None):
-        s = str(lo)
-        fb, fo = ("pP", 0) if zsrc is None else ("pA", 64)
-        zsrc, zt = (T.z[:, lo:hi], qs(lo, hi, "z")) if zsrc is None else (zsrc, zt)
-
-        def first():
-            mm(T[bank][:, lo:hi], T.w2[:], zsrc, True, True, ["w2"] + zt, ["u" + s], [bank])
-            ts(T.ha[:, lo:hi], T[bank][:, lo:hi], 1.0, None, OP.add, None, ["u" + s], ["ha" + s], [bank])
-
-        steps = [first,
-                 lambda: ts(T.hb[:, lo:hi], T.ha[:, lo:hi], 2047, None, OP.bitwise_and, None, ["ha" + s], ["hb" + s]),
-                 lambda: tt(T.hc[:, lo:hi], T.hb[:, lo:hi], T[fb][:, fo + lo:fo + hi], OP.mult, ["hb" + s] + qs(lo, hi, fb + "J"),
-                            ["hc" + s], [fb]),
-                 lambda: tt(T.hd[:, lo:hi] if out is None else out, T.hc[:, lo:hi], T[fb][:, L + fo + lo:L + fo + hi], OP.add,
-                            ["hc" + s] + qs(lo, hi, fb + "JA"), ["hd" + s] if out is None else ot, [fb])]
-        return steps + ([] if out is not None else finish(lo, hi))
-
-    def finish(lo, hi):
-        s = str(lo)
-        return [lambda: ts(T.he[:, lo:hi], T.hd[:, lo:hi], 5, W - 1, OP.arith_shift_right, OP.bitwise_and, ["hd" + s], ["he" + s]),
-                lambda: cp(T.hu[:, lo:hi], T.he[:, lo:hi], ["he" + s], qs(lo, hi, "hu"))]
+    for h in range(2):
+        picks(0, h, -DROP, [], 64, False)
 
     for t in range(ROUNDS):
         last = t == ROUNDS - 1
-        sv, lv, yh, ly = T["sv%d" % t], T["lv%d" % t], T["yh%d" % t], T["ly%d" % t]
-
-        def gather(n):
-            c0, c1 = PIECES[n]
-            act(T.xg[:, L * c0:L * c1], T.X[:, 0:W].indirect(T.hu[:, 16 * c0:16 * c1]), AF.Identity,
-                xall + qs(16 * c0, 16 * c1, "hu"), qs(16 * c0, 16 * c1, "x"))
-
-        def zrep(n):
-            c0, c1 = n
-            bank, o = "pZ%d" % (c0 // 8), 64 * (c0 % 8)
+        sm, lm, yh, ly = T["sm%d" % t], T["lm%d" % t], T["yh%d" % t], T["ly%d" % t]
+        for h in range(2):
             for r in range(4):
-                mm(T[bank][:, o + r:o + 64 * (c1 - c0):4], T.id1[:], T.z[:, 16 * c0:16 * c1], True, True,
-                   ["id1"] + qs(16 * c0, 16 * c1, "z"), qs(16 * c0, 16 * c1, "zp") + (["S10", "P10"] if c0 < 8 else []), [bank])
-
-        if t == 0:
-            weave(picks(0, 64, "pU"), picks(64, 128, "pA"))
-            gather(0)
-            weave(picks(128, 192, "pU"), picks(192, L, "pA"))
-            zrep((0, 8))
-            late = []
-        else:
-            zrep((0, 4))
-            gather(0)
-            weave(newz(t - 1, 64, 128) + picks(64, 128, "pU"), newz(t - 1, 128, 192) + picks(128, 192, "pA"))
-            late = newz(t - 1, 192, L) + picks(192, L, "pU")
-            zrep((4, 8))
-        gather(1)
-        gather(2)
-
-        def after_late():
-            zrep((8, 16))
-            for h in range(2):
-                for q in range(16):
-                    mm(T.pA[:, L + 8 * h:L + 8 * h + 8], T.wband[:, 15 - q:143 - q], T.z[:, 128 * h + 8 * q:128 * h + 8 * q + 8],
-                       q == 0, q == 15, ["wband"] + zall, ["ul"], ["pA"])
-
-        def idle():
-            act(T.bw[:, 0:L], T.z[:].indirect(colu), AF.Identity, zall + ["colu"], ["zq"], bias=LIFT - 0.25, scale=0.5)
-            if not last:
-                jl = T.jw[:, 2 * FA:3 * FA]
-                act(jl, tw[t][:, 0:L].indirect(T.repu[:, 16:16 + FA // 16]), AF.Identity, ["j%d" % t, "colu"], ["jl"])
-                forms(jl, ["jl"], 0, FA, -DROP, "pA", 64)
-
-        def mins(n, beside):
-            c0, c1 = PIECES[n]
-            bank, o = "pZ%d" % (c0 // 8), 64 * (c0 % 8)
+                mm(H, "pZ%d" % h, T["pZ%d" % h][:, r::4], T.id1[:], T.z[:, H * h:H * h + H], True, True, ["id1", "z%d" % h],
+                   ["zp%d" % h, "D%d" % h, "R%d" % h])
+        for lo, hi in PIECES:
+            h, n = lo // H, hi - lo
+            act(16 * n, T.xg[:, 16 * lo:16 * hi], T.X[:, 0:W].indirect(T.hu[:, lo:hi]), AF.Identity, xall + qs(lo, hi, "hu"),
+                qs(lo, hi, "x") + ["gq"], r=gat)
+            if lo % H == 0:
+                mm(H, "pT%d" % h, T["pT%d" % h][:, 0:H], T.c19[:], T.ones[:], True, False, ["c19", "ones"] + qs(lo, hi, "x"),
+                   ["tsum%d" % h])
             for k in range(4):
-                tt(T.mn[:, L * c0 + k:L * c1:4], T.xg[:, L * c0 + k:L * c1:4], T[bank][:, o:o + 64 * (c1 - c0)], OP.min,
-                   qs(16 * c0, 16 * c1, "x") + qs(16 * c0, 16 * c1, "zp"), ["m%d.%d" % (n, k)], [bank])
-                if k < len(beside):
-                    step(beside[k])
-
-        def sums(n, kind):
-            c0, c1 = PIECES[n]
-            h = c0 // 8
-            bank, o, _ = PLACE[h][kind]
-            rd = qs(16 * c0, 16 * c1, "x") if kind == 0 else ["m%d.%d" % (n, k) for k in range(4)]
-            for j in range(2 * c0, 2 * c1):
-                mm(T[bank][:, o + j % 16:o + 128:16], (T.xg, T.mn)[kind][:, 128 * j:128 * j + 128], T.blkm[:, 0::16], True, True,
-                   ["blkm"] + rd, ["S%d%d" % (h, kind)] + (qs(0, 128, "zp") if bank == "pZ0" else []), [bank])
-
-        def turn(h, kind, e):
-            bank, o, op_ = PLACE[h][kind]
-            s, sb = "%d%d" % (h, kind), T.ssb[:, 256 * h + 128 * kind:256 * h + 128 * kind + 128]
-            if e == "a":
-                act(sb, T[bank][:, o:o + 128], AF.Identity, ["S" + s], ["sb" + s], [bank], bias=1.0 - kind)
-            elif e == "v":
-                ts(sb, T[bank][:, o:o + 128], 1.0 - kind, None, OP.add, None, ["S" + s], ["sb" + s], [bank])
-            else:
-                mm(T[bank][:, op_:op_ + 128], sb, T.tri[:], True, True, ["sb" + s, "tri"], ["P" + s], [bank])
-
-        def tcopy(h, e):
-            bank, _, op_ = PLACE[h][0]
-            if e == "a":
-                act(T.ts[:, 128 * h:128 * h + 128], T[bank][:, op_:op_ + 128], AF.Identity, ["P%d0" % h], ["ts.%d" % h], [bank])
-            else:
-                cp(T.ts[:, 128 * h:128 * h + 128], T[bank][:, op_:op_ + 128], ["P%d0" % h], ["ts.%d" % h], [bank])
-
-        scanned = []
-
-        def runmax(c):
-            scanned.append(c)
-            scan(T.pm[:, L * c:L * c + L], T.mask[:], T.xg[:, L * c:L * c + L], OP.mult, OP.max, ["mask", "x%d" % c], ["pm%d" % c])
-
-        def low(h):
-            lo, hi, n, s = 128 * h, 128 * h + 128, 128, ".%d" % h
-            bank, _, o = PLACE[h][1]
-            sm = "P%d1" % h
-            g1, pa, pa2 = T.pD[:, lo:hi], T.pD[:, L + lo // 2:L + hi // 2], T.pD[:, L + lo // 2:L + lo // 2 + n // 4]
-            pb, pb2 = T.pb[:, lo // 2:hi // 2], T.pb[:, lo // 2:lo // 2 + n // 4]
-            c1_, c2_ = T.c1[:, lo:hi], T.c2[:, lo // 2:hi // 2]
-
-            def s1():
-                tt(pa, T[bank][:, o + 1:o + n:2], T.ts[:, lo:hi:2], OP.mult, [sm, "ts" + s], ["pa" + s, "D", "R"], [bank, "pD"])
-                tt(pb, T[bank][:, o:o + n:2], T.ts[:, lo + 1:hi:2], OP.mult, [sm, "ts" + s], ["pb" + s], [bank])
-
-            def s2():
-                tt(T.c1[:, lo + 1:hi:2], pa, pb, OP.is_gt, ["pa" + s, "pb" + s], ["c1" + s], ["pD"])
-
-            def s3():
-                scan(g1, c1_, T[bank][:, o:o + n], OP.max, OP.min, ["c1" + s, sm], ["g1" + s, "D"], [bank, "pD"])
-                scan(T.t1[:, lo:hi], c1_, T.ts[:, lo:hi], OP.max, OP.min, ["c1" + s, "ts" + s], ["t1" + s])
-
-            def s4():
-                tt(pa2, T.pD[:, lo + 3:hi:4], T.t1[:, lo + 1:hi:4], OP.mult, ["g1" + s, "t1" + s], ["pa" + s], ["pD"])
-                tt(pb2, T.pD[:, lo + 1:hi:4], T.t1[:, lo + 3:hi:4], OP.mult, ["g1" + s, "t1" + s], ["pb" + s], ["pD"])
-                scan(T.k1[:, lo:hi], c1_, T.kc[:, lo:hi], OP.max, OP.min, ["c1" + s, "kc"], ["k1" + s])
-
-            def s5():
-                tt(T.c2[:, lo // 2 + 1:hi // 2:2], pa2, pb2, OP.is_gt, ["pa" + s, "pb" + s], ["c2" + s], ["pD"])
-
-            def s6():
-                scan(T.g2[:, lo // 2:hi // 2], c2_, T.pD[:, lo + 1:hi:2], OP.max, OP.min, ["c2" + s, "g1" + s], ["g2" + s], ["pD"])
-                scan(T.t2[:, lo // 2:hi // 2], c2_, T.t1[:, lo + 1:hi:2], OP.max, OP.min, ["c2" + s, "t1" + s], ["t2" + s])
-
-            def s7():
-                scan(T.k2[:, lo // 2:hi // 2], c2_, T.k1[:, lo + 1:hi:2], OP.max, OP.min, ["c2" + s, "k1" + s], ["k2" + s])
-
-            return [s1, s2, s3, s4, s5, s6, s7]
-
-        record = [lambda: cp(T.ti[:], T.pA[:, L:L + 16], ["ul"], ["ti"], ["pA"]),
-                  lambda: ts(T.rc[:], T.ti[:], 31, None, OP.bitwise_and, None, ["ti"], ["rc"]),
-                  lambda: tt(T.rf[:], T.rc[:], T.l32[:, 16 * t:16 * t + 16], OP.add, ["rc", "l32.%d" % t], ["rf"]),
-                  lambda: cp(T.offr[:], T.rf[:], ["rf"], ["offr"]),
-                  lambda: tt(T.dx[:], T.rc[:], T.cx[:, 16 * t:16 * t + 16], OP.add, ["rc", "cx%d" % t], ["dx"])]
-        first = low(0)
-        second = low(1)
-        chains = {"d": late, "r": record, "L": first, "H": second}
-        single = {"s": lambda: runmax(len(scanned)), "|": lambda: (weave(late), after_late()), "i": idle, ".": lambda: None}
-
-        def step(what):
-            if what in single:
-                single[what]()
-            elif chains[what]:
-                chains[what].pop(0)()
-
-        for what in CFG["phase"].split():
-            if what[0] == "m":
-                mins(int(what[1]), what[2:])
-            elif what[0] == "g":
-                gather(int(what[1]))
-            elif what[0] in "TG":
-                sums(int(what[1]), "TG".index(what[0]))
-            elif what[0] in "avp":
-                turn(int(what[1]), int(what[2]), what[0])
-            elif what[0] == "t":
-                tcopy(int(what[1]), what[2])
-            else:
-                for x in what:
-                    step(x)
-        weave(first, second)
-
-        def pack(blk, e="a"):
-            bank = ("pP", "pU", "pZ1")[blk % 3]
-            c0 = 512 * blk
-            mm(T[bank][:], T.id1[:], T.X[:, c0:c0 + 512], True, False, ["id1"] + xall, [bank + "d"], [bank])
-            mm(T[bank][:], T.id16[:], T.X[:, W // 2 + c0:W // 2 + c0 + 512], False, True, ["id16"] + xall, [bank + "d"], [bank])
-            y0 = c0 + (YW - YH) * (blk // 4)
-            if e == "a":
-                act(T.Y[:, y0:y0 + 512], T[bank][:], AF.Identity, [bank + "d"], ["Y%d" % blk], [bank])
-            else:
-                cp(T.Y[:, y0:y0 + 512], T[bank][:], [bank + "d"], ["Y%d" % blk], [bank])
-
-        if last:
-            for blk in range(CFG["yearly"]):
-                pack(blk)
-
-        def filler():
-            if record:
-                record.pop(0)()
-
-        for n, cnt in ((3, 32), (4, 16)):
-            gi, ti_, ki, c_ = T["g%d" % (n - 1)], T["t%d" % (n - 1)], T["k%d" % (n - 1)], T["c%d" % n]
-            gn, tn, kn = [[x + "2.0", x + "2.1"] if n == 3 else [x + "3"] for x in "gtk"]
-            cn = ["c%d.0" % n]
-            tt(T.pa[:, 0:cnt], gi[:, 3::4], ti_[:, 1::4], OP.mult, gn + tn, ["pa"])
-            tt(T.pb[:, 0:cnt], gi[:, 1::4], ti_[:, 3::4], OP.mult, gn + tn, ["pb.0"])
-            filler()
-            tt(c_[:, 1::2], T.pa[:, 0:cnt], T.pb[:, 0:cnt], OP.is_gt, ["pa", "pb.0"], cn)
-            filler()
-            go, to = (T.g3[:], T.t3[:]) if n == 3 else (sv[:, 32:64], sv[:, 0:32])
-            scan(go, c_[:], gi[:, 1::2], OP.max, OP.min, cn + gn, ["g%d" % n])
-            scan(to, c_[:], ti_[:, 1::2], OP.max, OP.min, cn + tn, ["t%d" % n])
-            if n == 4:
-                swap(t, lv[:], sv[:, 0:64], ["g4", "t4"], ["lv"], "av%d" % t)
-            scan(T["k%d" % n][:], c_[:], ki[:, 1::2], OP.max, OP.min, cn + kn, ["k%d" % n])
-        filler()
-        ts(T.offy[:], T.k4[:, 1::2], 4096.0, None, OP.mult, None, ["k4"], ["offy"])
-
-        def profile(lo, hi, toks, sem):
-            top = 128 if hi <= 128 else L
-            act(yh[:, lo:hi], T.pm[:, 0:16 * top].indirect(T.offy[:, lo // 16:hi // 16]), AF.Identity,
-                qs(0, top, "pm") + ["offy"], qs(lo, hi, "yh"), scale=0.5)
-            swap(t, ly[:, lo:hi], yh[:, lo:hi], qs(lo, hi, "yh"), toks, sem)
-
-        def apart(lo, hi):
-            mm(T.pD[:, lo:hi], T.idm2[:], yh[:, lo:hi], True, False, ["idm2"] + qs(lo, hi, "yh"), ["D", "g1.0", "g1.1"], ["pD"])
-            for c in range(lo // 16, hi // 16):
-                h0 = 128 * (c // 8)
-                mm(T.pD[:, 16 * c:16 * c + 16], T.id1[:], T.z[:, h0 + c % 8:h0 + 128:8], False, c == hi // 16 - 1, ["id1"] + zall,
-                   ["D"], ["pD"])
-            act(T.bw[:, L + lo:L + hi], T.pD[:, lo:hi], AF.Abs, ["D"], qs(lo, hi, "zw"), ["pD"])
-
-        def change():
-            mm(T.pD[:, L:2 * L], (T.idmh if last else T.idh)[:], T.old[:], True, False, ["idh", "idmh", "old"],
-               ["R", "pa.0", "pa.1"], ["pD"])
-            mm(T.pD[:, L:2 * L], T.id1[:], yh[:], False, True, ["id1"] + qs(0, L, "yh"), ["R"], ["pD"])
-            act(T.rec[:], T.pD[:, L:2 * L], AF.Identity, ["R"], ["rec"], ["pD"], bias=LIFT - 0.25)
-
-        def oldrec():
-            act(T.old[:], T.X[:, 0:W].indirect(T.offr[:]), AF.Identity, xall + ["offr"], ["old"])
-            act(T.dd[:, 32:48], T.dx[:], AF.Identity, ["dx"], ["ddx"], scale=S20)
-
-        rest = [lambda c=c: runmax(c) for c in range(16) if c not in scanned]
-        tt(T.dd[:, 0:16], T.k4[:, 1::2], T.kb[:], OP.subtract, ["k4", "kb"], ["ddj"])
+                tt(4 * n, T.mn[:, 16 * lo + k:16 * hi:4], T.xg[:, 16 * lo + k:16 * hi:4], T["pZ%d" % h][:, 4 * (lo % H):4 * (lo % H + n)],
+                   OP.min, qs(lo, hi, "x") + ["zp%d" % h], ["m%d.%d" % (lo, k)], ["pZ%d" % h])
+            for kind, src in (("T", T.xg), ("G", T.mn)):
+                bank = "p%s%d" % (kind, h)
+                for j in range(lo // 8, hi // 8):
+                    q = j % 16
+                    mm(H, bank, T[bank][:, 0:H], T.band[:, 15 - q:143 - q], src[:, H * j:H * j + H], kind == "G" and q == 0, q == 15,
+                       ["band"] + (qs(lo, hi, "x") if kind == "T" else ["m%d.%d" % (lo, k) for k in range(4)]),
+                       ["%ssum%d" % (kind.lower(), h)])
+        for lo in range(0, L, run):
+            scan(16 * run, T.pm[:, 16 * lo:16 * (lo + run)], T.mask[:, 0:16 * run], T.xg[:, 16 * lo:16 * (lo + run)], OP.mult, OP.max,
+                 ["mask"] + qs(lo, lo + run, "x"), qs(lo, lo + run, "pm"), r=0.5)
+        for h in range(2):
+            for q in range(16):
+                mm(8, "pU", T.pU[:, L + 8 * h:L + 8 * h + 8], T.wband[:, 15 - q:143 - q], T.z[:, H * h + 8 * q:H * h + 8 * q + 8],
+                   q == 0, q == 15, ["wband", "z%d" % h, "hu7"], ["ul"])
+        cp(16, T.ti[:], T.pU[:, L:L + 16], ["ul"], ["ti"], ["pU"])
+        ts(16, T.rc[:], T.ti[:], 31, None, OP.bitwise_and, None, ["ti"], ["rc"])
+        tt(16, T.rf[:], T.rc[:], T.l32[:, 16 * t:16 * t + 16], OP.add, ["rc", "l32.%d" % t], ["rf"])
+        cp(16, T.offr[:], T.rf[:], ["rf"], ["offr"])
+        act(L, T.old[:], T.X[:, 0:W].indirect(T.offr[:]), AF.Identity, xall + ["offr"], ["old"], r=gat)
         ys = [["Y%d" % b for b in range(4 * hf, 4 * hf + 4)] + ["Yd%d" % hf] for hf in range(2)]
-        if not last:
-            profile(0, FA, ["lya"], "ay%d" % t)
-            act(sv[:, 64:96], sv[:, 0:32], AF.Identity, ["t4"], ["t4b"])
-            apart(0, FA)
-            n4 = FA // 16
-            rest.pop(0)()
-            tt(T.ow[:, 0:n4], T.dd[:, 0:n4], T.ol[:, 0:n4], OP.add, ["ddj", "ol0"], ["ow"])
-            rest.pop(0)()
-            ts(T.offw[:, 0:n4], T.ow[:, 0:n4], 2.0 ** 20, None, OP.mult, None, ["ow"], ["offw"])
-            oldrec()
-            weave(rest)
-            profile(FA, L, ["lyb"], "ab%d" % t)
-            jw, jw32, wa, wb = T.jw[:, 0:FA], T.jw[:, FA:2 * FA], T.wa[:, 0:FA], T.wa[:, FA:2 * FA]
-            act(jw, tw[t][:].indirect(T.offw[:, 0:n4]), AF.Identity, ["offw"] + shifted(t), ["jw"])
-            act(jw32, jw, AF.Identity, ["jw"], ["jw32"], bias=-DROP, scale=32.0)
-            ts(T.zz[:, L:L + FA], T.bw[:, L:L + FA], 1.0, None, OP.max, None, qs(0, FA, "zw"), ["zzw"])
-            mm(T.pU[:, 0:FA], T.w2[:], T.zz[:, L:L + FA], True, True, ["w2", "zzw"], ["u0"], ["pU"])
-            change()
-            apart(FA, L)
-            ts(wa, T.pU[:, 0:FA], 1.0, None, OP.add, None, ["u0"], ["wa"], ["pU"])
-            ts(wb, wa, 2047, None, OP.bitwise_and, None, ["wa"], ["wb"])
-            tt(T.wc[:], wb, jw, OP.mult, ["wb", "jw"], ["wc"])
-            tt(T.hw[:, L:L + FA], T.wc[:], jw32, OP.add, ["wc", "jw32"], ["hw"])
-        else:
-            act(sv[:, 64:96], sv[:, 0:32], AF.Identity, ["t4"], ["t4b"])
-            oldrec()
-            pack(CFG["yearly"])
-            weave(rest)
-            profile(0, L, ["lya", "lyb"], "ay%d" % t)
-            for blk in range(CFG["yearly"] + 1, 8):
-                pack(blk, "v")
-            change()
-            ts(T.ol[:, 32:48], T.lt[:, 96:112], q1, S20, OP.add, OP.mult, ["lt6", "q1"], ["ol32"])
-            ts(T.d1[:], T.rec[:, 0:128], -LIFT, None, OP.add, None, ["rec"], ["d1"])
-            ts(T.d16[:], T.rec[:, 128:L], -LIFT, 16.0, OP.add, OP.mult, ["rec"], ["d16"])
-            tt(T.ya[:, 0:64], T.Y[:, 0:YW].indirect(T.offr[:, 0:4]), T.d1[:, 0:64], OP.add, ys[0] + ["offr", "d1"], ["ya0"])
-            tt(T.ya[:, 64:128], T.Y[:, YW - YH:2 * YW].indirect(T.offr[:, 4:8]), T.d1[:, 64:128], OP.add,
-               ys[0] + ys[1] + ["offr", "d1"], ["ya1"])
-            apart(0, L)
-        nxt = T.jfin[:] if last else tw[t + 1][:, 0:L]
-
-        def deltas():
-            tt(T.wd[:], T.win[:].indirect(T.repu[:, 0:3]), T.dd[:], OP.mult, ["win", "repu", "ddj", "ddz", "ddx"], ["wd"])
+        if last:
+            ts(8, T.offh[:], T.rf[:, 8:16], -float(W // 2), None, OP.add, None, ["rf"], ["offh"])
+            for blk in range(8):
+                bank, c0 = ("pP", "pU")[blk % 2], 512 * blk
+                y0 = c0 + (YW - YH) * (blk // 4)
+                toks = ["pJ.0", "pJA.0"] if bank == "pP" else ["u.0", "ul"]
+                mm(512, bank, T[bank][:], T.id1[:], T.X[:, c0:c0 + 512], True, False, ["id1", "x15"] + xall, toks)
+                mm(512, bank, T[bank][:], T.id16[:], T.X[:, W // 2 + c0:W // 2 + c0 + 512], False, True, ["id16"] + xall, toks)
+                if blk < 8 - CFG["vpack"]:
+                    act(512, T.Y[:, y0:y0 + 512], T[bank][:], AF.Identity, toks, ["Y%d" % blk], [bank])
+                else:
+                    cp(512, T.Y[:, y0:y0 + 512], T[bank][:], toks, ["Y%d" % blk], [bank])
+        for h in range(2):
+            s, lo, bT, bG, bZ = ".%d" % h, H * h, "pT%d" % h, "pG%d" % h, "pZ%d" % h
+            pT, pG, pZ = T[bT], T[bG], T[bZ]
+            half = slice(lo, lo + H)
+            lead[0] = CFG["lead"] if h == 0 else 0.0
+            scan(H, T.ts[:, half], T.mask[:, 0:H], pT[:, 0:H], OP.mult, OP.add, ["mask", "tsum%d" % h], ["ts" + s], [bT])
+            scan(H, T.gs[:, half], T.mask[:, 0:H], pG[:, 0:H], OP.mult, OP.add, ["mask", "gsum%d" % h], ["gs" + s], [bG])
+            g1, pa, pb = pT[:, H:L], pT[:, L:L + 64], T.pb[:, 64 * h:64 * h + 64]
+            tt(64, pa, pG[:, 1:H:2], T.ts[:, lo:lo + H:2], OP.mult, ["gsum%d" % h, "ts" + s], ["pa" + s], [bG, bT])
+            tt(64, pb, pT[:, 1:H:2], T.gs[:, lo:lo + H:2], OP.mult, ["tsum%d" % h, "gs" + s], ["pb" + s], [bT])
+            tt(64, T.c1[:, lo + 1:lo + H:2], pa, pb, OP.is_gt, ["pa" + s, "pb" + s], ["c1" + s], [bT])
+            scan(H, g1, T.c1[:, half], T.gs[:, half], OP.max, OP.min, ["c1" + s, "gs" + s], ["g1" + s], [bT])
+            scan(H, T.t1[:, half], T.c1[:, half], T.ts[:, half], OP.max, OP.min, ["c1" + s, "ts" + s], ["t1" + s])
+            scan(H, T.k1[:, half], T.c1[:, half], T.kc[:], OP.max, OP.min, ["c1" + s, "kc"], ["k1" + s])
+            src = {"g": (pT, H, "g1" + s), "t": (T.t1, lo, "t1" + s), "k": (T.k1, lo, "k1" + s)}
+            for n in (2, 3, 4):
+                m = L >> n
+                c_, co, cn = T["c%d" % n], m * h, "c%d%s" % (n, s)
+                (gb, go, gn), (tb, to, tn) = src["g"], src["t"]
+                pa_, pb_, bk = T.pa[:, 16 * h:16 * h + m // 2], T.pb[:, 64 * h:64 * h + m // 2], []
+                if n == 2:
+                    pa_, bk = pT[:, L:L + m // 2], [bT]
+                tt(m // 2, pa_, gb[:, go + 3:go + 2 * m:4], tb[:, to + 1:to + 2 * m:4], OP.mult, [gn, tn], ["pa" + s], bk)
+                tt(m // 2, pb_, gb[:, go + 1:go + 2 * m:4], tb[:, to + 3:to + 2 * m:4], OP.mult, [gn, tn], ["pb" + s], bk)
+                tt(m // 2, c_[:, co + 1:co + m:2], pa_, pb_, OP.is_gt, ["pa" + s, "pb" + s], [cn], bk)
+                dst = {"g": (T.g3, 32 * h), "t": (T.t3, 32 * h), "k": (T["k%d" % n], m * h)}
+                if n == 2:
+                    dst.update(g=(sm, lo + 64), t=(sm, lo))
+                if n == 4:
+                    dst.update(g=(T.sv, 48 * h + 16), t=(T.sv, 48 * h))
+                for x in "gtk":
+                    (sb, so, sn), (db, do_) = src[x], dst[x]
+                    tok = "%s%d%s" % (x, n, s) + ("r%d" % t if n == 2 and x != "k" else "")
+                    scan(m, db[:, do_:do_ + m], c_[:, co:co + m], sb[:, so + 1:so + 2 * m:2], OP.max, OP.min, [cn, sn], [tok],
+                         bk if x == "g" else [])
+                    src[x] = (db, do_, tok)
+                if n == 2:
+                    swap(t, lm[:, half], sm[:, half], [src["g"][2], src["t"][2]], "lm%d%s" % (t, s), "av%d%d" % (h, t), CFG["late"][h])
+            k4 = T.k4[:, 16 * h + 1:16 * h + 16:2]
+            o = 32 * h
+            act(H, T.rp[:, half], T.sv[:, 48 * h:48 * h + 40].indirect(rep8), AF.Identity, ["g4" + s, "t4" + s, "rep8g", "rep8t"],
+                ["rp" + s], r=gat)
+            ts(8, T.offy[:, 8 * h:8 * h + 8], k4, 4096.0, None, OP.mult, None, ["k4" + s], ["offy" + s])
+            tt(8, T.sd[:, 64 * h:64 * h + 64:8], k4, T.kj[:], OP.subtract, ["k4" + s, "kj"], ["sdj" + s])
+            x0 = 192 + 64 * h
+            if last:
+                ts(64, T.sd[:, x0:x0 + 64], ib, -16 * S19, qc["xl"], OP.mult, OP.add, ["ib", "qcxl"], ["sdx" + s])
+                for hf in range(2):
+                    act(4, T.sd[:, x0 + 32 * hf:x0 + 32 * hf + 32:8], T.rf[:, 8 * h + 4 * hf:8 * h + 4 * hf + 4], AF.Identity, ["rf"],
+                        ["sdx" + s], scale=-S19, bias=(TOP + W // 2 * h + YH * hf) * S19)
+            else:
+                tt(8, T.sa[:, 64 * h:64 * h + 64:8], k4, T.kb[:], OP.subtract, ["k4" + s, "kb"], ["sa" + s])
+                act(8, T.sd[:, x0:x0 + 64:8], T.rf[:, 8 * h:8 * h + 8], AF.Identity, ["rf"], ["sdx" + s], scale=-S19, bias=TOP * S19)
+            yt = "yh%d%s" % (t, s)
+            act(H, yh[:, half], T.pm[:, 16 * lo:16 * (lo + H)].indirect(T.offy[:, 8 * h:8 * h + 8]), AF.Identity,
+                qs(lo, lo + H, "pm") + ["offy" + s], [yt], scale=0.5, r=gat)
+            swap(t, ly[:, half], yh[:, half], [yt], "ly%d%s" % (t, s), "ay%d%d" % (h, t), CFG["late"][2 + h])
+            lead[0] = 0.0
+            mm(H, bZ, pZ[:, H:L], (T.idmh if last else T.idh)[:], T.old[:, half], True, False, ["idh", "idmh", "old"], ["R%d" % h, "zp%d" % h])
+            mm(H, bZ, pZ[:, H:L], T.id1[:], yh[:, half], False, True, ["id1", yt], ["R%d" % h])
+            act(H, T.rec[:, half], pZ[:, H:L], AF.Identity, ["R%d" % h], ["rec" + s], [bZ], bias=LIFT - 0.25)
+            act(H, T.zq[:, half], T.z[:, half].indirect(colu), AF.Identity, ["z%d" % h, "colu"], ["zq" + s],
+                bias=LIFT - 0.25, scale=0.5, r=gat)
+            mm(H, bZ, pZ[:, 0:H], T.idm2[:], yh[:, half], True, False, ["idm2", yt], ["D%d" % h, "zp%d" % h])
+            for c in range(8):
+                mm(16, bZ, pZ[:, 16 * c:16 * c + 16], T.id1[:], T.z[:, lo + c:lo + H:8], False, c == 7, ["id1", "z%d" % h], ["D%d" % h])
+            act(H, T.zd_[:, half], pZ[:, 0:H], AF.Abs, ["D%d" % h], ["zd" + s], [bZ])
+            act(H, T.zz[:, L * h + H:L * h + L], T.zd_[:, half], AF.Identity, ["zd" + s], ["zw" + s], bias=LIFT)
+            if last:
+                dl, yv, of = (T.d1, T.ya, T.offr) if h == 0 else (T.d16, T.yb, T.offh)
+                ts(H, dl[:], T.rec[:, half], -LIFT, 16.0 if h else 1.0, OP.add, OP.mult, ["rec" + s], ["dl" + s], r=0.5)
+                for hf in range(2):
+                    tt(64, yv[:, 64 * hf:64 * hf + 64], T.Y[:, (YW - YH) * hf:YW * (hf + 1)].indirect(of[:, 4 * hf:4 * hf + 4]),
+                       dl[:, 64 * hf:64 * hf + 64], OP.add, ys[0] + ys[hf] + ["offr", "offh", "dl" + s], ["yv%d%s" % (hf, s)], r=gat)
+            c5, so = T.c5[:, 64 * h:64 * h + 64], 192 * h
+            tt(H, T.qq[:, half], T.rp[:, half], lm[:, half], OP.mult, ["rp" + s, "lm%d%s" % (t, s)], ["qq" + s])
+            tt(64, c5, T.qq[:, lo:lo + 64], T.qq[:, lo + 64:lo + H], OP.is_ge if rank < (rank ^ STEPS[t]) else OP.is_gt,
+               ["qq" + s], ["c5" + s])
             if not last:
-                mm(T.pD[:, 0:16], T.c4096[:], T.wd[:, 0:16], True, True, ["c4096", "wd"], ["D"], ["pD"])
-                act(T.aj[:], T.pD[:, 0:16], AF.Identity, ["D"], ["acol"], ["pD"], bias=-DROP / 16, scale=32.0,
-                    acc=T.acol[:, 0:1])
-
-        def offsets():
-            ts(T.off[:], T.oo[:], 2.0 ** 20, None, OP.mult, None, ["oo"], ["off"])
-            act(nxt, tw[t][:].indirect(T.off[:, 0:16]), AF.Identity, ["off"] + shifted(t), ["j%d" % (t + 1)])
-
-        meet = [lambda: tt(T.qq[:], sv[:, 33:96:2], lv[:, 1::2], OP.mult, ["g4", "t4b", "lv"], ["qq"]),
-                lambda: tt(T.win[:], T.qq[:, 0:16], T.qq[:, 16:32], OP.is_ge if rank < (rank ^ STEPS[t]) else OP.is_gt,
-                           ["qq"], ["win"]),
-                deltas,
-                lambda: tt(T.oo[:], T.wd[:], T.ol[:], OP.add, ["wd", "ol0", "ol16", "ol32"], ["oo"]),
-                offsets]
-        if not last:
-            scat, lo = [], 0
-            for n in CFG["scat"]:
-                scat.append(lambda lo=lo, n=n: tt(T.X[:, 0:W + L].indirect(T.off[:, 32 + lo // 16:32 + (lo + n) // 16]),
-                                                  T.rec[:, lo:lo + n], T.neg[:, 0:n], OP.add, ["off", "rec", "neg", "Xd"], xall))
-                lo += n
-            lose = [lambda: tt(T.zl[:, 0:FA], ly[:, 0:FA], T.bw[:, 0:FA], OP.add, ["lya", "zq"], qs(0, FA, "zl")),
-                    lambda: ts(T.zz[:, 0:FA], T.zl[:, 0:FA], -LIFT, 1.0, OP.add, OP.max, qs(0, FA, "zl"), ["zzl"])]
-            lose += picks(0, FA, "pU", T.zz[:, 0:FA], ["zzl"], T.hw[:, 0:FA], ["hl"])
-            pick = [lambda: ts(T.hd[:, 0:FA], T.hw[:].indirect(T.off[:, 16:16 + n4]), T.acol[:, 0:1], DROP, OP.add, OP.add,
-                               ["hl", "hw", "off", "acol"], ["hd0"])] + finish(0, FA)
-            for x in CFG["meet"].replace(" ", ""):
-                {"M": meet, "l": lose, "S": scat, "P": pick}[x].pop(0)()
-            lists(t + 1, [])
-            forms(tw[t + 1][:, FA:L], ["j%d" % (t + 1), "acol"], FA, L, T.acol[:, 0:1])
-            act(T.base[:, FA:L], T.bw[:].indirect(T.off[:, 16 + n4:32]), AF.Identity, ["zq", "off"] + qs(0, L, "zw"), ["base"])
-            act(T.z[:, 0:FA], T.zz[:].indirect(T.off[:, 16:16 + n4]), AF.Identity, ["zzl", "zzw", "off"], qs(0, FA, "z"))
-        else:
-            weave(meet)
-            act(T.base[:], T.bw[:].indirect(T.off[:, 16:32]), AF.Identity, ["zq", "off"] + qs(0, L, "zw"), ["base"])
-            znew = newz(t, 0, L)
-            for hf in range(2):
-                yw, c = T.Y[:, hf * YW:hf * YW + YW], 64 * hf
-                lo, hi = T.off[:, 32 + 4 * hf:36 + 4 * hf], T.off[:, 40 + 4 * hf:44 + 4 * hf]
-                cp(yw.indirect(lo), T.ya[:, c:c + 64], ["off", "ya%d" % hf], ys[hf])
-                tt(T.yb[:, c:c + 64], yw.indirect(hi), T.d16[:, c:c + 64], OP.add, ys[hf] + ["off", "d16"], ["yb%d" % hf])
-                cp(yw.indirect(hi), T.yb[:, c:c + 64], ["off", "yb%d" % hf], ys[hf])
-                dma("s", T.yx[:, hf * YH:hf * YH + YH], T.Y[:, hf * YW:hf * YW + YH], ys[hf], ["yx%d" % hf], "outx")
-            dma("a", T.yj[:], T.jfin[:], ["j4"], ["yj"], "outj")
-            weave(znew)
-    dma("a", T.yz[:], T.z[:], zall, ["yz"], "outz")
-    add("s", None, ["yj", "yx0", "yx1", "yz"])
-    emit(g, T, ops)
+                scan(64, T.sb[:, 64 * h:64 * h + 64], c5, T.sa[:, 64 * h:64 * h + 64], OP.min, OP.max, ["c5" + s, "sa" + s], ["sb" + s])
+                for c in range(8):
+                    mm(1, "pG0", T.pG0[:, L + h:L + h + 1], T.c17[:], T.sb[:, 64 * h + 8 * c + 7:64 * h + 8 * c + 8], c == 0, c == 7,
+                       ["c17", "sb" + s], ["asum" + s])
+            for i, (x, d0) in enumerate((("j" + s, 64 * h), ("z", 128), ("x" + s, x0))):
+                scan(64, T.se[:, so + 64 * i:so + 64 * i + 64], c5, T.sd[:, d0:d0 + 64], OP.min, OP.max, ["c5" + s, "sd" + x],
+                     ["se%d%s" % (i, s)])
+            ts(16, T.off[:, o:o + 16], T.se[:, so + 7:so + 128:8], 1 / S19, None, OP.mult, None, ["se0" + s, "se1" + s], ["off" + s])
+            ts(8, T.off[:, o + 16:o + 24], T.se[:, so + 135:so + 192:8], -1 / S19, float(TOP), OP.mult, OP.add, ["se2" + s], ["offx" + s])
+            offz = T.off[:, o + 8:o + 16]
+            act(H, T.jfin[:, half] if last else tw[t + 1][:, slab(t + 1, h, 0, 1)], tw[t][:, slab(t, h, 0, SLABS)].indirect(T.off[:, o:o + 8]),
+                AF.Identity, ["off" + s] + shifted(t, h), ["j%d%s" % (t + 1, s)], r=gat)
+            if not last:
+                lists(t + 1, h, [])
+            tt(H, T.zz[:, L * h:L * h + H], ly[:, half], T.zq[:, half], OP.add, ["ly%d%s" % (t, s), "zq" + s], ["zl" + s])
+            ts(H, T.z[:, half], T.zz[:, L * h:L * h + L].indirect(offz), -LIFT, 1.0, OP.add, OP.max, ["zl" + s, "zw" + s, "off" + s],
+               ["z%d" % h], r=gat)
+            if not last:
+                n = CFG["scat"]
+                for c0 in range(0, H, n):
+                    tt(n, T.X[:, 0:W + L].indirect(T.off[:, o + 16 + c0 // 16:o + 16 + (c0 + n) // 16]), T.rec[:, lo + c0:lo + c0 + n],
+                       T.neg[:, 0:n], OP.add, ["offx" + s, "rec" + s, "neg", "Xd"], xall, r=sca)
+                if h == 0:
+                    picks(t + 1, 0, -DROP, [], H, True)
+                else:
+                    for c0 in (0, 64):
+                        ts(64, T.hd[:, c0:c0 + 64], T.hf[:, c0:c0 + 64], T.pG0[:, L:L + 1], T.pG0[:, L + 1:L + 2], OP.add, OP.add,
+                           qs(c0, c0 + 64, "hf") + ["asum.0", "asum.1"], qs(c0, c0 + 64, "hd"), ["pG0"])
+                        finish(c0, c0 + 64)
+                    act(2, T.aj[:, 0:2], T.pG0[:, L:L + 2], AF.Identity, ["asum.0", "asum.1", "hd4"], ["acol"], ["pG0"], bias=-DROP / 2,
+                        acc=T.acol[:, 0:1])
+                    picks(t + 1, 1, T.acol[:, 0:1], ["acol"], H, False)
+            else:
+                for hf in range(2):
+                    cp(64, T.Y[:, hf * YW:hf * YW + YW].indirect(T.off[:, o + 16 + 4 * hf:o + 20 + 4 * hf]), yv[:, 64 * hf:64 * hf + 64],
+                       ["offx" + s, "yv%d%s" % (hf, s)], ys[hf], r=sca)
+                    if h:
+                        dma("s", T.yx[:, hf * YH:hf * YH + YH], T.Y[:, hf * YW:hf * YW + YH], ys[hf], ["yx%d" % hf], "outx", 0.7)
+        if last:
+            dma("a", T.yj[:], T.jfin[:], names(4), ["yj"], "outj")
+            dma("a", T.yz[:], T.z[:], zall, ["yz"], "outz")
+    add("s", None, ["yj", "yx0", "yx1", "yz"], ["sq"])
+    emit(g, T, arrange(ops))
     g.wait_ge(T.sem.sent, sent[0])

@@ -15,29 +15,36 @@ TOP = 16384
 LIFT = 192.0
 DROP = 32.0 * 5 * W
 
-PIECES = ((0, 64), (64, 128), (128, 192), (192, 224), (224, 256))
-CFG = {"run": 32, "scat": 64, "vpack": 2, "lead": 0.0, "late": (0.5, 0.4, 0.1, 0.2),
-       "cyc": 0.00087, "pe": 0.00044, "wake": 0.2, "gat": 1.56, "sca": 3.8, "dma": 2.2, "far": 3.2, "passes": 2, "look": 0.1, "fit": 0.03}
+CFG = {"cuts": (0, 16, 64, 80, 128, 192, 224, 256),
+       "vg": (0, 64), "mod": "av", "parts0": 128,
+       "run": 16, "scat": 64, "vpack": 2, "lead": (0.0, 0.0), "late": (0.3, 0.3, 0.1, 0.1), "early": (2, 2), "parts": 64, "hold": True,
+       "cyc": 0.00083, "pe": 0.00042, "wake": 0.2, "gat": 1.56, "sca": 3.8, "dma": 2.2, "far": 3.3, "passes": 2, "look": 0.1, "fit": 0.03}
 TURN_Q = ((32, 2), (2, 0), (16, 3), (1, 0))
 TURN_C = (((4, 8),), ((1, 2), (32, 4)), ((2, 8),), ((16, 8),))
+
+SENT = [16 >> e for e in CFG["early"]]
+PW = 8 * 17
 
 F, B, I, U = "float32", "bfloat16", "int32", "uint16"
 SCRATCH = {}
 for _names, _n, _d in (
         ("X", W + L, B), ("Y", 2 * YW, B), ("xg mn pm", 16 * L, B), ("mask", 1024, B), ("jin ha hb hd he", L, I), ("hu", L, U),
-        ("zin z old rec zd_", L, B), ("ones neg blkm w2 id1 id16 idm2 idh idmh c19 c17 sb d1 d16 ya yb", H, B), ("bm band wband", 144, B),
-        ("bandv", 144, F), ("blkv kv kc hf c2 k2 pb c5 sa", H, F), ("hc zq jfin gs ts c1 t1 k1 qq rp lt", L, F), ("zz", 2 * L, B),
-        ("sd", 320, F), ("se", 384, F), ("sv", 96, F), ("c3 g3 t3 k3 l32 pa", 64, F), ("c4 k4", 32, F), ("q1 rf aj", 16, F),
-        ("w acol kb kj col", 8, F), ("pi", 8, I), ("ti rc", 16, I), ("offr offy", 16, U), ("offh", 8, U), ("off lists", 64, U)):
+        ("zin z old rec zd_", L, B), ("ones neg blkm w2 id1 id16 idm2 idh idmh idk ids c19 c17 d1 d16 ya yb", H, B), ("bm band wband", 144, B),
+        ("jj hf rp", 2 * L, F), ("mq k3i c1", L, B), ("kvs", 64, B), ("bandv", 144, F), ("blkv kv c2 g2 t2 k2 pb lt", H, F),
+        ("hc zq jfin gs ts g1 t1", L, F), ("zz", 2 * L, B),
+        ("sd se", 6 * PW, F), ("ia", 4 * PW, F), ("sa c5", 2 * PW, F), ("sb", 2 * PW, B), ("c3 g3 t3 k3 l32 pa sv", 64, F), ("c4 k4", 32, F), ("q1", 24, F), ("rf", 16, F),
+        ("w kb kj", 8, F), ("drop", 8, B), ("pi", 8, I), ("ti rc", 16, I), ("offr offy", 16, U), ("offh", 8, U), ("off lists", 64, U)):
     for _x in _names.split():
         SCRATCH[_x] = ("sbuf", [128, _n], _d)
+for _h in range(2):
+    SCRATCH["qq%d" % _h] = ("sbuf", [128, 16, SENT[_h] + 1], F)
 for _x in ("pT0", "pT1", "pG0", "pG1", "pZ0", "pZ1", "pU", "pP"):
     SCRATCH[_x] = ("psum", [128, 512], F)
 SEMAPHORES = ["v", "a", "p", "g", "ldz", "ldw", "ldj", "ldx", "ldx2", "sent", "outj", "outz", "outx"]
 for _t in range(ROUNDS):
     SCRATCH["tw%d" % _t] = ("sbuf", [128, SLABS * L], F)
-    SCRATCH["sm%d" % _t] = ("sbuf", [128, L], F)
-    SCRATCH["lm%d" % _t] = ("sbuf", [128, L], F)
+    SCRATCH["sm%d" % _t] = ("sbuf", [128, 2 * L], F)
+    SCRATCH["lm%d" % _t] = ("sbuf", [128, 2 * L], F)
     SCRATCH["yh%d" % _t] = ("sbuf", [128, L], B)
     SCRATCH["ly%d" % _t] = ("sbuf", [128, L], B)
     SCRATCH["do%d" % _t] = ("dram", [16, 16 * H], F)
@@ -76,6 +83,12 @@ def arrange(ops):
     chain = [0.0] * n
     for i in reversed(range(n)):
         chain[i] = max([gap(i, k) + chain[k] for k in succs[i]] + [sum(ops[i][7])])
+    if "log" in CFG:
+        i, path = max(range(n), key=lambda k: chain[k]), []
+        while succs[i]:
+            path.append((round(chain[i], 2), ops[i][0], ops[i][3][:1]))
+            i = max(succs[i], key=lambda k: gap(i, k) + chain[k])
+        CFG["log"].append(path)
     chain = [c + op[8] for c, op in zip(chain, ops)]
 
     def place(rank, back):
@@ -274,7 +287,7 @@ def rank_program(g, core, T, topo):
         peer = T.cores[rank ^ STEPS[t]]
         rid, pid, _ = topo.addr(peer)
         add("g", lambda: g.remote_dma(out, in_, T.sem[sem], T.sem.sent, pid, rid, topo.mask(core, peer)), rd, ["went" + sem], (), "",
-            cost=(0.3, 0.0))
+            cost=(0.3 if sent[0] else 1.3, 0.0))
         sent[0] += len(topo.engines(core, peer))
         add(None, None, ["went" + sem], [tok], ext=(sem, len(topo.engines(peer, core))), cost=(0.0, CFG["far"] - 0.3 + late))
 
@@ -282,7 +295,10 @@ def rank_program(g, core, T, topo):
         return ["%s%d" % (name, q) for q in range(lo // 16, hi // 16)]
 
     tw = [T["tw%d" % t] for t in range(ROUNDS)]
-    zall, xall = ["z0", "z1"], ["X", "X2"]
+    zall, xall = ["z0", "z1", "z2", "z3"], ["X", "X2"]
+
+    def zs(lo, hi):
+        return zall[lo // 64:min(hi, L) // 64]
 
     def names(t):
         return ["j%d.0" % t, "j%d.1" % t]
@@ -298,17 +314,23 @@ def rank_program(g, core, T, topo):
         dma("s", dr[rows, :], w_[:, slab(t, h, 16, 17)], ["jr" + s], ["dr" + s], "sr" + sem)
         for k in range(15):
             dma("s", w_[k::16, slab(t, h, 1, 16 - k)], do[rows, (k + 1) * H:16 * H], ["do" + s], ["to%s.%d" % (s, k)], "tp" + sem)
+        if h == 0:
+            rival(t, h, [])
+
+    def rival(t, h, after):
+        s, rows = "%d.%d" % (t, h), slice(8 * h, 8 * h + 8)
         for k in range(1, 16):
-            dma("s", w_[k::16, slab(t, h, 16 - k, 16)], dr[rows, 0:k * H], ["dr" + s], ["tr%s.%d" % (s, k)], "tp" + sem)
+            dma("s", tw[t][k::16, slab(t, h, 16 - k, 16)], T["dr%d" % t][rows, 0:k * H], ["dr" + s] + after, ["tr%s.%d" % (s, k)],
+                "tp%d%d" % (h, t))
 
     def shifted(t, h):
         s = "%d.%d" % (t, h)
         return ["j" + s, "jr" + s] + ["to%s.%d" % (s, k) for k in range(15)] + ["tr%s.%d" % (s, k) for k in range(1, 16)]
 
-    dma("s", T.zin[:], T.zd[:], [], ["zin"], "ldz", 0.5)
-    dma("a", T.X[:, 0:W // 2], T.xt[:, 0:W // 2], [], ["X"], "ldx", 1.0)
-    dma("s", T.w[:, 0:1], T.wt[:], [], ["w"], "ldw", 0.5)
-    dma("s", T.jin[:], T.jn[:], [], ["jin"], "ldj", 0.5)
+    dma("s", T.zin[:], T.zd[:], [], ["zin"], "ldz", 0.01)
+    dma("a", T.jin[:], T.jn[:], [], ["jin"], "ldj", 0.01)
+    dma("s", T.w[:, 0:1], T.wt[:], [], ["w"], "ldw", 0.01)
+    dma("s", T.X[:, 0:W // 2], T.xt[:, 0:W // 2], [], ["X"], "ldx", 1.3)
     dma("s", T.X[:, W // 2:W], T.xt[:, W // 2:W], [], ["X2"], "ldx2", 2.5)
     iota(T.pi[:, 0:1], [[0, 1]], 0, 1, ["pi"], False)
     iota(T.blkv[:], [[16, 8], [0, 16]], 0, -1, ["blkv"])
@@ -317,25 +339,22 @@ def rank_program(g, core, T, topo):
     for t, pat in enumerate(TURN_C):
         iota(T.lt[:, 16 * t:16 * t + 16], [[32 * H, 2]] + [[32 * s, n] for s, n in pat], 0, 0, ["lt%d" % t])
     iota(T.lt[:, 64:80], [[H, 2], [1, 4], [64, 2]], 0, 0, ["lt4"])
-    iota(T.lt[:, 80:88], [[-16, 2], [4, 4]], 17, 0, ["lt5"])
-    iota(T.lt[:, 128:192], [[1, 8], [0, 8]], 0, 0, ["ia"])
-    iota(T.lt[:, 192:256], [[0, 2], [1, 4], [0, 8]], 0, 0, ["ib"])
-    q1, q128, q4, q22, qm, qe, w = [T.q1[:, i:i + 1] for i in (0, 1, 2, 3, 8, 9)] + [T.w[:, 0:1]]
-    firstu, colu, rep8 = T.lists[:, 0:16], T.lists[:, 16:24], T.lists[:, 24:32]
-    ia, ib = T.lt[:, 128:192], T.lt[:, 192:256]
+    q1, q128, q4, w = [T.q1[:, i:i + 1] for i in (0, 1, 2)] + [T.w[:, 0:1]]
+    firstu, colu = T.lists[:, 0:16], T.lists[:, 16:24]
+
+    def slots(buf, h, i, at=None, c0=0, c1=8, parts=3):
+        n, o = SENT[h] + 1, PW * (buf.shape[1] // (2 * PW) * h) + 8 * (SENT[h] + 1) * i
+        return buf[:, o:o + 8 * n] if at is None else buf[:, o + n * c0 + at:o + n * c1:n]
+
     ts(1, T.pi[:, 1:2], T.pi[:, 0:1], 15, None, OP.bitwise_and, None, ["pi"], ["qi"])
     ts(1, T.pi[:, 2:3], T.pi[:, 0:1], 2, 3, OP.arith_shift_right, OP.bitwise_and, ["pi"], ["qi2"])
     ts(1, T.pi[:, 3:4], T.pi[:, 0:1], 3, 1, OP.arith_shift_right, OP.bitwise_and, ["pi"], ["qi3"])
-    ts(1, T.pi[:, 4:5], T.pi[:, 0:1], 7, None, OP.bitwise_and, None, ["pi"], ["qi7"])
     cp(1, q1, T.pi[:, 1:2], ["qi"], ["q1"])
     for ap, c, tok in ((q4, 4.0, "q4"), (q128, 128.0, "q128")):
         ts(1, ap, T.pi[:, 1:2], c, None, OP.mult, None, ["qi"], [tok])
-    ts(1, q22, T.pi[:, 3:4], 2.0, None, OP.mult, None, ["qi3"], ["q22"])
-    ts(1, qm, T.pi[:, 4:5], 0.0, None, OP.not_equal, None, ["qi7"], ["qm"])
-    ts(1, qe, T.pi[:, 4:5], 0.0, 32.0, OP.is_equal, OP.mult, ["qi7"], ["qe"])
     qc = {}
-    for i, (x, m, c) in enumerate((("j", 8, 0), ("z", 1, 0), ("zw", 1, H), ("x0", -1, TOP - W), ("x1", -1, TOP - W - H),
-                                   ("xl", -1, TOP - YH))):
+    for i, (x, m, c) in enumerate((("j", 8, 0), ("z", 1, 0), ("zw", 1, 64), ("x0", -1, TOP - W), ("x1", -1, TOP - W - H),
+                                   ("xl", -1, TOP - YH), ("k", -8, -128))):
         qc[x] = T.q1[:, 10 + i:11 + i]
         ts(1, qc[x], T.pi[:, 1:2], m * S19, c * S19, OP.mult, OP.add, ["qi"], ["qc" + x])
     for t, (m, sh) in enumerate(TURN_Q):
@@ -345,32 +364,40 @@ def rank_program(g, core, T, topo):
             ts(1, qa, T.pi[:, sh:sh + 1], -32.0 * 127, qa, OP.mult, OP.add, ["qi%d" % sh, "qa%d" % t], ["qa%d" % t])
         ts(16, T.l32[:, 16 * t:16 * t + 16], T.lt[:, 16 * t:16 * t + 16], qa, None, OP.add, None, ["lt%d" % t, "qa%d" % t], ["l32.%d" % t])
     ts(16, firstu, T.lt[:, 64:80], q4, None, OP.add, None, ["lt4", "q4"], ["firstu"])
-    ts(4, T.lt[:, 88:92], T.lt[:, 80:84], q22, None, OP.add, None, ["lt5", "q22"], ["lt6"])
-    ts(4, T.lists[:, 24:28], T.lt[:, 88:92], qm, qe, OP.mult, OP.add, ["lt6", "qm", "qe"], ["rep8g"])
-    ts(4, T.lists[:, 28:32], T.lt[:, 84:88], q22, None, OP.add, None, ["lt5", "q22"], ["rep8t"])
     ts(H, T.blkm[:], T.blkv[:], q1, 0.0, OP.add, OP.is_equal, ["blkv", "q1"], ["blkm"])
     ts(H, T.id1[:], T.bandv[:, 0:128], 0.0, None, OP.is_equal, None, ["bandv"], ["id1"])
     ts(144, T.bm[:], T.bandv[:], q1, 15.0, OP.add, OP.is_equal, ["bandv", "q1"], ["bm"])
     act(144, T.band[:], T.bm[:], AF.Identity, ["bm"], ["band"], scale=S12)
-    for name, c in (("id16", 16.0), ("idm2", -2.0), ("idh", 0.5), ("idmh", -0.5)):
+    ms(L, T.k3i[:], 0.0, ["k3i"])
+    ms(H, T.k3i[:, 1::2], 2048 * LIFT * S12 / 32 / 128, ["k3i"])
+    for name, c in (("idk", -2048.0), ("ids", S12), ("id16", 16.0), ("idm2", -2.0), ("idh", 0.5), ("idmh", -0.5)):
         act(H, T[name][:], T.id1[:], AF.Identity, ["id1"], [name], scale=c)
-    ts(H, T.kc[:], T.kv[:], q128, S12, OP.add, OP.mult, ["kv", "q128"], ["kc"])
-    ts(8, T.col[:], T.kv[:, 0::16], q128, 1.0 / 16, OP.add, OP.mult, ["kv", "q128"], ["col"])
-    ts(8, T.kb[:], T.kc[:, 0::16], -S12, None, OP.add, None, ["kc"], ["kb"])
-    ts(8, T.kj[:], T.kc[:, 0::16], 1 - S19 / (16 * S12), -S12, OP.mult, OP.add, ["kc"], ["kj"])
-    cp(8, colu, T.col[:], ["col"], ["colu"])
+    act(64, T.kvs[:], T.kv[:, 0::2], AF.Identity, ["kv"], ["kvs"], scale=S12)
+    ts(8, colu, T.kv[:, 0::16], q128, 1.0 / 16, OP.add, OP.mult, ["kv", "q128"], ["colu"])
+    ts(8, T.kb[:], T.kv[:, 0::16], -1.0, S12, OP.add, OP.mult, ["kv"], ["kb"])
+    ts(8, T.kj[:], T.kv[:, 0::16], S12 - S19 / 16, qc["k"], OP.mult, OP.add, ["kv", "qck"], ["kj"])
     ms(H, T.c19[:], 2.0 ** -19, ["c19"])
     ms(H, T.c17[:], 32 / S12, ["c17"])
-    ms(H, T.sa[:], 0.0, ["sa.0", "sa.1"])
-    ms(96, T.sv[:], -1.0, ["g4.0", "t4.0", "g4.1", "t4.1"])
+    ms(8, T.drop[:], -DROP * S12 / 32 / 128, ["drop"])
+    ms(2 * PW, T.sa[:], 0.0, ["sa.0", "sa.1"])
     run = CFG["run"]
     ms(16 * run, T.mask[:, 0:16 * run], 1.0, ["mask"])
     ms(run, T.mask[:, 0:16 * run:16], 0.0, ["mask"])
-    ts(64, T.sd[:, 128:192], ia, 16 * S19, qc["z"], OP.mult, OP.add, ["ia", "qcz"], ["sdz"])
-    ts(8, T.sd[:, 128:192:8], T.lt[:, 128:192:8], 16 * S19, qc["zw"], OP.mult, OP.add, ["ia", "qczw"], ["sdz"])
     for h in range(2):
-        ts(64, T.sd[:, 64 * h:64 * h + 64], ia, S19, qc["j"], OP.mult, OP.add, ["ia", "qcj"], ["sdj.%d" % h])
-        ts(64, T.sd[:, 192 + 64 * h:256 + 64 * h], ia, -16 * S19, qc["x%d" % h], OP.mult, OP.add, ["ia", "qcx%d" % h], ["sdx.%d" % h])
+        n, s = SENT[h], ".%d" % h
+        iota(slots(T.ia, h, 0), [[1, 8], [0, n + 1]], 0, 0, ["ia" + s])
+        iota(slots(T.ia, h, 1), [[0, 2], [1, 4], [0, n + 1]], 0, 0, ["ib" + s])
+        iota(T.lt[:, 80 + 16 * h:80 + 16 * h + n], [[-16, 2], [32 // n, n // 2]], 17, 0, ["lt5" + s])
+        ts(1, T.pi[:, 4 + h:5 + h], T.pi[:, 1:2], 4 - CFG["early"][h], None, OP.arith_shift_right, None, ["qi"], ["qn" + s])
+        ts(1, T.q1[:, 8 + h:9 + h], T.pi[:, 4 + h:5 + h], 2.0, None, OP.mult, None, ["qn" + s], ["q2n" + s])
+        ts(n, T.lists[:, 32 + 16 * h:32 + 16 * h + n], T.lt[:, 80 + 16 * h:80 + 16 * h + n], T.q1[:, 8 + h:9 + h], None, OP.add, None,
+           ["lt5" + s, "q2n" + s], ["rep" + s])
+        for i, (x, m) in enumerate((("j", 1), ("z", 16), ("x%d" % h, -16))):
+            ts(8 * n, slots(T.sd, h, i), slots(T.ia, h, i % 2), m * S19, qc[x], OP.mult, OP.add, ["ia" + s, "ib" + s, "qc" + x],
+               ["sd%d%s" % (i, s)])
+        ts(8, slots(T.sd, h, 1, 0), slots(T.ia, h, 1, 0), 16 * S19, qc["zw"], OP.mult, OP.add, ["ib" + s, "qczw"], ["sd1" + s])
+        ms(8, T["qq%d" % h][:, 0:8, 0], -1.0, ["qq" + s])
+        ms(8, T["qq%d" % h][:, 8:16, 0], 0.0, ["qq" + s])
     ts(H, T.w2[:], T.blkm[:], w, 2.0, OP.mult, OP.mult, ["blkm", "w"], ["w2"], r=0.5)
     ts(144, T.wband[:], T.bm[:], w, None, OP.mult, None, ["bm", "w"], ["wband"], r=0.5)
     act(L, T.z[:], T.zin[:].indirect(firstu), AF.Identity, ["zin", "firstu"], zall, r=gat)
@@ -392,20 +419,46 @@ def rank_program(g, core, T, topo):
     def picks(t, h, bias, rd, parts, later):
         lo, s = H * h, ".%d" % h
         bJ, bU = ("pP", "pT1")[h], ("pU", "pG1")[h]
-        act(H, T[bJ][:, H:L], tw[t][:, slab(t, h, 0, 1)], AF.Identity, ["j%d%s" % (t, s)], ["pJ" + s] + ["g1.1"] * h, [bJ])
-        act(H, T[bJ][:, L:L + H], tw[t][:, slab(t, h, 0, 1)], AF.Identity, ["j%d%s" % (t, s)] + rd, ["pJA" + s] + ["pa.1"] * h, [bJ],
-            bias=bias, scale=32.0)
-        mm(H, bU, T[bU][:, lo:lo + H], T.w2[:], T.z[:, lo:lo + H], True, True, ["w2", "z%d" % h], ["u" + s])
+        jt, j0 = "j%d%s" % (t, s), slab(t, h, 0, 1).start
+        if CFG["mod"][h] == "a":
+            act(H, T.jj[:, 2 * lo:2 * lo + L:2], tw[t][:, j0:j0 + H], AF.Identity, [jt], ["ja" + s])
+            act(H, T.jj[:, 2 * lo + 1:2 * lo + L:2], tw[t][:, j0:j0 + H], AF.Identity, [jt], ["jb" + s], bias=-DROP, scale=33.0)
+            for c0 in range(lo, lo + H, parts):
+                c1, o, v0 = c0 + parts, c0 - lo, L + 2 * (c0 - lo)
+                bu, vt = bU if o == 0 else ("pZ1", "pU")[h], ["v%d" % c0] + ["pa.1"] * h
+                mm(parts, bu, T[bu][:, 384 + o:384 + o + parts], T.w2[:], T.z[:, c0:c1], True, True, ["w2"] + zs(c0, c1), ["u%d" % c0])
+                act(parts, T.mq[:, c0:c1], T[bu][:, 384 + o:384 + o + parts], AF.Identity, ["u%d" % c0], qs(c0, c1, "mq"), [bu],
+                    bias=LIFT - 0.5 + 2.0 ** -11, scale=2.0 ** -11)
+                mm(2 * parts, bJ, T[bJ][:, v0:v0 + 2 * parts], T.c17[:], T.k3i[:, 0:2 * parts], True, False, ["c17", "k3i"] + zs(c0, c1), vt)
+                mm(parts, bJ, T[bJ][:, v0 + 1:v0 + 2 * parts:2], T.w2[:], T.z[:, c0:c1], False, False, ["w2"] + zs(c0, c1), vt)
+                mm(parts, bJ, T[bJ][:, v0 + 1:v0 + 2 * parts:2], T.idk[:], T.mq[:, c0:c1], False, True, ["idk"] + qs(c0, c1, "mq"), vt)
+                scan(2 * parts, T.hf[:, 2 * c0:2 * c1], T[bJ][:, v0:v0 + 2 * parts], T.jj[:, 2 * c0:2 * c1], OP.mult, OP.add,
+                     vt + ["ja" + s, "jb" + s], qs(c0, c1, "hf"), [bJ])
+                if not later:
+                    with_a(c0, c1, rd)
+            return
+        if True:
+            ts(H, T.hc[:, lo:lo + H], tw[t][:, j0:j0 + H], 32.0, bias, OP.mult, OP.add, [jt] + rd, qs(lo, lo + H, "hc"),
+               ["pG0"] if rd else [])
         for c0 in range(lo, lo + H, parts):
             c1, o = c0 + parts, c0 - lo
-            ts(parts, T.ha[:, c0:c1], T[bU][:, c0:c1], 1.0, None, OP.add, None, ["u" + s], qs(c0, c1, "ha"), [bU])
+            bu = bU if o == 0 or later else ("pG0", "pU")[h]
+            mm(parts, bu, T[bu][:, H + o:H + o + parts], T.w2[:], T.z[:, c0:c1], True, True, ["w2"] + zs(c0, c1), ["u%d" % c0])
+            ts(parts, T.ha[:, c0:c1], T[bu][:, H + o:H + o + parts], 1.0, None, OP.add, None, ["u%d" % c0], qs(c0, c1, "ha"), [bu])
             ts(parts, T.hb[:, c0:c1], T.ha[:, c0:c1], 2047, None, OP.bitwise_and, None, qs(c0, c1, "ha"), qs(c0, c1, "hb"))
-            tt(parts, T.hc[:, c0:c1], T.hb[:, c0:c1], T[bJ][:, H + o:H + o + parts], OP.mult, qs(c0, c1, "hb") + ["pJ" + s],
-               qs(c0, c1, "hc"), [bJ])
-            tt(parts, (T.hf if later else T.hd)[:, c0:c1], T.hc[:, c0:c1], T[bJ][:, L + o:L + o + parts], OP.add,
-               qs(c0, c1, "hc") + ["pJA" + s], qs(c0, c1, "hf" if later else "hd"), [bJ])
-            if not later:
-                finish(c0, c1)
+            tt(parts, T[bJ][:, H + o:H + o + parts], T.hb[:, c0:c1], tw[t][:, j0 + o:j0 + o + parts], OP.mult,
+               qs(c0, c1, "hb") + [jt], ["pc%d" % c0], [bJ], r=2)
+            tt(parts, T.hd[:, c0:c1], T[bJ][:, H + o:H + o + parts], T.hc[:, c0:c1], OP.add, qs(c0, c1, "hc") + ["pc%d" % c0],
+               qs(c0, c1, "hd"), [bJ])
+            finish(c0, c1)
+
+    def with_a(c0, c1, rd):
+        if rd:
+            ts(c1 - c0, T.hd[:, c0:c1], T.hf[:, 2 * c0 + 1:2 * c1:2], T.pG0[:, L:L + 1], DROP, OP.add, OP.add, qs(c0, c1, "hf") + rd,
+               qs(c0, c1, "hd"), ["pG0"])
+        else:
+            cp(c1 - c0, T.hd[:, c0:c1], T.hf[:, 2 * c0 + 1:2 * c1:2], qs(c0, c1, "hf"), qs(c0, c1, "hd"))
+        finish(c0, c1)
 
     def finish(c0, c1):
         n = c1 - c0
@@ -419,37 +472,42 @@ def rank_program(g, core, T, topo):
         last = t == ROUNDS - 1
         sm, lm, yh, ly = T["sm%d" % t], T["lm%d" % t], T["yh%d" % t], T["ly%d" % t]
         for h in range(2):
-            for r in range(4):
-                mm(H, "pZ%d" % h, T["pZ%d" % h][:, r::4], T.id1[:], T.z[:, H * h:H * h + H], True, True, ["id1", "z%d" % h],
-                   ["zp%d" % h, "D%d" % h, "R%d" % h])
-        for lo, hi in PIECES:
-            h, n = lo // H, hi - lo
-            act(16 * n, T.xg[:, 16 * lo:16 * hi], T.X[:, 0:W].indirect(T.hu[:, lo:hi]), AF.Identity, xall + qs(lo, hi, "hu"),
-                qs(lo, hi, "x") + ["gq"], r=gat)
-            if lo % H == 0:
-                mm(H, "pT%d" % h, T["pT%d" % h][:, 0:H], T.c19[:], T.ones[:], True, False, ["c19", "ones"] + qs(lo, hi, "x"),
-                   ["tsum%d" % h])
-            for k in range(4):
-                tt(4 * n, T.mn[:, 16 * lo + k:16 * hi:4], T.xg[:, 16 * lo + k:16 * hi:4], T["pZ%d" % h][:, 4 * (lo % H):4 * (lo % H + n)],
-                   OP.min, qs(lo, hi, "x") + ["zp%d" % h], ["m%d.%d" % (lo, k)], ["pZ%d" % h])
-            for kind, src in (("T", T.xg), ("G", T.mn)):
-                bank = "p%s%d" % (kind, h)
-                for j in range(lo // 8, hi // 8):
-                    q = j % 16
-                    mm(H, bank, T[bank][:, 0:H], T.band[:, 15 - q:143 - q], src[:, H * j:H * j + H], kind == "G" and q == 0, q == 15,
-                       ["band"] + (qs(lo, hi, "x") if kind == "T" else ["m%d.%d" % (lo, k) for k in range(4)]),
-                       ["%ssum%d" % (kind.lower(), h)])
-        for lo in range(0, L, run):
-            scan(16 * run, T.pm[:, 16 * lo:16 * (lo + run)], T.mask[:, 0:16 * run], T.xg[:, 16 * lo:16 * (lo + run)], OP.mult, OP.max,
-                 ["mask"] + qs(lo, lo + run, "x"), qs(lo, lo + run, "pm"), r=0.5)
-        for h in range(2):
             for q in range(16):
                 mm(8, "pU", T.pU[:, L + 8 * h:L + 8 * h + 8], T.wband[:, 15 - q:143 - q], T.z[:, H * h + 8 * q:H * h + 8 * q + 8],
-                   q == 0, q == 15, ["wband", "z%d" % h, "hu7"], ["ul"])
+                   q == 0, q == 15, ["wband", "hu7", "ha15", "mq15"] + zs(H * h, H * h + H), ["ul"])
         cp(16, T.ti[:], T.pU[:, L:L + 16], ["ul"], ["ti"], ["pU"])
         ts(16, T.rc[:], T.ti[:], 31, None, OP.bitwise_and, None, ["ti"], ["rc"])
         tt(16, T.rf[:], T.rc[:], T.l32[:, 16 * t:16 * t + 16], OP.add, ["rc", "l32.%d" % t], ["rf"])
         cp(16, T.offr[:], T.rf[:], ["rf"], ["offr"])
+        for h in range(2):
+            for r in range(4):
+                mm(H, "pZ%d" % h, T["pZ%d" % h][:, r::4], T.id1[:], T.z[:, H * h:H * h + H], True, True,
+                   ["id1"] + zs(H * h, H * h + H), ["zp%d" % h, "D%d" % h, "R%d" % h] + ["u64"] * h)
+        for lo, hi in zip(CFG["cuts"], CFG["cuts"][1:]):
+            h, n = lo // H, hi - lo
+            if lo in CFG["vg"]:
+                cp(16 * n, T.xg[:, 16 * lo:16 * hi], T.X[:, 0:W].indirect(T.hu[:, lo:hi]), xall + qs(lo, hi, "hu"), qs(lo, hi, "x"), r=gat)
+                continue
+            act(16 * n, T.xg[:, 16 * lo:16 * hi], T.X[:, 0:W].indirect(T.hu[:, lo:hi]), AF.Identity, xall + qs(lo, hi, "hu"),
+                qs(lo, hi, "x") + ["gq"], r=gat)
+        for lo, hi in zip(CFG["cuts"], CFG["cuts"][1:]):
+            h, n = lo // H, hi - lo
+            if lo % H == 0:
+                mm(H, "pT%d" % h, T["pT%d" % h][:, 0:H], T.c19[:], T.ones[:], True, False, ["c19", "ones"] + qs(lo, hi, "x"),
+                   ["tsum%d" % h])
+            mins = ["m%d.%d" % (lo, k) for k in range(4)]
+            for k in range(4):
+                tt(4 * n, T.mn[:, 16 * lo + k:16 * hi:4], T.xg[:, 16 * lo + k:16 * hi:4],
+                   T["pZ%d" % h][:, 4 * (lo % H):4 * (lo % H + n)], OP.min, qs(lo, hi, "x") + ["zp%d" % h], [mins[k]], ["pZ%d" % h])
+            for kind, src, rd in (("T", T.xg, qs(lo, hi, "x")), ("G", T.mn, mins)):
+                bank = "p%s%d" % (kind, h)
+                for j in range(lo // 8, hi // 8):
+                    q = j % 16
+                    mm(H, bank, T[bank][:, 0:H], T.band[:, 15 - q:143 - q], src[:, H * j:H * j + H], kind == "G" and q == 0, q == 15,
+                       ["band"] + rd, ["%ssum%d" % (kind.lower(), h)])
+        for lo in range(0, L, run):
+            scan(16 * run, T.pm[:, 16 * lo:16 * (lo + run)], T.mask[:, 0:16 * run], T.xg[:, 16 * lo:16 * (lo + run)], OP.mult, OP.max,
+                 ["mask"] + qs(lo, lo + run, "x"), qs(lo, lo + run, "pm"), r=0.5)
         act(L, T.old[:], T.X[:, 0:W].indirect(T.offr[:]), AF.Identity, xall + ["offr"], ["old"], r=gat)
         ys = [["Y%d" % b for b in range(4 * hf, 4 * hf + 4)] + ["Yd%d" % hf] for hf in range(2)]
         if last:
@@ -457,7 +515,7 @@ def rank_program(g, core, T, topo):
             for blk in range(8):
                 bank, c0 = ("pP", "pU")[blk % 2], 512 * blk
                 y0 = c0 + (YW - YH) * (blk // 4)
-                toks = ["pJ.0", "pJA.0"] if bank == "pP" else ["u.0", "ul"]
+                toks = ["v0", "v64"] if bank == "pP" else ["u0", "u192", "ul"]
                 mm(512, bank, T[bank][:], T.id1[:], T.X[:, c0:c0 + 512], True, False, ["id1", "x15"] + xall, toks)
                 mm(512, bank, T[bank][:], T.id16[:], T.X[:, W // 2 + c0:W // 2 + c0 + 512], False, True, ["id16"] + xall, toks)
                 if blk < 8 - CFG["vpack"]:
@@ -468,55 +526,67 @@ def rank_program(g, core, T, topo):
             s, lo, bT, bG, bZ = ".%d" % h, H * h, "pT%d" % h, "pG%d" % h, "pZ%d" % h
             pT, pG, pZ = T[bT], T[bG], T[bZ]
             half = slice(lo, lo + H)
-            lead[0] = CFG["lead"] if h == 0 else 0.0
-            scan(H, T.ts[:, half], T.mask[:, 0:H], pT[:, 0:H], OP.mult, OP.add, ["mask", "tsum%d" % h], ["ts" + s], [bT])
-            scan(H, T.gs[:, half], T.mask[:, 0:H], pG[:, 0:H], OP.mult, OP.add, ["mask", "gsum%d" % h], ["gs" + s], [bG])
-            g1, pa, pb = pT[:, H:L], pT[:, L:L + 64], T.pb[:, 64 * h:64 * h + 64]
-            tt(64, pa, pG[:, 1:H:2], T.ts[:, lo:lo + H:2], OP.mult, ["gsum%d" % h, "ts" + s], ["pa" + s], [bG, bT])
-            tt(64, pb, pT[:, 1:H:2], T.gs[:, lo:lo + H:2], OP.mult, ["tsum%d" % h, "gs" + s], ["pb" + s], [bT])
-            tt(64, T.c1[:, lo + 1:lo + H:2], pa, pb, OP.is_gt, ["pa" + s, "pb" + s], ["c1" + s], [bT])
-            scan(H, g1, T.c1[:, half], T.gs[:, half], OP.max, OP.min, ["c1" + s, "gs" + s], ["g1" + s], [bT])
-            scan(H, T.t1[:, half], T.c1[:, half], T.ts[:, half], OP.max, OP.min, ["c1" + s, "ts" + s], ["t1" + s])
-            scan(H, T.k1[:, half], T.c1[:, half], T.kc[:], OP.max, OP.min, ["c1" + s, "kc"], ["k1" + s])
-            src = {"g": (pT, H, "g1" + s), "t": (T.t1, lo, "t1" + s), "k": (T.k1, lo, "k1" + s)}
-            for n in (2, 3, 4):
+            lead[0] = CFG["lead"][last] if h == 0 else 0.0
+            early, ns = CFG["early"][h], SENT[h]
+
+            def home(n, x):
+                m = H if n == 0 else L >> n
+                if n == early and x != "k":
+                    return sm, L * h + m * (x == "g"), "%s%d%sr%d" % (x, n, s, t)
+                if n == 4 and x != "k":
+                    return T.sv, 32 * h + 16 * (x == "g"), x + "4" + s
+                return (None, 0, "") if (n, x) == (0, "k") else (T[x + (str(n) if n else "s")], m * h, "%s%d%s" % (x, n, s))
+
+            src = {x: home(0, x) for x in "gtk"}
+            for x, bank in (("t", bT), ("g", bG)):
+                scan(H, src[x][0][:, src[x][1]:src[x][1] + H], T.mask[:, 0:H], T[bank][:, 0:H], OP.mult, OP.add,
+                     ["mask", "%ssum%d" % (x, h)], [src[x][2]], [bank])
+            for n in range(5):
                 m = L >> n
-                c_, co, cn = T["c%d" % n], m * h, "c%d%s" % (n, s)
                 (gb, go, gn), (tb, to, tn) = src["g"], src["t"]
-                pa_, pb_, bk = T.pa[:, 16 * h:16 * h + m // 2], T.pb[:, 64 * h:64 * h + m // 2], []
-                if n == 2:
-                    pa_, bk = pT[:, L:L + m // 2], [bT]
-                tt(m // 2, pa_, gb[:, go + 3:go + 2 * m:4], tb[:, to + 1:to + 2 * m:4], OP.mult, [gn, tn], ["pa" + s], bk)
-                tt(m // 2, pb_, gb[:, go + 1:go + 2 * m:4], tb[:, to + 3:to + 2 * m:4], OP.mult, [gn, tn], ["pb" + s], bk)
-                tt(m // 2, c_[:, co + 1:co + m:2], pa_, pb_, OP.is_gt, ["pa" + s, "pb" + s], [cn], bk)
-                dst = {"g": (T.g3, 32 * h), "t": (T.t3, 32 * h), "k": (T["k%d" % n], m * h)}
-                if n == 2:
-                    dst.update(g=(sm, lo + 64), t=(sm, lo))
-                if n == 4:
-                    dst.update(g=(T.sv, 48 * h + 16), t=(T.sv, 48 * h))
-                for x in "gtk":
-                    (sb, so, sn), (db, do_) = src[x], dst[x]
-                    tok = "%s%d%s" % (x, n, s) + ("r%d" % t if n == 2 and x != "k" else "")
-                    scan(m, db[:, do_:do_ + m], c_[:, co:co + m], sb[:, so + 1:so + 2 * m:2], OP.max, OP.min, [cn, sn], [tok],
-                         bk if x == "g" else [])
-                    src[x] = (db, do_, tok)
-                if n == 2:
-                    swap(t, lm[:, half], sm[:, half], [src["g"][2], src["t"][2]], "lm%d%s" % (t, s), "av%d%d" % (h, t), CFG["late"][h])
+                if n:
+                    c_, co, cn = T["c%d" % n], m * h, "c%d%s" % (n, s)
+                    pb = T.pb[:, 64 * h:64 * h + m // 2]
+                    if n == 1:
+                        pa, bk = pT[:, L:L + 64], [bT]
+                        tt(64, pa, pG[:, 1:H:2], tb[:, to:to + H:2], OP.mult, ["gsum%d" % h, tn], ["pa" + s], [bG, bT])
+                        tt(64, pb, pT[:, 1:H:2], gb[:, go:go + H:2], OP.mult, ["tsum%d" % h, gn], ["pb" + s], [bT])
+                    else:
+                        pa, bk = T.pa[:, 32 * h:32 * h + m // 2], []
+                        tt(m // 2, pa, gb[:, go + 3:go + 2 * m:4], tb[:, to + 1:to + 2 * m:4], OP.mult, [gn, tn], ["pa" + s])
+                        tt(m // 2, pb, gb[:, go + 1:go + 2 * m:4], tb[:, to + 3:to + 2 * m:4], OP.mult, [gn, tn], ["pb" + s])
+                    tt(m // 2, c_[:, co + 1:co + m:2], pa, pb, OP.is_gt, ["pa" + s, "pb" + s], [cn], bk)
+                    for x in "gtk":
+                        if (n, x) == (1, "k"):
+                            mm(64, bG, pG[:, 320:384], T.id1[:], T.kvs[:], True, False, ["id1", "kvs", cn], ["k1" + s])
+                            mm(64, bG, pG[:, 320:384], T.ids[:], c_[:, co + 1:co + m:2], False, True, ["ids", cn], ["k1" + s])
+                            continue
+                        (sb, so, sn), (db, do_, tok) = src[x], home(n, x)
+                        if (n, x) == (2, "k"):
+                            scan(m, db[:, do_:do_ + m], c_[:, co:co + m], pG[:, 320:384], OP.max, OP.min, [cn, "k1" + s], [tok], [bG])
+                        else:
+                            scan(m, db[:, do_:do_ + m], c_[:, co:co + m], sb[:, so:so + m] if n == 1 else sb[:, so + 1:so + 2 * m:2],
+                                 OP.max, OP.min, [cn, sn], [tok])
+                        src[x] = (db, do_, tok)
+                if n == early:
+                    wide = 2 * min(H, m)
+                    swap(t, lm[:, L * h:L * h + wide], sm[:, L * h:L * h + wide], [src["g"][2], src["t"][2]], "lm%d%s" % (t, s),
+                         "av%d%d" % (h, t), CFG["late"][h])
+                    if h == 0:
+                        rival(t, 1, [src["g"][2], src["t"][2]] if CFG["hold"] and not last else [])
+                    theirs = lm[:, L * h:L * h + wide] if n == 0 else lm[:, L * h + 1:L * h + wide:2]
             k4 = T.k4[:, 16 * h + 1:16 * h + 16:2]
             o = 32 * h
-            act(H, T.rp[:, half], T.sv[:, 48 * h:48 * h + 40].indirect(rep8), AF.Identity, ["g4" + s, "t4" + s, "rep8g", "rep8t"],
-                ["rp" + s], r=gat)
-            ts(8, T.offy[:, 8 * h:8 * h + 8], k4, 4096.0, None, OP.mult, None, ["k4" + s], ["offy" + s])
-            tt(8, T.sd[:, 64 * h:64 * h + 64:8], k4, T.kj[:], OP.subtract, ["k4" + s, "kj"], ["sdj" + s])
-            x0 = 192 + 64 * h
+            ts(8, T.offy[:, 8 * h:8 * h + 8], k4, 4096.0, q128, OP.mult, OP.add, ["k4" + s, "q128"], ["offy" + s])
+            tt(8, slots(T.sd, h, 0, 0), k4, T.kj[:], OP.subtract, ["k4" + s, "kj"], ["sd0" + s])
             if last:
-                ts(64, T.sd[:, x0:x0 + 64], ib, -16 * S19, qc["xl"], OP.mult, OP.add, ["ib", "qcxl"], ["sdx" + s])
+                ts(8 * ns, slots(T.sd, h, 2), slots(T.ia, h, 1), -16 * S19, qc["xl"], OP.mult, OP.add, ["ib" + s, "qcxl"], ["sd2" + s])
                 for hf in range(2):
-                    act(4, T.sd[:, x0 + 32 * hf:x0 + 32 * hf + 32:8], T.rf[:, 8 * h + 4 * hf:8 * h + 4 * hf + 4], AF.Identity, ["rf"],
-                        ["sdx" + s], scale=-S19, bias=(TOP + W // 2 * h + YH * hf) * S19)
+                    act(4, slots(T.sd, h, 2, 0, 4 * hf, 4 * hf + 4), T.rf[:, 8 * h + 4 * hf:8 * h + 4 * hf + 4], AF.Identity, ["rf"],
+                        ["sd2" + s], scale=-S19, bias=(TOP + W // 2 * h + YH * hf) * S19)
             else:
-                tt(8, T.sa[:, 64 * h:64 * h + 64:8], k4, T.kb[:], OP.subtract, ["k4" + s, "kb"], ["sa" + s])
-                act(8, T.sd[:, x0:x0 + 64:8], T.rf[:, 8 * h:8 * h + 8], AF.Identity, ["rf"], ["sdx" + s], scale=-S19, bias=TOP * S19)
+                tt(8, slots(T.sa, h, 0, 0), k4, T.kb[:], OP.subtract, ["k4" + s, "kb"], ["sa" + s])
+                act(8, slots(T.sd, h, 2, 0), T.rf[:, 8 * h:8 * h + 8], AF.Identity, ["rf"], ["sd2" + s], scale=-S19, bias=TOP * S19)
             yt = "yh%d%s" % (t, s)
             act(H, yh[:, half], T.pm[:, 16 * lo:16 * (lo + H)].indirect(T.offy[:, 8 * h:8 * h + 8]), AF.Identity,
                 qs(lo, lo + H, "pm") + ["offy" + s], [yt], scale=0.5, r=gat)
@@ -525,56 +595,57 @@ def rank_program(g, core, T, topo):
             mm(H, bZ, pZ[:, H:L], (T.idmh if last else T.idh)[:], T.old[:, half], True, False, ["idh", "idmh", "old"], ["R%d" % h, "zp%d" % h])
             mm(H, bZ, pZ[:, H:L], T.id1[:], yh[:, half], False, True, ["id1", yt], ["R%d" % h])
             act(H, T.rec[:, half], pZ[:, H:L], AF.Identity, ["R%d" % h], ["rec" + s], [bZ], bias=LIFT - 0.25)
-            act(H, T.zq[:, half], T.z[:, half].indirect(colu), AF.Identity, ["z%d" % h, "colu"], ["zq" + s],
+            act(H, T.zq[:, half], T.z[:, half].indirect(colu), AF.Identity, zs(lo, lo + H) + ["colu", "x15"], ["zq" + s],
                 bias=LIFT - 0.25, scale=0.5, r=gat)
             mm(H, bZ, pZ[:, 0:H], T.idm2[:], yh[:, half], True, False, ["idm2", yt], ["D%d" % h, "zp%d" % h])
             for c in range(8):
-                mm(16, bZ, pZ[:, 16 * c:16 * c + 16], T.id1[:], T.z[:, lo + c:lo + H:8], False, c == 7, ["id1", "z%d" % h], ["D%d" % h])
+                mm(16, bZ, pZ[:, 16 * c:16 * c + 16], T.id1[:], T.z[:, lo + c:lo + H:8], False, c == 7, ["id1"] + zs(lo, lo + H), ["D%d" % h])
             act(H, T.zd_[:, half], pZ[:, 0:H], AF.Abs, ["D%d" % h], ["zd" + s], [bZ])
-            act(H, T.zz[:, L * h + H:L * h + L], T.zd_[:, half], AF.Identity, ["zd" + s], ["zw" + s], bias=LIFT)
+            for c0 in (lo, lo + 64):
+                act(64, T.zz[:, 2 * c0 + 64:2 * c0 + H], T.zd_[:, c0:c0 + 64], AF.Identity, ["zd" + s], ["zw%d" % c0], bias=LIFT)
             if last:
                 dl, yv, of = (T.d1, T.ya, T.offr) if h == 0 else (T.d16, T.yb, T.offh)
                 ts(H, dl[:], T.rec[:, half], -LIFT, 16.0 if h else 1.0, OP.add, OP.mult, ["rec" + s], ["dl" + s], r=0.5)
                 for hf in range(2):
                     tt(64, yv[:, 64 * hf:64 * hf + 64], T.Y[:, (YW - YH) * hf:YW * (hf + 1)].indirect(of[:, 4 * hf:4 * hf + 4]),
                        dl[:, 64 * hf:64 * hf + 64], OP.add, ys[0] + ys[hf] + ["offr", "offh", "dl" + s], ["yv%d%s" % (hf, s)], r=gat)
-            c5, so = T.c5[:, 64 * h:64 * h + 64], 192 * h
-            tt(H, T.qq[:, half], T.rp[:, half], lm[:, half], OP.mult, ["rp" + s, "lm%d%s" % (t, s)], ["qq" + s])
-            tt(64, c5, T.qq[:, lo:lo + 64], T.qq[:, lo + 64:lo + H], OP.is_ge if rank < (rank ^ STEPS[t]) else OP.is_gt,
-               ["qq" + s], ["c5" + s])
+            c5, qq, wide = slots(T.c5, h, 0), T["qq%d" % h], 8 * (ns + 1)
+            mine = T.rp[:, L * h:L * h + 16 * ns]
+            act(16 * ns, mine, T.sv[:, o:o + 32].indirect(T.lists[:, 32 + 16 * h:32 + 16 * h + ns]), AF.Identity,
+                ["g4" + s, "t4" + s, "rep" + s], ["rp" + s], r=gat)
+            tt(16 * ns, qq[:, :, 1:ns + 1], mine, theirs, OP.mult, ["rp" + s, "lm%d%s" % (t, s)], ["qq" + s])
+            tt(wide, c5, qq[:, 0:8, :], qq[:, 8:16, :], OP.is_ge if rank < (rank ^ STEPS[t]) else OP.is_gt, ["qq" + s], ["c5" + s])
             if not last:
-                scan(64, T.sb[:, 64 * h:64 * h + 64], c5, T.sa[:, 64 * h:64 * h + 64], OP.min, OP.max, ["c5" + s, "sa" + s], ["sb" + s])
+                scan(wide, slots(T.sb, h, 0), c5, slots(T.sa, h, 0), OP.min, OP.max, ["c5" + s, "sa" + s], ["sb" + s])
+                if h == 0:
+                    mm(1, "pG0", T.pG0[:, L:L + 1], T.c17[:], T.drop[:, 0:1], True, False, ["c17", "drop", "sb" + s], ["asum"])
                 for c in range(8):
-                    mm(1, "pG0", T.pG0[:, L + h:L + h + 1], T.c17[:], T.sb[:, 64 * h + 8 * c + 7:64 * h + 8 * c + 8], c == 0, c == 7,
-                       ["c17", "sb" + s], ["asum" + s])
-            for i, (x, d0) in enumerate((("j" + s, 64 * h), ("z", 128), ("x" + s, x0))):
-                scan(64, T.se[:, so + 64 * i:so + 64 * i + 64], c5, T.sd[:, d0:d0 + 64], OP.min, OP.max, ["c5" + s, "sd" + x],
-                     ["se%d%s" % (i, s)])
-            ts(16, T.off[:, o:o + 16], T.se[:, so + 7:so + 128:8], 1 / S19, None, OP.mult, None, ["se0" + s, "se1" + s], ["off" + s])
-            ts(8, T.off[:, o + 16:o + 24], T.se[:, so + 135:so + 192:8], -1 / S19, float(TOP), OP.mult, OP.add, ["se2" + s], ["offx" + s])
-            offz = T.off[:, o + 8:o + 16]
+                    mm(1, "pG0", T.pG0[:, L:L + 1], T.c17[:], slots(T.sb, h, 0, ns, c, c + 1), False, h == 1 and c == 7,
+                       ["c17", "sb" + s], ["asum"])
+            for i in range(3):
+                scan(wide, slots(T.se, h, i), c5, slots(T.sd, h, i), OP.min, OP.max, ["c5" + s, "sd%d%s" % (i, s)], ["se%d%s" % (i, s)])
+            ts(16, T.off[:, o:o + 16], slots(T.se, h, 0, ns, 0, 16), 1 / S19, None, OP.mult, None, ["se0" + s, "se1" + s], ["off" + s])
+            ts(8, T.off[:, o + 16:o + 24], slots(T.se, h, 2, ns), -1 / S19, float(TOP), OP.mult, OP.add, ["se2" + s], ["offx" + s])
             act(H, T.jfin[:, half] if last else tw[t + 1][:, slab(t + 1, h, 0, 1)], tw[t][:, slab(t, h, 0, SLABS)].indirect(T.off[:, o:o + 8]),
                 AF.Identity, ["off" + s] + shifted(t, h), ["j%d%s" % (t + 1, s)], r=gat)
             if not last:
                 lists(t + 1, h, [])
-            tt(H, T.zz[:, L * h:L * h + H], ly[:, half], T.zq[:, half], OP.add, ["ly%d%s" % (t, s), "zq" + s], ["zl" + s])
-            ts(H, T.z[:, half], T.zz[:, L * h:L * h + L].indirect(offz), -LIFT, 1.0, OP.add, OP.max, ["zl" + s, "zw" + s, "off" + s],
-               ["z%d" % h], r=gat)
+            for c0 in (lo, lo + 64):
+                tt(64, T.zz[:, 2 * c0:2 * c0 + 64], ly[:, c0:c0 + 64], T.zq[:, c0:c0 + 64], OP.add, ["ly%d%s" % (t, s), "zq" + s],
+                   ["zl%d" % c0])
+                ts(64, T.z[:, c0:c0 + 64], T.zz[:, 2 * c0:2 * c0 + H].indirect(T.off[:, o + 8 + c0 % H // 16:o + 12 + c0 % H // 16]),
+                   -LIFT, 1.0, OP.add, OP.max, ["zl%d" % c0, "zw%d" % c0, "off" + s], zs(c0, c0 + 64), r=gat)
             if not last:
                 n = CFG["scat"]
                 for c0 in range(0, H, n):
                     tt(n, T.X[:, 0:W + L].indirect(T.off[:, o + 16 + c0 // 16:o + 16 + (c0 + n) // 16]), T.rec[:, lo + c0:lo + c0 + n],
                        T.neg[:, 0:n], OP.add, ["offx" + s, "rec" + s, "neg", "Xd"], xall, r=sca)
                 if h == 0:
-                    picks(t + 1, 0, -DROP, [], H, True)
+                    picks(t + 1, 0, -DROP, [], CFG["parts0"], True)
                 else:
                     for c0 in (0, 64):
-                        ts(64, T.hd[:, c0:c0 + 64], T.hf[:, c0:c0 + 64], T.pG0[:, L:L + 1], T.pG0[:, L + 1:L + 2], OP.add, OP.add,
-                           qs(c0, c0 + 64, "hf") + ["asum.0", "asum.1"], qs(c0, c0 + 64, "hd"), ["pG0"])
-                        finish(c0, c0 + 64)
-                    act(2, T.aj[:, 0:2], T.pG0[:, L:L + 2], AF.Identity, ["asum.0", "asum.1", "hd4"], ["acol"], ["pG0"], bias=-DROP / 2,
-                        acc=T.acol[:, 0:1])
-                    picks(t + 1, 1, T.acol[:, 0:1], ["acol"], H, False)
+                        with_a(c0, c0 + 64, ["asum"])
+                    picks(t + 1, 1, T.pG0[:, L:L + 1], ["asum"], CFG["parts"], False)
             else:
                 for hf in range(2):
                     cp(64, T.Y[:, hf * YW:hf * YW + YW].indirect(T.off[:, o + 16 + 4 * hf:o + 20 + 4 * hf]), yv[:, 64 * hf:64 * hf + 64],

from concourse.mybir import AluOpType, ActivationFunctionType

OP = AluOpType
AF = ActivationFunctionType
ROUNDS = 4
STEPS = (1, 2, 3, 1)
W = 8192
L = 256
H = 128
YH, YW = 2048, 2176
SLABS = 17
S12 = 2.0 ** -12
S19 = 2.0 ** -19
TOP = 16384
LIFT = 192.0
DROP = 32.0 * 5 * W

CFG = {"cuts": (0, 16, 64, 80, 128, 192, 224, 256),
       "vg": (0, 64), "mod": "av", "parts0": 128,
       "run": 16, "scat": 64, "vpack": 2, "lead": (0.0, 0.0), "late": (0.3, 0.3, 0.1, 0.1), "early": (2, 2), "parts": 64, "hold": True,
       "cyc": 0.00083, "pe": 0.00042, "wake": 0.2, "gat": 1.56, "sca": 3.8, "dma": 2.2, "far": 3.3, "passes": 2, "look": 0.1, "fit": 0.03}
TURN_Q = ((32, 2), (2, 0), (16, 3), (1, 0))
TURN_C = (((4, 8),), ((1, 2), (32, 4)), ((2, 8),), ((16, 8),))

SENT = [16 >> e for e in CFG["early"]]
PW = 8 * 17

F, B, I, U = "float32", "bfloat16", "int32", "uint16"
SCRATCH = {}
for _names, _n, _d in (
        ("X", W + L, B), ("Y", 2 * YW, B), ("xg mn pm", 16 * L, B), ("mask", 1024, B), ("jin ha hb hd he", L, I), ("hu", L, U),
        ("zin z old rec zd_", L, B), ("ones neg blkm w2 id1 id16 idm2 idh idmh idk ids c19 c17 d1 d16 ya yb", H, B), ("bm band wband", 144, B),
        ("jj hf rp", 2 * L, F), ("mq k3i c1", L, B), ("kvs", 64, B), ("bandv", 144, F), ("blkv kv c2 g2 t2 k2 pb lt", H, F),
        ("hc zq jfin gs ts g1 t1", L, F), ("zz", 2 * L, B),
        ("sd se", 6 * PW, F), ("ia", 4 * PW, F), ("sa c5", 2 * PW, F), ("sb", 2 * PW, B), ("c3 g3 t3 k3 l32 pa sv", 64, F), ("c4 k4", 32, F), ("q1", 24, F), ("rf", 16, F),
        ("w kb kj", 8, F), ("drop", 8, B), ("pi", 8, I), ("ti rc", 16, I), ("offr offy", 16, U), ("offh", 8, U), ("off lists", 64, U)):
    for _x in _names.split():
        SCRATCH[_x] = ("sbuf", [128, _n], _d)
for _h in range(2):
    SCRATCH["qq%d" % _h] = ("sbuf", [128, 16, SENT[_h] + 1], F)
for _x in ("pT0", "pT1", "pG0", "pG1", "pZ0", "pZ1", "pU", "pP"):
    SCRATCH[_x] = ("psum", [128, 512], F)
SEMAPHORES = ["v", "a", "p", "g", "ldz", "ldw", "ldj", "ldx", "ldx2", "sent", "outj", "outz", "outx"]
for _t in range(ROUNDS):
    SCRATCH["tw%d" % _t] = ("sbuf", [128, SLABS * L], F)
    SCRATCH["sm%d" % _t] = ("sbuf", [128, 2 * L], F)
    SCRATCH["lm%d" % _t] = ("sbuf", [128, 2 * L], F)
    SCRATCH["yh%d" % _t] = ("sbuf", [128, L], B)
    SCRATCH["ly%d" % _t] = ("sbuf", [128, L], B)
    SCRATCH["do%d" % _t] = ("dram", [16, 16 * H], F)
    SCRATCH["dr%d" % _t] = ("dram", [16, 16 * H], F)
    SEMAPHORES += ["%s%d%d" % (x, h, _t) for x in ("aj", "av", "ay", "so", "sr", "tp") for h in range(2)]


TURNS = {"sq", "gq"}


def arrange(ops):
    n, wake = len(ops), CFG["wake"]
    preds, succs, writer, readers = [set() for _ in ops], [[] for _ in ops], {}, {}
    for i, op in enumerate(ops):
        for tok in op[2] + op[3]:
            if tok in writer:
                preds[i].add(writer[tok])
        for tok in op[3]:
            preds[i].update(readers.get(tok, ()))
        preds[i].discard(i)
        for tok in op[2]:
            readers.setdefault(tok, []).append(i)
        for tok in op[3]:
            writer[tok], readers[tok] = i, []
    for i in range(n):
        for j in preds[i]:
            succs[j].append(i)

    def gap(j, i):
        busy, late = ops[j][7]
        if ops[j][0] == ops[i][0] and (ops[i][0] == "p" or not set(ops[j][3]) & set(ops[i][2] + ops[i][3]) - TURNS
                                       and not set(ops[j][2]) & set(ops[i][3])):
            return busy
        return busy + late + (wake if ops[i][0] else 0.0)

    chain = [0.0] * n
    for i in reversed(range(n)):
        chain[i] = max([gap(i, k) + chain[k] for k in succs[i]] + [sum(ops[i][7])])
    if "log" in CFG:
        i, path = max(range(n), key=lambda k: chain[k]), []
        while succs[i]:
            path.append((round(chain[i], 2), ops[i][0], ops[i][3][:1]))
            i = max(succs[i], key=lambda k: gap(i, k) + chain[k])
        CFG["log"].append(path)
    chain = [c + op[8] for c, op in zip(chain, ops)]

    def place(rank, back):
        before, after = (succs, preds) if back else (preds, succs)
        ready, left, time = [op[7][1] if back else 0.0 for op in ops], [len(p) for p in before], [0.0] * n
        pool, free, bank = {}, {}, {}
        for i in range(n):
            if not left[i]:
                pool.setdefault(ops[i][0], []).append(i)

        def earliest(i):
            t = max(ready[i], free.get(ops[i][0], 0.0)) if ops[i][0] else ready[i]
            for b in ops[i][4]:
                if b in bank and bank[b][0] != ops[i][0]:
                    t = max(t, bank[b][1] + wake)
            return t

        for _ in range(n):
            t0, e = min((min(earliest(i) for i in p), str(e)) for e, p in pool.items() if p)
            e = None if e == "None" else e
            near = [(earliest(i), i) for i in pool[e]]
            t, i = max((x for x in near if x[0] <= t0 + CFG["look"]), key=lambda x: (rank[x[1]], -x[1]))
            fits = [x for x in near if x[0] + ops[x[1]][7][0] <= t + CFG["fit"] and x[1] != i]
            if t > t0 and fits:
                t, i = max(fits, key=lambda x: (rank[x[1]], -x[1]))
            pool[e].remove(i)
            busy = ops[i][7][0]
            time[i], free[e] = t, t + busy
            for b in ops[i][4]:
                bank[b] = (e, t + busy)
            for k in after[i]:
                ready[k] = max(ready[k], t + (gap(k, i) - ops[k][7][0] + busy if back else gap(i, k)))
                left[k] -= 1
                if not left[k]:
                    pool.setdefault(ops[k][0], []).append(k)
        return time

    best = None
    for _ in range(CFG["passes"]):
        time = place(chain, False)
        end = max(time[i] + sum(ops[i][7]) for i in range(n))
        CFG.get("log", []).append((end, time))
        if best is None or end < best[0]:
            best = (end, time)
        back = place([time[i] + ops[i][7][0] for i in range(n)], True)
        chain = [back[i] + ops[i][7][0] for i in range(n)]
    return [ops[i] for i in sorted(range(n), key=lambda i: (best[1][i], i))]


def emit(g, T, ops):
    queue = {"v": g.vector, "a": g.scalar, "p": g.tensor, "g": g, "s": g.sync}
    writer, readers, count, dmas = {}, {}, {}, {}
    known = {e: {} for e in queue}
    snap, waits, wanted = {}, [], set()
    for e, fn, rd, wr, banks, dsem, ext in [op[:7] for op in ops]:
        wr = [tok for tok in wr if tok not in TURNS]
        if ext is not None:
            for tok in wr:
                writer[tok] = ext
                readers[tok] = []
            snap[ext] = {}
            waits.append(None)
            continue
        deps = []
        for tok in rd:
            if tok in writer:
                deps.append(writer[tok])
        for tok in wr:
            if tok in writer:
                deps.append(writer[tok])
            deps += readers.get(tok, [])
        for tok in banks:
            if tok in writer and writer[tok][0] != e:
                deps.append(writer[tok])
        need = {}
        for key, n in deps:
            if key == "p" and e == "p":
                continue
            if key in dmas:
                n = dmas[key]
            need[key] = max(need.get(key, 0), n)
        mine = []
        for key in sorted(need):
            n = need[key]
            if known[e].get(key, 0) >= n:
                continue
            if any(snap[(k2, need[k2])].get(key, 0) >= n for k2 in need if k2 != key):
                continue
            mine.append((key, n))
        for key, n in mine:
            for k2, n2 in snap[(key, n)].items():
                known[e][k2] = max(known[e].get(k2, 0), n2)
            known[e][key] = max(known[e].get(key, 0), n)
            wanted.add((key, n))
        waits.append(mine)
        if fn is None or dsem == "":
            continue
        if dsem is not None:
            prev = snap.get((dsem, dmas.get(dsem, 0)), {})
            dmas[dsem] = dmas.get(dsem, 0) + 16
            me = (dsem, dmas[dsem])
            s = dict(known[e])
            for k2, n2 in prev.items():
                s[k2] = max(s.get(k2, 0), n2)
            snap[me] = s
        else:
            count[e] = count.get(e, 0) + 1
            me = (e, count[e])
            snap[me] = dict(known[e])
        for tok in rd:
            readers.setdefault(tok, []).append(me)
        for tok in wr:
            writer[tok] = me
            readers[tok] = []
        for tok in banks:
            writer[tok] = me
    level, seen, count = {}, {}, {}
    for (e, fn, rd, wr, banks, dsem, ext), mine in zip([op[:7] for op in ops], waits):
        if ext is not None:
            continue
        for key, n in mine:
            queue[e].wait_ge(T.sem[key], level[(key, n)] if key in queue else n)
        if fn is None:
            continue
        ins = fn()
        if dsem == "":
            continue
        if dsem is not None:
            ins.then_inc(T.sem[dsem], 16)
        else:
            count[e] = count.get(e, 0) + 1
            if (e, count[e]) in wanted:
                seen[e] = seen.get(e, 0) + 1
                level[(e, count[e])] = seen[e]
                ins.then_inc(T.sem[e], 1)


def rank_program(g, core, T, topo):
    rank = T.rank_of(core)
    if rank is None:
        return
    ops = []
    v, a, pe = g.vector, g.scalar, g.tensor
    sent, lead = [0], [0.0]
    cyc, gat, sca = CFG["cyc"], CFG["gat"], CFG["sca"]

    def add(e, fn, rd=(), wr=(), banks=(), dsem=None, ext=None, cost=(0.0, 0.0)):
        ops.append((e, fn, list(rd), list(wr), list(banks), dsem, ext, cost, lead[0]))

    def dve(n, r):
        return (max(64.0, n * r) * cyc if r <= 1 or r == 2 else 0.05 + n * r * cyc, 0.0)

    def ts(n, out, in0, s1, s2, o0, o1, rd, wr, banks=(), r=1):
        if o1 is None:
            add("v", lambda: v.tensor_scalar(out, in0, s1, None, o0), rd, wr, banks, cost=dve(n, r))
        else:
            add("v", lambda: v.tensor_scalar(out, in0, s1, s2, o0, o1), rd, wr, banks, cost=dve(n, r))

    def tt(n, out, in0, in1, op, rd, wr, banks=(), r=None):
        add("v", lambda: v.tensor_tensor(out, in0, in1, op), rd, wr, banks, cost=dve(n, r or (1 if banks else 2)))

    def cp(n, out, in_, rd, wr, banks=(), r=1):
        add("v", lambda: v.tensor_copy(out, in_), rd, wr, banks, cost=dve(n, r))

    def ms(n, ap, c, wr):
        add("v", lambda: v.memset(ap, c), (), wr, cost=dve(n, 0.5))

    def scan(n, out, d0, d1, o0, o1, rd, wr, banks=(), r=1):
        add("v", lambda: v.tensor_tensor_scan(out, d0, d1, 0.0, o0, o1), rd, wr, banks, cost=dve(n, r))

    def act(n, out, in_, func, rd, wr, banks=(), bias=0.0, scale=1.0, acc=None, r=1):
        cost = (0.06 + max(64.0, n * r) * cyc + (0.0 if acc is None else 0.02), 0.0)
        if acc is None:
            add("a", lambda: a.activation(out, in_, func, bias=bias, scale=scale), rd, wr, banks, cost=cost)
        else:
            add("a", lambda: a.activation(out, in_, func, bias=bias, scale=scale, accum_out=acc), rd, wr, banks, cost=cost)

    def mm(n, bank, out, lhs, rhs, start, stop, rd, wr):
        add("p", lambda: pe.matmul(out, lhs, rhs, start, stop), rd, wr + ["group" + bank], [bank],
            cost=(max(64, n) * CFG["pe"], 0.03))

    def dma(e, out, in_, rd, wr, sem, late=0.0):
        q = g.sync if e == "s" else g.scalar
        add(e, lambda: q.dma_start(out, in_), rd, wr + (["sq"] if late and e == "s" else []), (), sem, cost=(0.06, CFG["dma"] + late))

    def iota(out, pat, base, mult, wr, flag=True):
        n = 1
        for _, k in pat:
            n *= k
        if flag:
            add("g", lambda: g.iota(out, pat, base, mult, allow_small_or_imprecise_dtypes=True), (), wr, cost=(0.13 + 2 * n * cyc, 0.0))
        else:
            add("g", lambda: g.iota(out, pat, base, mult), (), wr, cost=(0.13 + 2 * n * cyc, 0.0))

    def swap(t, out, in_, rd, tok, sem, late=0.0):
        peer = T.cores[rank ^ STEPS[t]]
        rid, pid, _ = topo.addr(peer)
        add("g", lambda: g.remote_dma(out, in_, T.sem[sem], T.sem.sent, pid, rid, topo.mask(core, peer)), rd, ["went" + sem], (), "",
            cost=(0.3 if sent[0] else 1.3, 0.0))
        sent[0] += len(topo.engines(core, peer))
        add(None, None, ["went" + sem], [tok], ext=(sem, len(topo.engines(peer, core))), cost=(0.0, CFG["far"] - 0.3 + late))

    def qs(lo, hi, name):
        return ["%s%d" % (name, q) for q in range(lo // 16, hi // 16)]

    tw = [T["tw%d" % t] for t in range(ROUNDS)]
    zall, xall = ["z0", "z1", "z2", "z3"], ["X", "X2"]

    def zs(lo, hi):
        return zall[lo // 64:min(hi, L) // 64]

    def names(t):
        return ["j%d.0" % t, "j%d.1" % t]

    def slab(t, h, s0, s1):
        return slice(SLABS * H * h + H * s0, SLABS * H * h + H * s1)

    def lists(t, h, after):
        w_, do, dr, s, rows = tw[t], T["do%d" % t], T["dr%d" % t], "%d.%d" % (t, h), slice(8 * h, 8 * h + 8)
        sem = "%d%d" % (h, t)
        swap(t, w_[:, slab(t, h, 16, 17)], w_[:, slab(t, h, 0, 1)], ["j" + s] + after[:1], "jr" + s, "aj" + sem, 0.8)
        dma("s", do[rows, :], w_[:, slab(t, h, 0, 1)], ["j" + s] + after, ["do" + s], "so" + sem)
        dma("s", dr[rows, :], w_[:, slab(t, h, 16, 17)], ["jr" + s], ["dr" + s], "sr" + sem)
        for k in range(15):
            dma("s", w_[k::16, slab(t, h, 1, 16 - k)], do[rows, (k + 1) * H:16 * H], ["do" + s], ["to%s.%d" % (s, k)], "tp" + sem)
        if h == 0:
            rival(t, h, [])

    def rival(t, h, after):
        s, rows = "%d.%d" % (t, h), slice(8 * h, 8 * h + 8)
        for k in range(1, 16):
            dma("s", tw[t][k::16, slab(t, h, 16 - k, 16)], T["dr%d" % t][rows, 0:k * H], ["dr" + s] + after, ["tr%s.%d" % (s, k)],
                "tp%d%d" % (h, t))

    def shifted(t, h):
        s = "%d.%d" % (t, h)
        return ["j" + s, "jr" + s] + ["to%s.%d" % (s, k) for k in range(15)] + ["tr%s.%d" % (s, k) for k in range(1, 16)]

    dma("s", T.zin[:], T.zd[:], [], ["zin"], "ldz", 0.01)
    dma("a", T.jin[:], T.jn[:], [], ["jin"], "ldj", 0.01)
    dma("s", T.w[:, 0:1], T.wt[:], [], ["w"], "ldw", 0.01)
    dma("s", T.X[:, 0:W // 2], T.xt[:, 0:W // 2], [], ["X"], "ldx", 1.3)
    dma("s", T.X[:, W // 2:W], T.xt[:, W // 2:W], [], ["X2"], "ldx2", 2.5)
    iota(T.pi[:, 0:1], [[0, 1]], 0, 1, ["pi"], False)
    iota(T.blkv[:], [[16, 8], [0, 16]], 0, -1, ["blkv"])
    iota(T.bandv[:], [[1, 144]], 0, -1, ["bandv"])
    iota(T.kv[:], [[16, 8], [1, 16]], 0, 0, ["kv"])
    for t, pat in enumerate(TURN_C):
        iota(T.lt[:, 16 * t:16 * t + 16], [[32 * H, 2]] + [[32 * s, n] for s, n in pat], 0, 0, ["lt%d" % t])
    iota(T.lt[:, 64:80], [[H, 2], [1, 4], [64, 2]], 0, 0, ["lt4"])
    q1, q128, q4, w = [T.q1[:, i:i + 1] for i in (0, 1, 2)] + [T.w[:, 0:1]]
    firstu, colu = T.lists[:, 0:16], T.lists[:, 16:24]

    def slots(buf, h, i, at=None, c0=0, c1=8, parts=3):
        n, o = SENT[h] + 1, PW * (buf.shape[1] // (2 * PW) * h) + 8 * (SENT[h] + 1) * i
        return buf[:, o:o + 8 * n] if at is None else buf[:, o + n * c0 + at:o + n * c1:n]

    ts(1, T.pi[:, 1:2], T.pi[:, 0:1], 15, None, OP.bitwise_and, None, ["pi"], ["qi"])
    ts(1, T.pi[:, 2:3], T.pi[:, 0:1], 2, 3, OP.arith_shift_right, OP.bitwise_and, ["pi"], ["qi2"])
    ts(1, T.pi[:, 3:4], T.pi[:, 0:1], 3, 1, OP.arith_shift_right, OP.bitwise_and, ["pi"], ["qi3"])
    cp(1, q1, T.pi[:, 1:2], ["qi"], ["q1"])
    for ap, c, tok in ((q4, 4.0, "q4"), (q128, 128.0, "q128")):
        ts(1, ap, T.pi[:, 1:2], c, None, OP.mult, None, ["qi"], [tok])
    qc = {}
    for i, (x, m, c) in enumerate((("j", 8, 0), ("z", 1, 0), ("zw", 1, 64), ("x0", -1, TOP - W), ("x1", -1, TOP - W - H),
                                   ("xl", -1, TOP - YH), ("k", -8, -128))):
        qc[x] = T.q1[:, 10 + i:11 + i]
        ts(1, qc[x], T.pi[:, 1:2], m * S19, c * S19, OP.mult, OP.add, ["qi"], ["qc" + x])
    for t, (m, sh) in enumerate(TURN_Q):
        qa = T.q1[:, 4 + t:5 + t]
        ts(1, qa, T.pi[:, 1:2], 32.0 * m, None, OP.mult, None, ["qi"], ["qa%d" % t])
        if sh:
            ts(1, qa, T.pi[:, sh:sh + 1], -32.0 * 127, qa, OP.mult, OP.add, ["qi%d" % sh, "qa%d" % t], ["qa%d" % t])
        ts(16, T.l32[:, 16 * t:16 * t + 16], T.lt[:, 16 * t:16 * t + 16], qa, None, OP.add, None, ["lt%d" % t, "qa%d" % t], ["l32.%d" % t])
    ts(16, firstu, T.lt[:, 64:80], q4, None, OP.add, None, ["lt4", "q4"], ["firstu"])
    ts(H, T.blkm[:], T.blkv[:], q1, 0.0, OP.add, OP.is_equal, ["blkv", "q1"], ["blkm"])
    ts(H, T.id1[:], T.bandv[:, 0:128], 0.0, None, OP.is_equal, None, ["bandv"], ["id1"])
    ts(144, T.bm[:], T.bandv[:], q1, 15.0, OP.add, OP.is_equal, ["bandv", "q1"], ["bm"])
    act(144, T.band[:], T.bm[:], AF.Identity, ["bm"], ["band"], scale=S12)
    ms(L, T.k3i[:], 0.0, ["k3i"])
    ms(H, T.k3i[:, 1::2], 2048 * LIFT * S12 / 32 / 128, ["k3i"])
    for name, c in (("idk", -2048.0), ("ids", S12), ("id16", 16.0), ("idm2", -2.0), ("idh", 0.5), ("idmh", -0.5)):
        act(H, T[name][:], T.id1[:], AF.Identity, ["id1"], [name], scale=c)
    act(64, T.kvs[:], T.kv[:, 0::2], AF.Identity, ["kv"], ["kvs"], scale=S12)
    ts(8, colu, T.kv[:, 0::16], q128, 1.0 / 16, OP.add, OP.mult, ["kv", "q128"], ["colu"])
    ts(8, T.kb[:], T.kv[:, 0::16], -1.0, S12, OP.add, OP.mult, ["kv"], ["kb"])
    ts(8, T.kj[:], T.kv[:, 0::16], S12 - S19 / 16, qc["k"], OP.mult, OP.add, ["kv", "qck"], ["kj"])
    ms(H, T.c19[:], 2.0 ** -19, ["c19"])
    ms(H, T.c17[:], 32 / S12, ["c17"])
    ms(8, T.drop[:], -DROP * S12 / 32 / 128, ["drop"])
    ms(2 * PW, T.sa[:], 0.0, ["sa.0", "sa.1"])
    run = CFG["run"]
    ms(16 * run, T.mask[:, 0:16 * run], 1.0, ["mask"])
    ms(run, T.mask[:, 0:16 * run:16], 0.0, ["mask"])
    for h in range(2):
        n, s = SENT[h], ".%d" % h
        iota(slots(T.ia, h, 0), [[1, 8], [0, n + 1]], 0, 0, ["ia" + s])
        iota(slots(T.ia, h, 1), [[0, 2], [1, 4], [0, n + 1]], 0, 0, ["ib" + s])
        iota(T.lt[:, 80 + 16 * h:80 + 16 * h + n], [[-16, 2], [32 // n, n // 2]], 17, 0, ["lt5" + s])
        ts(1, T.pi[:, 4 + h:5 + h], T.pi[:, 1:2], 4 - CFG["early"][h], None, OP.arith_shift_right, None, ["qi"], ["qn" + s])
        ts(1, T.q1[:, 8 + h:9 + h], T.pi[:, 4 + h:5 + h], 2.0, None, OP.mult, None, ["qn" + s], ["q2n" + s])
        ts(n, T.lists[:, 32 + 16 * h:32 + 16 * h + n], T.lt[:, 80 + 16 * h:80 + 16 * h + n], T.q1[:, 8 + h:9 + h], None, OP.add, None,
           ["lt5" + s, "q2n" + s], ["rep" + s])
        for i, (x, m) in enumerate((("j", 1), ("z", 16), ("x%d" % h, -16))):
            ts(8 * n, slots(T.sd, h, i), slots(T.ia, h, i % 2), m * S19, qc[x], OP.mult, OP.add, ["ia" + s, "ib" + s, "qc" + x],
               ["sd%d%s" % (i, s)])
        ts(8, slots(T.sd, h, 1, 0), slots(T.ia, h, 1, 0), 16 * S19, qc["zw"], OP.mult, OP.add, ["ib" + s, "qczw"], ["sd1" + s])
        ms(8, T["qq%d" % h][:, 0:8, 0], -1.0, ["qq" + s])
        ms(8, T["qq%d" % h][:, 8:16, 0], 0.0, ["qq" + s])
    ts(H, T.w2[:], T.blkm[:], w, 2.0, OP.mult, OP.mult, ["blkm", "w"], ["w2"], r=0.5)
    ts(144, T.wband[:], T.bm[:], w, None, OP.mult, None, ["bm", "w"], ["wband"], r=0.5)
    act(L, T.z[:], T.zin[:].indirect(firstu), AF.Identity, ["zin", "firstu"], zall, r=gat)
    for h in range(2):
        cp(H, tw[0][:, slab(0, h, 0, 1)], T.jin[:].indirect(T.lists[:, 8 * h:8 * h + 8]), ["jin", "firstu"], ["j0.%d" % h], r=gat)
        lists(0, h, xall)

    def fill(ap, n, c, wr):
        iota(ap, [[0, n]], int(c), 0, wr)

    fill(T.ones[:], H, 1, ["ones"])
    for n in (1, 2, 3, 4):
        fill(T["c%d" % n][:], 512 >> n, 1, ["c%d.0" % n, "c%d.1" % n])
    fill(T.neg[:], H, -LIFT, ["neg"])
    fill(T.X[:, W:W + L], L, 0, ["Xd"])
    for hf in range(2):
        fill(T.Y[:, hf * YW + YH:hf * YW + YW], YW - YH, 0, ["Yd%d" % hf])

    def picks(t, h, bias, rd, parts, later):
        lo, s = H * h, ".%d" % h
        bJ, bU = ("pP", "pT1")[h], ("pU", "pG1")[h]
        jt, j0 = "j%d%s" % (t, s), slab(t, h, 0, 1).start
        if CFG["mod"][h] == "a":
            act(H, T.jj[:, 2 * lo:2 * lo + L:2], tw[t][:, j0:j0 + H], AF.Identity, [jt], ["ja" + s])
            act(H, T.jj[:, 2 * lo + 1:2 * lo + L:2], tw[t][:, j0:j0 + H], AF.Identity, [jt], ["jb" + s], bias=-DROP, scale=33.0)
            for c0 in range(lo, lo + H, parts):
                c1, o, v0 = c0 + parts, c0 - lo, L + 2 * (c0 - lo)
                bu, vt = bU if o == 0 else ("pZ1", "pU")[h], ["v%d" % c0] + ["pa.1"] * h
                mm(parts, bu, T[bu][:, 384 + o:384 + o + parts], T.w2[:], T.z[:, c0:c1], True, True, ["w2"] + zs(c0, c1), ["u%d" % c0])
                act(parts, T.mq[:, c0:c1], T[bu][:, 384 + o:384 + o + parts], AF.Identity, ["u%d" % c0], qs(c0, c1, "mq"), [bu],
                    bias=LIFT - 0.5 + 2.0 ** -11, scale=2.0 ** -11)
                mm(2 * parts, bJ, T[bJ][:, v0:v0 + 2 * parts], T.c17[:], T.k3i[:, 0:2 * parts], True, False, ["c17", "k3i"] + zs(c0, c1), vt)
                mm(parts, bJ, T[bJ][:, v0 + 1:v0 + 2 * parts:2], T.w2[:], T.z[:, c0:c1], False, False, ["w2"] + zs(c0, c1), vt)
                mm(parts, bJ, T[bJ][:, v0 + 1:v0 + 2 * parts:2], T.idk[:], T.mq[:, c0:c1], False, True, ["idk"] + qs(c0, c1, "mq"), vt)
                scan(2 * parts, T.hf[:, 2 * c0:2 * c1], T[bJ][:, v0:v0 + 2 * parts], T.jj[:, 2 * c0:2 * c1], OP.mult, OP.add,
                     vt + ["ja" + s, "jb" + s], qs(c0, c1, "hf"), [bJ])
                if not later:
                    with_a(c0, c1, rd)
            return
        if True:
            ts(H, T.hc[:, lo:lo + H], tw[t][:, j0:j0 + H], 32.0, bias, OP.mult, OP.add, [jt] + rd, qs(lo, lo + H, "hc"),
               ["pG0"] if rd else [])
        for c0 in range(lo, lo + H, parts):
            c1, o = c0 + parts, c0 - lo
            bu = bU if o == 0 or later else ("pG0", "pU")[h]
            mm(parts, bu, T[bu][:, H + o:H + o + parts], T.w2[:], T.z[:, c0:c1], True, True, ["w2"] + zs(c0, c1), ["u%d" % c0])
            ts(parts, T.ha[:, c0:c1], T[bu][:, H + o:H + o + parts], 1.0, None, OP.add, None, ["u%d" % c0], qs(c0, c1, "ha"), [bu])
            ts(parts, T.hb[:, c0:c1], T.ha[:, c0:c1], 2047, None, OP.bitwise_and, None, qs(c0, c1, "ha"), qs(c0, c1, "hb"))
            tt(parts, T[bJ][:, H + o:H + o + parts], T.hb[:, c0:c1], tw[t][:, j0 + o:j0 + o + parts], OP.mult,
               qs(c0, c1, "hb") + [jt], ["pc%d" % c0], [bJ], r=2)
            tt(parts, T.hd[:, c0:c1], T[bJ][:, H + o:H + o + parts], T.hc[:, c0:c1], OP.add, qs(c0, c1, "hc") + ["pc%d" % c0],
               qs(c0, c1, "hd"), [bJ])
            finish(c0, c1)

    def with_a(c0, c1, rd):
        if rd:
            ts(c1 - c0, T.hd[:, c0:c1], T.hf[:, 2 * c0 + 1:2 * c1:2], T.pG0[:, L:L + 1], DROP, OP.add, OP.add, qs(c0, c1, "hf") + rd,
               qs(c0, c1, "hd"), ["pG0"])
        else:
            cp(c1 - c0, T.hd[:, c0:c1], T.hf[:, 2 * c0 + 1:2 * c1:2], qs(c0, c1, "hf"), qs(c0, c1, "hd"))
        finish(c0, c1)

    def finish(c0, c1):
        n = c1 - c0
        ts(n, T.he[:, c0:c1], T.hd[:, c0:c1], 5, W - 1, OP.arith_shift_right, OP.bitwise_and, qs(c0, c1, "hd"), qs(c0, c1, "he"))
        cp(n, T.hu[:, c0:c1], T.he[:, c0:c1], qs(c0, c1, "he"), qs(c0, c1, "hu"))

    for h in range(2):
        picks(0, h, -DROP, [], 64, False)

    for t in range(ROUNDS):
        last = t == ROUNDS - 1
        sm, lm, yh, ly = T["sm%d" % t], T["lm%d" % t], T["yh%d" % t], T["ly%d" % t]
        for h in range(2):
            for q in range(16):
                mm(8, "pU", T.pU[:, L + 8 * h:L + 8 * h + 8], T.wband[:, 15 - q:143 - q], T.z[:, H * h + 8 * q:H * h + 8 * q + 8],
                   q == 0, q == 15, ["wband", "hu7", "ha15", "mq15"] + zs(H * h, H * h + H), ["ul"])
        cp(16, T.ti[:], T.pU[:, L:L + 16], ["ul"], ["ti"], ["pU"])
        ts(16, T.rc[:], T.ti[:], 31, None, OP.bitwise_and, None, ["ti"], ["rc"])
        tt(16, T.rf[:], T.rc[:], T.l32[:, 16 * t:16 * t + 16], OP.add, ["rc", "l32.%d" % t], ["rf"])
        cp(16, T.offr[:], T.rf[:], ["rf"], ["offr"])
        for h in range(2):
            for r in range(4):
                mm(H, "pZ%d" % h, T["pZ%d" % h][:, r::4], T.id1[:], T.z[:, H * h:H * h + H], True, True,
                   ["id1"] + zs(H * h, H * h + H), ["zp%d" % h, "D%d" % h, "R%d" % h] + ["u64"] * h)
        for lo, hi in zip(CFG["cuts"], CFG["cuts"][1:]):
            h, n = lo // H, hi - lo
            if lo in CFG["vg"]:
                cp(16 * n, T.xg[:, 16 * lo:16 * hi], T.X[:, 0:W].indirect(T.hu[:, lo:hi]), xall + qs(lo, hi, "hu"), qs(lo, hi, "x"), r=gat)
                continue
            act(16 * n, T.xg[:, 16 * lo:16 * hi], T.X[:, 0:W].indirect(T.hu[:, lo:hi]), AF.Identity, xall + qs(lo, hi, "hu"),
                qs(lo, hi, "x") + ["gq"], r=gat)
        for lo, hi in zip(CFG["cuts"], CFG["cuts"][1:]):
            h, n = lo // H, hi - lo
            if lo % H == 0:
                mm(H, "pT%d" % h, T["pT%d" % h][:, 0:H], T.c19[:], T.ones[:], True, False, ["c19", "ones"] + qs(lo, hi, "x"),
                   ["tsum%d" % h])
            mins = ["m%d.%d" % (lo, k) for k in range(4)]
            for k in range(4):
                tt(4 * n, T.mn[:, 16 * lo + k:16 * hi:4], T.xg[:, 16 * lo + k:16 * hi:4],
                   T["pZ%d" % h][:, 4 * (lo % H):4 * (lo % H + n)], OP.min, qs(lo, hi, "x") + ["zp%d" % h], [mins[k]], ["pZ%d" % h])
            for kind, src, rd in (("T", T.xg, qs(lo, hi, "x")), ("G", T.mn, mins)):
                bank = "p%s%d" % (kind, h)
                for j in range(lo // 8, hi // 8):
                    q = j % 16
                    mm(H, bank, T[bank][:, 0:H], T.band[:, 15 - q:143 - q], src[:, H * j:H * j + H], kind == "G" and q == 0, q == 15,
                       ["band"] + rd, ["%ssum%d" % (kind.lower(), h)])
        for lo in range(0, L, run):
            scan(16 * run, T.pm[:, 16 * lo:16 * (lo + run)], T.mask[:, 0:16 * run], T.xg[:, 16 * lo:16 * (lo + run)], OP.mult, OP.max,
                 ["mask"] + qs(lo, lo + run, "x"), qs(lo, lo + run, "pm"), r=0.5)
        act(L, T.old[:], T.X[:, 0:W].indirect(T.offr[:]), AF.Identity, xall + ["offr"], ["old"], r=gat)
        ys = [["Y%d" % b for b in range(4 * hf, 4 * hf + 4)] + ["Yd%d" % hf] for hf in range(2)]
        if last:
            ts(8, T.offh[:], T.rf[:, 8:16], -float(W // 2), None, OP.add, None, ["rf"], ["offh"])
            for blk in range(8):
                bank, c0 = ("pP", "pU")[blk % 2], 512 * blk
                y0 = c0 + (YW - YH) * (blk // 4)
                toks = ["v0", "v64"] if bank == "pP" else ["u0", "u192", "ul"]
                mm(512, bank, T[bank][:], T.id1[:], T.X[:, c0:c0 + 512], True, False, ["id1", "x15"] + xall, toks)
                mm(512, bank, T[bank][:], T.id16[:], T.X[:, W // 2 + c0:W // 2 + c0 + 512], False, True, ["id16"] + xall, toks)
                if blk < 8 - CFG["vpack"]:
                    act(512, T.Y[:, y0:y0 + 512], T[bank][:], AF.Identity, toks, ["Y%d" % blk], [bank])
                else:
                    cp(512, T.Y[:, y0:y0 + 512], T[bank][:], toks, ["Y%d" % blk], [bank])
        for h in range(2):
            s, lo, bT, bG, bZ = ".%d" % h, H * h, "pT%d" % h, "pG%d" % h, "pZ%d" % h
            pT, pG, pZ = T[bT], T[bG], T[bZ]
            half = slice(lo, lo + H)
            lead[0] = CFG["lead"][last] if h == 0 else 0.0
            early, ns = CFG["early"][h], SENT[h]

            def home(n, x):
                m = H if n == 0 else L >> n
                if n == early and x != "k":
                    return sm, L * h + m * (x == "g"), "%s%d%sr%d" % (x, n, s, t)
                if n == 4 and x != "k":
                    return T.sv, 32 * h + 16 * (x == "g"), x + "4" + s
                return (None, 0, "") if (n, x) == (0, "k") else (T[x + (str(n) if n else "s")], m * h, "%s%d%s" % (x, n, s))

            src = {x: home(0, x) for x in "gtk"}
            for x, bank in (("t", bT), ("g", bG)):
                scan(H, src[x][0][:, src[x][1]:src[x][1] + H], T.mask[:, 0:H], T[bank][:, 0:H], OP.mult, OP.add,
                     ["mask", "%ssum%d" % (x, h)], [src[x][2]], [bank])
            for n in range(5):
                m = L >> n
                (gb, go, gn), (tb, to, tn) = src["g"], src["t"]
                if n:
                    c_, co, cn = T["c%d" % n], m * h, "c%d%s" % (n, s)
                    pb = T.pb[:, 64 * h:64 * h + m // 2]
                    if n == 1:
                        pa, bk = pT[:, L:L + 64], [bT]
                        tt(64, pa, pG[:, 1:H:2], tb[:, to:to + H:2], OP.mult, ["gsum%d" % h, tn], ["pa" + s], [bG, bT])
                        tt(64, pb, pT[:, 1:H:2], gb[:, go:go + H:2], OP.mult, ["tsum%d" % h, gn], ["pb" + s], [bT])
                    else:
                        pa, bk = T.pa[:, 32 * h:32 * h + m // 2], []
                        tt(m // 2, pa, gb[:, go + 3:go + 2 * m:4], tb[:, to + 1:to + 2 * m:4], OP.mult, [gn, tn], ["pa" + s])
                        tt(m // 2, pb, gb[:, go + 1:go + 2 * m:4], tb[:, to + 3:to + 2 * m:4], OP.mult, [gn, tn], ["pb" + s])
                    tt(m // 2, c_[:, co + 1:co + m:2], pa, pb, OP.is_gt, ["pa" + s, "pb" + s], [cn], bk)
                    for x in "gtk":
                        if (n, x) == (1, "k"):
                            mm(64, bG, pG[:, 320:384], T.id1[:], T.kvs[:], True, False, ["id1", "kvs", cn], ["k1" + s])
                            mm(64, bG, pG[:, 320:384], T.ids[:], c_[:, co + 1:co + m:2], False, True, ["ids", cn], ["k1" + s])
                            continue
                        (sb, so, sn), (db, do_, tok) = src[x], home(n, x)
                        if (n, x) == (2, "k"):
                            scan(m, db[:, do_:do_ + m], c_[:, co:co + m], pG[:, 320:384], OP.max, OP.min, [cn, "k1" + s], [tok], [bG])
                        else:
                            scan(m, db[:, do_:do_ + m], c_[:, co:co + m], sb[:, so:so + m] if n == 1 else sb[:, so + 1:so + 2 * m:2],
                                 OP.max, OP.min, [cn, sn], [tok])
                        src[x] = (db, do_, tok)
                if n == early:
                    wide = 2 * min(H, m)
                    swap(t, lm[:, L * h:L * h + wide], sm[:, L * h:L * h + wide], [src["g"][2], src["t"][2]], "lm%d%s" % (t, s),
                         "av%d%d" % (h, t), CFG["late"][h])
                    if h == 0:
                        rival(t, 1, [src["g"][2], src["t"][2]] if CFG["hold"] and not last else [])
                    theirs = lm[:, L * h:L * h + wide] if n == 0 else lm[:, L * h + 1:L * h + wide:2]
            k4 = T.k4[:, 16 * h + 1:16 * h + 16:2]
            o = 32 * h
            ts(8, T.offy[:, 8 * h:8 * h + 8], k4, 4096.0, q128, OP.mult, OP.add, ["k4" + s, "q128"], ["offy" + s])
            tt(8, slots(T.sd, h, 0, 0), k4, T.kj[:], OP.subtract, ["k4" + s, "kj"], ["sd0" + s])
            if last:
                ts(8 * ns, slots(T.sd, h, 2), slots(T.ia, h, 1), -16 * S19, qc["xl"], OP.mult, OP.add, ["ib" + s, "qcxl"], ["sd2" + s])
                for hf in range(2):
                    act(4, slots(T.sd, h, 2, 0, 4 * hf, 4 * hf + 4), T.rf[:, 8 * h + 4 * hf:8 * h + 4 * hf + 4], AF.Identity, ["rf"],
                        ["sd2" + s], scale=-S19, bias=(TOP + W // 2 * h + YH * hf) * S19)
            else:
                tt(8, slots(T.sa, h, 0, 0), k4, T.kb[:], OP.subtract, ["k4" + s, "kb"], ["sa" + s])
                act(8, slots(T.sd, h, 2, 0), T.rf[:, 8 * h:8 * h + 8], AF.Identity, ["rf"], ["sd2" + s], scale=-S19, bias=TOP * S19)
            yt = "yh%d%s" % (t, s)
            act(H, yh[:, half], T.pm[:, 16 * lo:16 * (lo + H)].indirect(T.offy[:, 8 * h:8 * h + 8]), AF.Identity,
                qs(lo, lo + H, "pm") + ["offy" + s], [yt], scale=0.5, r=gat)
            swap(t, ly[:, half], yh[:, half], [yt], "ly%d%s" % (t, s), "ay%d%d" % (h, t), CFG["late"][2 + h])
            lead[0] = 0.0
            mm(H, bZ, pZ[:, H:L], (T.idmh if last else T.idh)[:], T.old[:, half], True, False, ["idh", "idmh", "old"], ["R%d" % h, "zp%d" % h])
            mm(H, bZ, pZ[:, H:L], T.id1[:], yh[:, half], False, True, ["id1", yt], ["R%d" % h])
            act(H, T.rec[:, half], pZ[:, H:L], AF.Identity, ["R%d" % h], ["rec" + s], [bZ], bias=LIFT - 0.25)
            act(H, T.zq[:, half], T.z[:, half].indirect(colu), AF.Identity, zs(lo, lo + H) + ["colu", "x15"], ["zq" + s],
                bias=LIFT - 0.25, scale=0.5, r=gat)
            mm(H, bZ, pZ[:, 0:H], T.idm2[:], yh[:, half], True, False, ["idm2", yt], ["D%d" % h, "zp%d" % h])
            for c in range(8):
                mm(16, bZ, pZ[:, 16 * c:16 * c + 16], T.id1[:], T.z[:, lo + c:lo + H:8], False, c == 7, ["id1"] + zs(lo, lo + H), ["D%d" % h])
            act(H, T.zd_[:, half], pZ[:, 0:H], AF.Abs, ["D%d" % h], ["zd" + s], [bZ])
            for c0 in (lo, lo + 64):
                act(64, T.zz[:, 2 * c0 + 64:2 * c0 + H], T.zd_[:, c0:c0 + 64], AF.Identity, ["zd" + s], ["zw%d" % c0], bias=LIFT)
            if last:
                dl, yv, of = (T.d1, T.ya, T.offr) if h == 0 else (T.d16, T.yb, T.offh)
                ts(H, dl[:], T.rec[:, half], -LIFT, 16.0 if h else 1.0, OP.add, OP.mult, ["rec" + s], ["dl" + s], r=0.5)
                for hf in range(2):
                    tt(64, yv[:, 64 * hf:64 * hf + 64], T.Y[:, (YW - YH) * hf:YW * (hf + 1)].indirect(of[:, 4 * hf:4 * hf + 4]),
                       dl[:, 64 * hf:64 * hf + 64], OP.add, ys[0] + ys[hf] + ["offr", "offh", "dl" + s], ["yv%d%s" % (hf, s)], r=gat)
            c5, qq, wide = slots(T.c5, h, 0), T["qq%d" % h], 8 * (ns + 1)
            mine = T.rp[:, L * h:L * h + 16 * ns]
            act(16 * ns, mine, T.sv[:, o:o + 32].indirect(T.lists[:, 32 + 16 * h:32 + 16 * h + ns]), AF.Identity,
                ["g4" + s, "t4" + s, "rep" + s], ["rp" + s], r=gat)
            tt(16 * ns, qq[:, :, 1:ns + 1], mine, theirs, OP.mult, ["rp" + s, "lm%d%s" % (t, s)], ["qq" + s])
            tt(wide, c5, qq[:, 0:8, :], qq[:, 8:16, :], OP.is_ge if rank < (rank ^ STEPS[t]) else OP.is_gt, ["qq" + s], ["c5" + s])
            if not last:
                scan(wide, slots(T.sb, h, 0), c5, slots(T.sa, h, 0), OP.min, OP.max, ["c5" + s, "sa" + s], ["sb" + s])
                if h == 0:
                    mm(1, "pG0", T.pG0[:, L:L + 1], T.c17[:], T.drop[:, 0:1], True, False, ["c17", "drop", "sb" + s], ["asum"])
                for c in range(8):
                    mm(1, "pG0", T.pG0[:, L:L + 1], T.c17[:], slots(T.sb, h, 0, ns, c, c + 1), False, h == 1 and c == 7,
                       ["c17", "sb" + s], ["asum"])
            for i in range(3):
                scan(wide, slots(T.se, h, i), c5, slots(T.sd, h, i), OP.min, OP.max, ["c5" + s, "sd%d%s" % (i, s)], ["se%d%s" % (i, s)])
            ts(16, T.off[:, o:o + 16], slots(T.se, h, 0, ns, 0, 16), 1 / S19, None, OP.mult, None, ["se0" + s, "se1" + s], ["off" + s])
            ts(8, T.off[:, o + 16:o + 24], slots(T.se, h, 2, ns), -1 / S19, float(TOP), OP.mult, OP.add, ["se2" + s], ["offx" + s])
            act(H, T.jfin[:, half] if last else tw[t + 1][:, slab(t + 1, h, 0, 1)], tw[t][:, slab(t, h, 0, SLABS)].indirect(T.off[:, o:o + 8]),
                AF.Identity, ["off" + s] + shifted(t, h), ["j%d%s" % (t + 1, s)], r=gat)
            if not last:
                lists(t + 1, h, [])
            for c0 in (lo, lo + 64):
                tt(64, T.zz[:, 2 * c0:2 * c0 + 64], ly[:, c0:c0 + 64], T.zq[:, c0:c0 + 64], OP.add, ["ly%d%s" % (t, s), "zq" + s],
                   ["zl%d" % c0])
                ts(64, T.z[:, c0:c0 + 64], T.zz[:, 2 * c0:2 * c0 + H].indirect(T.off[:, o + 8 + c0 % H // 16:o + 12 + c0 % H // 16]),
                   -LIFT, 1.0, OP.add, OP.max, ["zl%d" % c0, "zw%d" % c0, "off" + s], zs(c0, c0 + 64), r=gat)
            if not last:
                n = CFG["scat"]
                for c0 in range(0, H, n):
                    tt(n, T.X[:, 0:W + L].indirect(T.off[:, o + 16 + c0 // 16:o + 16 + (c0 + n) // 16]), T.rec[:, lo + c0:lo + c0 + n],
                       T.neg[:, 0:n], OP.add, ["offx" + s, "rec" + s, "neg", "Xd"], xall, r=sca)
                if h == 0:
                    picks(t + 1, 0, -DROP, [], CFG["parts0"], True)
                else:
                    for c0 in (0, 64):
                        with_a(c0, c0 + 64, ["asum"])
                    picks(t + 1, 1, T.pG0[:, L:L + 1], ["asum"], CFG["parts"], False)
            else:
                for hf in range(2):
                    cp(64, T.Y[:, hf * YW:hf * YW + YW].indirect(T.off[:, o + 16 + 4 * hf:o + 20 + 4 * hf]), yv[:, 64 * hf:64 * hf + 64],
                       ["offx" + s, "yv%d%s" % (hf, s)], ys[hf], r=sca)
                    if h:
                        dma("s", T.yx[:, hf * YH:hf * YH + YH], T.Y[:, hf * YW:hf * YW + YH], ys[hf], ["yx%d" % hf], "outx", 0.7)
        if last:
            dma("a", T.yj[:], T.jfin[:], names(4), ["yj"], "outj")
            dma("a", T.yz[:], T.z[:], zall, ["yz"], "outz")
    add("s", None, ["yj", "yx0", "yx1", "yz"], ["sq"])
    emit(g, T, arrange(ops))
    g.wait_ge(T.sem.sent, sent[0])
